import numpy as np, ml_dtypes
CORES = [30,158,46,174,86,214]
N = 6
BF = ml_dtypes.bfloat16
def gentries(a):
    return np.ascontiguousarray(a.reshape(8, 16, -1).transpose(0, 2, 1)).reshape(8, -1)
def gtable(e):
    e = np.asarray(e); return np.ascontiguousarray(e.reshape(8, -1, 16).transpose(0, 2, 1)).reshape(128, -1).astype(np.int32)
V, B, CAP, D, VOTE, RO, ST = 896, 160, 48, 3, 9, 3, 1024
def ranks():
    return np.arange(N).reshape(N, 1, 1, 1)
def heights(rng):
    b = rng.integers(0, 256, (N, 8, 1, V)); b[..., :B] += rng.choice(np.array([-30, 0, 40, 90]), (N, 8, 1, 1))
    return np.clip(b + rng.integers(-60, 61, (N, 8, 16, V)), 0, 255)
def weights(rng):
    return np.clip(rng.integers(0, 256, (N, 8, 1, D, V)) + rng.integers(-60, 61, (N, 8, 16, D, V)), 0, 255)
def names(rng):
    s = (N, 8, D, V); r = ranks()
    own = np.where(rng.random(s) < 0.5, (np.arange(V) + rng.integers(-24, 25, s)) % V, rng.integers(0, V, s))
    return np.where(rng.random(s) < 0.7, ST * r + own, ST * ((r + rng.integers(1, N, s)) % N) + rng.integers(0, B, s))
def pack(h, w, n):
    return {"h0": h.reshape(N, 128, V).astype(np.float32).astype(BF), "w0": w.reshape(N, 128, D * V).astype(np.float32).astype(BF), "nb": np.stack([gtable(a.reshape(8, -1)) for a in n])}
def setup_inputs(rng):
    h = heights(rng); w = weights(rng); n = names(rng)
    return pack(h, w, n)
def elsewhere(p):
    return np.concatenate([ST * q + np.arange(B) for q in range(N) if q != p])
def setup_inputs_room(rng):
    w = weights(rng); n = names(rng); h = np.zeros((N, 8, 16, V), np.int64); tops = np.zeros((N, 8, V), bool)
    for q in range(N):
        for g in range(8):
            k = int(rng.choice(np.array([0, 1, CAP - 1, CAP, CAP + 1, B])))
            if q < 2: k = (CAP, CAP + 1, B, CAP - 1, 1, 0, CAP, CAP + 1)[(g + 3 * q) % 8]
            top = np.zeros(V, bool); top[rng.permutation(B)[:k]] = True; top[B + rng.permutation(V - B)[:(V - B) // 4]] = True
            inner = B + np.flatnonzero(top[B:]); low = B + np.flatnonzero(~top[B:]); tops[q, g] = top
            h[q, g] = np.where(top, rng.integers(160, 256, (16, V)), rng.integers(0, 120, (16, V)))
            n[q, g] = np.where(top, ST * q + rng.choice(low, (D, V)), n[q, g])
            n[q, g, D - 1] = np.where(top, n[q, g, D - 1], ST * q + rng.choice(inner, V))
    a, b = [int(x) for x in 2 + rng.permutation(N - 2)[:2]]
    dead = np.concatenate([ST * q + np.flatnonzero(tops[q, 0, :B])[:CAP] for q in range(N) if q != a])
    h[a, 0] = rng.integers(0, 120, (16, V)); w[a, 0, :, 0] = rng.integers(200, 256, (16, V))
    n[a, 0, 0] = rng.choice(dead, V)
    n[a, 0, 1:] = rng.permutation(np.resize(elsewhere(a), (D - 1) * V)).reshape(D - 1, V)
    h[b, 1] = np.where(rng.random(V) < 0.5, rng.integers(245, 256, (16, V)), rng.integers(0, 120, (16, V)))
    n[b, 1] = rng.permutation(np.resize(elsewhere(b), D * V)).reshape(D, V)
    low = rng.permutation(B)[CAP:]; top = np.ones(V, bool); top[low] = False
    h[a, 2] = np.where(top, rng.integers(160, 256, (16, V)), rng.integers(0, 120, (16, V)))
    t = ST * a + rng.choice(low, (D, V)); t[:, low] = ST * a + rng.integers(B, V, (D, low.size)); t[0, low] = ST * a + V - 1 - rng.permutation(low.size)
    n[a, 2] = t
    return pack(h, w, n)
def setup_inputs_ties(rng):
    n = names(rng); me = ST * ranks() + np.arange(V)
    c = rng.choice(np.array([0, 0, 0, 0, 0, 0, 0, VOTE - 1, VOTE, VOTE, 16]), (N, 8, 1, V))
    h = rng.integers(20, 200, (1, 8, 1, 1)) + (np.argsort(rng.random((N, 8, 16, V)), axis=2) < c)
    w = rng.choice(np.array([0, 60, 120, 180]), (N, 8, 1, D, V)) + 3 * ((np.arange(16).reshape(16, 1, 1) + rng.integers(0, 16, (N, 8, 1, D, V))) % 16)
    n[:, :, 1] = np.where(rng.random((N, 8, V)) < 0.3, n[:, :, 0], n[:, :, 1])
    n[:, :, D - 1] = np.where(rng.random((N, 8, V)) < 0.2, n[:, :, 0], n[:, :, D - 1])
    n = np.where(rng.random(n.shape) < 0.1, me, n)
    return pack(h, w, n)
def late(rng, h, n, g):
    s = (D, V)
    for q in range(N):
        o = B + rng.permutation(V - B); y, z = int(o[0]), int(o[1]); low = np.concatenate([np.arange(B), o[2:]])
        h[q, g] = rng.integers(0, 120, (16, V)); h[q, g, :, z] = rng.integers(150, 190, 16); h[q, g, :, y] = rng.integers(200, 256, 16)
        t = np.where(rng.random(s) < 0.7, ST * q + rng.choice(low, s), ST * ((q + rng.integers(1, N, s)) % N) + rng.integers(0, B, s))
        l = rng.integers(0, D, V); t[l, np.arange(V)] = ST * q + z; t[l[z], z] = ST * q + y
        n[q, g] = t
def setup_inputs_alike(rng):
    h = heights(rng) // 2; w = weights(rng); n = names(rng); r = ranks(); s = (N, 4, D, V); hub = np.array([0, B - 1, V - 1])
    mine = ST * r + rng.choice(hub, s); far = ST * ((r + rng.integers(1, N, s)) % N) + rng.choice(hub[:2], s)
    n[:, 1::2] = np.where(rng.random(s) < 0.5, mine, far)
    n[:, ::4] = np.array(n[:, ::4, :1])
    h[..., hub] = rng.integers(200, 256, (N, 8, 16, 3)); n[..., hub] = ST * r + rng.integers(B, V - 1, (N, 8, D, 3))
    late(rng, h, n, int(rng.choice(np.array([2, 6]))))
    return pack(h, w, n)
def setup_inputs_bare(rng):
    h = heights(rng); w = weights(rng); n = names(rng); r = ranks(); me = ST * r + np.arange(V); nx = ST * r + (np.arange(V) + 1) % V
    n = np.where(rng.random(n.shape) < 0.4, me, n); g = rng.permutation(8); q = rng.permutation(N)
    h[:, g[0]] = 77; n[:, g[0]] = np.where(n[:, g[0]] == me[:, 0], nx[:, 0], n[:, g[0]])
    n[q[0], g[1]] = me[q[0], 0]
    w[:, g[2]] = 0
    return pack(h, w, n)
def setup_inputs_spread(rng):
    h = (np.exp2(8 * rng.random((N, 8, 1, V))) * rng.random((N, 8, 16, V))).astype(np.int64)
    w = np.minimum((2 * np.exp2(8 * rng.random((N, 8, 1, D, V))) * rng.random((N, 8, 16, D, V))).astype(np.int64), 255)
    s = (N, 8, D, V); r = ranks(); u = rng.random(s) ** 3
    n = np.where(rng.random(s) < 0.6, ST * r + (V * u).astype(np.int64), ST * ((r + rng.integers(1, N, s)) % N) + (B * u).astype(np.int64))
    return pack(h, w, n)
def check_inputs(d):
    bad = []
    for k in ("h0", "w0"):
        a = np.asarray(d[k]).astype(np.float64)
        if not np.all((a >= 0) & (a <= 255) & (a == np.floor(a))): bad.append("whole numbers from 0 to 255 in " + k)
    e = np.stack([gentries(a) for a in d["nb"]]).astype(np.int64); q = e // ST; v = e - ST * q
    if not np.all((q >= 0) & (q < N) & (v < np.where(q == np.arange(N).reshape(N, 1, 1), V, B))): bad.append("names in nb")
    return bad
def reference(h0, w0, nb):
    h = h0.astype(np.float32).astype(np.int32).reshape(N, 8, 16, V); w = w0.astype(np.float32).astype(np.int32).reshape(N, 8, 16, D, V)
    m = np.stack([gentries(a) for a in nb]).astype(np.int64).reshape(N, 8, D, V); m = (m // ST) * V + m % ST
    live = np.ones((N, 8, V), bool); rising = (2 * D - 1 - np.arange(2 * D)).reshape(2 * D, 1)
    for rnd in range(RO):
        hg = h.transpose(1, 2, 0, 3).reshape(8, 16, N * V); wg = w.transpose(1, 2, 3, 0, 4).reshape(8, 16, D, N * V); mg = m.transpose(1, 2, 0, 3).reshape(8, D, N * V)
        die = []
        for r in range(N):
            a = np.take_along_axis(hg, m[r].reshape(8, 1, D * V), 2).reshape(8, 16, D, V)
            votes = np.add.reduce((h[r][:, :, None, :] > a).astype(np.int32), axis=1)
            die.append(np.all((votes >= VOTE) | (m[r] == r * V + np.arange(V)), axis=1))
        die = np.stack(die) & live
        e = die[:, :, :B].astype(np.int64); before = np.add.accumulate(e, axis=2) - e
        die[:, :, :B] = (e == 1) & (before < CAP)
        live = live & ~die; dg = die.transpose(1, 0, 2).reshape(8, N * V)
        hn, wn, mn = [], [], []
        for r in range(N):
            me = r * V + np.arange(V)
            gone = np.take_along_axis(dg, m[r].reshape(8, D * V), 1).reshape(8, D, V)
            hit = live[r] & np.any(gone, axis=1)
            s = np.argmax(gone, axis=1)[:, None, :]; d = np.take_along_axis(m[r], s, 1)
            ws = np.take_along_axis(w[r], s[:, None], 2)
            wd = np.take_along_axis(wg, d[:, None], 3); hd = np.take_along_axis(hg, d, 2)[:, :, None, :]
            cw = np.concatenate([w[r], np.clip(ws + wd - hd, 0, 255)], axis=2)
            cm = np.concatenate([m[r], np.take_along_axis(mg, d, 2)], axis=1)
            q = cm // V; v = cm - q * V
            out = (cm == me) | np.take_along_axis(dg, cm.reshape(8, -1), 1).reshape(cm.shape) | ((q != r) & (v >= B))
            key = np.where(out, -1, 2 * D * np.add.reduce(cw, axis=1) + rising)
            twin = np.any((cm[:, :, None] == cm[:, None]) & (key[:, :, None] > key[:, None]), axis=1)
            key = np.where(twin, -1, key)
            o = np.argsort(-key, axis=1, kind="stable")[:, :D]; full = np.take_along_axis(key, o, 1) >= 0
            nm = np.where(full, np.take_along_axis(cm, o, 1), me); nw = np.where(full[:, None], np.take_along_axis(cw, o[:, None], 2), 0)
            mn.append(np.where(hit[:, None], nm, m[r])); wn.append(np.where(hit[:, None, None], nw, w[r]))
            hn.append(np.where(hit[:, None], (h[r] + np.maximum(h[r], ws[:, :, 0])) >> 1, h[r]))
        h, w, m = np.stack(hn), np.stack(wn), np.stack(mn)
    m = (m // V) * ST + m % V
    return {"yh": h.reshape(N, 128, V).astype(np.float32).astype(BF), "yw": w.reshape(N, 128, D * V).astype(np.float32).astype(BF), "yn": np.stack([gtable(a.reshape(8, -1)) for a in m]).astype(np.float32)}

@@ -1,0 +1,659 @@
+from concourse.bass import DstId, RemoteDMATransfer
+from concourse.mybir import AluOpType as A, ActivationFunctionType as F
+
+V, B, CAP, NR, RO = 896, 160, 48, 6, 3
+X = V + NR * CAP
+UB = X
+HW = UB + NR * B
+HB = 7 * X
+FL = 32768.0
+SC = 2.0 ** -13
+CH = [(0, 10), (10, 32), (32, 56)]
+HV = [(0, 32, 224), (32, 56, 176)]
+
+bf, f4, i4, u2 = "bfloat16", "float32", "int32", "uint16"
+
+
+def _s(n, d):
+    return ("sbuf", [128] + list(n), d)
+
+
+SCRATCH = {
+    "nbi": _s([168], i4), "ia": _s([168], i4), "ib": _s([168], i4), "fa": _s([168], f4), "fb": _s([168], f4),
+    "NU": _s([3, 56], u2), "RF": _s([3, 56], f4), "ON": _s([3, 56], f4), "EM": _s([3, 56], bf),
+    "H128": _s([3, 56], bf), "h32": _s([3, 56], f4), "LOs": _s([3, 56], bf), "HIs": _s([3, 56], bf),
+    "gm": _s([3, 56], bf), "HP": _s([3, 56], bf), "DA": _s([56], bf), "cmp": _s([2688], bf),
+    "ok": _s([176], bf), "d01": _s([56], bf), "die": _s([56], bf), "dieB": _s([16], bf), "cs": _s([16], bf),
+    "keep": _s([16], bf), "pos": _s([16], bf), "so1": _s([16], f4), "so2": _s([16], f4), "so3": _s([16], f4),
+    "SU": _s([16], u2), "LW": _s([208], bf), "LU": _s([4], u2), "tmp48": _s([48], bf), "LS": _s([3, 48], bf),
+    "G": _s([2688], bf), "Gc": _s([3, 48], bf), "TB": _s([512], bf), "TC": _s([48], bf), "TM": _s([48], bf),
+    "gI": _s([1056], bf),
+    "VI": _s([3, 56], i4), "m01": _s([56], i4), "m": _s([56], i4), "oi": _s([56], i4), "OU": _s([56], u2),
+    "hx": _s([56], f4), "a1": _s([56], i4), "a3": _s([56], f4), "a4": _s([56], f4), "WU": _s([56], u2),
+    "nh": _s([3, 56], bf), "vbp": _s([168], f4), "vb": _s([3, 56], f4), "ws": _s([V], bf), "tt": _s([V], bf),
+    "wd2": _s([V], bf), "Fg": _s([V], bf), "hr": _s([V], bf), "hy": _s([V], bf), "hyb": _s([B], bf),
+    "TT": _s([RO * X], bf), "P1": _s([400], bf), "P2": _s([400], bf), "n7": _s([408], f4), "dn": _s([400], f4),
+    "k0": _s([400], f4), "RB": _s([3, 408], f4), "QB": _s([3, 408], f4), "nq": _s([400], bf), "pen": _s([400], bf),
+    "Ki": _s([3, 56], i4), "xi": _s([3, 56], i4), "xf": _s([3, 56], f4), "ef": _s([3, 56], f4),
+    "EU": _s([3, 56], u2), "NF3": _s([3, 56], f4), "WF": _s([2688], bf), "HO": _s([4 * V], bf),
+    "YN": _s([168], f4), "q128": _s([168], bf),
+    "PI": _s([2], i4), "PF": _s([16], f4), "J": _s([144], f4), "JG": _s([128], f4), "QS": _s([144], bf),
+    "QK": _s([144], bf), "QH": _s([144], bf), "FM": _s([144], bf), "QF": _s([3, 144], bf), "PT": _s([16, 144], bf),
+    "OH": _s([16], f4), "ID": _s([128], bf), "NI": _s([128], bf), "HI": _s([128], bf), "ONE": _s([128], bf),
+    "TRI": _s([128], bf), "tri0": _s([128], bf), "CT": _s([V], bf), "cl": _s([56], bf), "chh": _s([56], bf),
+    "VW": _s([3, 56], f4), "SF": _s([3, 56], f4), "sl": _s([56], bf), "sh": _s([56], bf), "slf": _s([56], f4),
+    "shf": _s([56], f4), "PR": _s([168], bf), "TIE": _s([400], bf), "RST": _s([400], f4), "BL": _s([14], u2),
+    "bli": _s([14], i4), "c48": _s([16], f4), "o16": _s([16], bf),
+    "pA": ("psum", [128, 512], f4), "pV": ("psum", [128, 512], f4), "pN": ("psum", [128, 512], f4),
+    "pK": ("psum", [128, 512], f4), "pT0": ("psum", [128, 512], f4), "pT1": ("psum", [128, 512], f4),
+    "pH0": ("psum", [128, 512], f4), "pH1": ("psum", [128, 512], f4),
+}
+for _r in range(RO):
+    SCRATCH["BG%d" % _r] = _s([HB + HW], bf)
+    SCRATCH["DW%d" % _r] = _s([HW], bf)
+    SCRATCH["LA%d" % _r] = _s([NR, 4 * CAP], bf)
+
+SEMAPHORES = ["cv", "cs", "ct", "cg", "snt", "dnb", "dhb", "dh", "dw", "dz0", "dz1", "dout"] + \
+    ["%s%d" % (k, r) for k in ("mh", "md", "ma", "mb") for r in range(RO)]
+
+
+def rank_program(g, core, T, topo):
+    rk = T.rank_of(core)
+    if rk is None:
+        return
+    Q = {"v": g.vector, "s": g.scalar, "t": g.tensor, "g": g, "y": g.sync}
+    cnt = {"cv": 0, "cs": 0, "ct": 0, "cg": 0}
+    waited = {e: {} for e in Q}
+    wr, rd, bank = {}, {}, {}
+
+    def need(e, R, W, Bk):
+        deps = {}
+        ps = [wr[t] for t in R if t in wr] + [wr[t] for t in W if t in wr]
+        for t in W:
+            ps += list(rd.get(t, {}).items())
+        for b in Bk:
+            ps += [p for p in bank.get(b, {}).items() if p[0] != "c" + e]
+        for s, n in ps:
+            if not (e == "t" and s == "ct"):
+                deps[s] = max(deps.get(s, 0), n)
+        for s, n in deps.items():
+            if waited[e].get(s, 0) < n:
+                Q[e].wait_ge(T.sem[s], n)
+                waited[e][s] = n
+
+    def note(p, R, W, Bk):
+        for t in R:
+            rd.setdefault(t, {})[p[0]] = p[1]
+        for t in W:
+            wr[t] = p
+            rd[t] = {}
+        for b in Bk:
+            bank.setdefault(b, {})[p[0]] = p[1]
+
+    def op(e, fn, R, W, Bk=()):
+        need(e, R, W, Bk)
+        s = "c" + e
+        fn().then_inc(T.sem[s], 1)
+        cnt[s] += 1
+        note((s, cnt[s]), R, W, Bk)
+
+    def mms(lst, R, W, Bk):
+        need("t", R, W, Bk)
+        for a in lst[:-1]:
+            g.tensor.matmul(*a)
+        g.tensor.matmul(*lst[-1]).then_inc(T.sem.ct, 1)
+        cnt["ct"] += 1
+        note(("ct", cnt["ct"]), R, W, Bk)
+
+    def dma(e, sem, pairs, R, W):
+        need(e, R, W, ())
+        for o, i in pairs:
+            Q[e].dma_start(o, i).then_inc(T.sem[sem], 16)
+            cnt[sem] = cnt.get(sem, 0) + 16
+        note((sem, cnt[sem]), R, W, ())
+
+    peers = [c for c in T.cores if c != core]
+    mask = -1
+    for c in peers:
+        mask &= topo.mask(core, c)
+    ne = len([e for e in topo.engines(core, peers[0]) if mask >> e & 1])
+    ids = [DstId(rid=topo.addr(c, core)[0], pnc=topo.addr(c, core)[1]) for c in peers]
+
+    def send(ap, sem, R, tok, src=None):
+        need("g", R, [], ())
+        g.remote_dma_fused([RemoteDMATransfer(dst_ids=ids, dma_engine_mask=mask, remote_sem=T.sem[sem],
+                                              src=ap if src is None else src, dsts=[ap] * len(ids))], local_sem=T.sem.snt)
+        cnt["snt"] = cnt.get("snt", 0) + ne
+        cnt[sem] = ne * len(ids)
+        wr[tok] = (sem, cnt[sem])
+
+    v, s = g.vector, g.scalar
+
+    def ts(o, i, a, b, o0, o1, R, W, Bk=()):
+        op("v", (lambda: v.tensor_scalar(o, i, a, b, o0, o1)) if o1 is not None else
+           (lambda: v.tensor_scalar(o, i, a, None, o0)), R, W, Bk)
+
+    def tt(o, i, j, o0, R, W, Bk=()):
+        op("v", lambda: v.tensor_tensor(o, i, j, o0), R, W, Bk)
+
+    def cp(o, i, R, W, Bk=()):
+        op("v", lambda: v.tensor_copy(o, i), R, W, Bk)
+
+    def ms(o, c, W, Bk=()):
+        op("v", lambda: v.memset(o, c), [], W, Bk)
+
+    def scan(o, a, b, c, o0, o1, R, W, Bk=()):
+        op("v", lambda: v.tensor_tensor_scan(o, a, b, c, o0, o1), R, W, Bk)
+
+    def ac(o, i, f, R, W, Bk=(), bias=0.0, scale=1.0):
+        op("s", lambda: s.activation(o, i, f, bias=bias, scale=scale), R, W, Bk)
+
+    def io(o, pat, base, cm, W, fl=True):
+        op("g", (lambda: g.iota(o, pat, base, cm, allow_small_or_imprecise_dtypes=True)) if fl else
+           (lambda: g.iota(o, pat, base, cm)), [], W)
+
+    BG = [T["BG%d" % r] for r in range(RO)]
+    DW = [T["DW%d" % r] for r in range(RO)]
+    LA = [T["LA%d" % r] for r in range(RO)]
+    ub = UB + B * rk
+    pT, pH = [T.pT0, T.pT1], [T.pH0, T.pH1]
+    I, Re, Cp = F.Identity, F.Relu, F.Copy
+
+    def wblk(r, l, a=0, b=V):
+        return BG[r][:, (6 - l) * X + a:(6 - l) * X + b]
+
+    def hwin(r, a=0, b=V):
+        return BG[r][:, HB + a:HB + b]
+
+    def hown(r, a=0, b=V):
+        return T.HO[:, r * V + a:r * V + b]
+
+    def twin(r, a=0, b=X):
+        return T.TT[:, r * X + a:r * X + b]
+
+    def sel(tab, i):
+        return tab[:, 15 - i:143 - i]
+
+    def split_names(h):
+        c0, c1, _ = HV[h]
+        k = str(h)
+        ac(T.H128[:, :, c0:c1], T.NF3[:, :, c0:c1], I, ["NF" + k], ["H128" + k], bias=127.516, scale=256.0)
+        ac(T.h32[:, :, c0:c1], T.H128[:, :, c0:c1], I, ["H128" + k], ["h32" + k], bias=0.5, scale=-1 / 256.0)
+        ac(T.HP[:, :, c0:c1], T.H128[:, :, c0:c1], I, ["H128" + k], ["HP" + k], bias=-0.5, scale=1 / 256.0)
+
+    def low_names(h):
+        c0, c1, _ = HV[h]
+        tt(T.LOs[:, :, c0:c1], T.NF3[:, :, c0:c1], T.h32[:, :, c0:c1], A.add, ["NF%d" % h, "h32%d" % h], ["LOs%d" % h])
+
+    PT = ["PT%d" % i for i in range(16)]
+
+    def table(r, h, i0, i1):
+        c0, c1, _ = HV[h]
+        n = 16 * (c1 - c0)
+        lst = [(pT[h][:, 0:n], T.ID[:], BG[r][:, 0:n], True, False)] if i0 == 0 else []
+        for i in range(i0, i1):
+            for l in range(3):
+                lst += [(pT[h][:, i:n:16], sel(T.PT[:, i, :], l), T.LOs[:, l, c0:c1], False, False),
+                        (pT[h][:, i:n:16], sel(T.PT[:, i, :], 3 + l), T.HP[:, l, c0:c1], False, h == 0 and i == 15 and l == 2)]
+        mms(lst, ["ID", "z%d" % r, "LOs%d" % h, "HP%d" % h] + PT, ["pT%d" % h], ["pT%d" % h])
+
+    dma("y", "dhb", [(hwin(0, ub, ub + B), T.h0[:, 0:B])], [], ["hb0"])
+    dma("s", "dnb", [(T.nbi[:], T.nb[:])], [], ["nbi"])
+    dma("y", "dh", [(hown(0), T.h0[:]), (hwin(0), T.h0[:])], [], ["h0", "hw0"])
+    dma("s", "dw", [(wblk(0, l), T.w0[:, l * V:(l + 1) * V]) for l in range(3)], [], ["w0_0", "w0_1"])
+    io(T.PI[:, 0:1], [[0, 1]], 0, 1, ["PI0"], False)
+    io(T.J[:], [[1, 144]], 0, 0, ["J"])
+    io(T.chh[:], [[16, 56]], 0, 0, ["chh"])
+    io(T.JG[:], [[16, 8], [0, 16]], 0, 0, ["JG"])
+    io(T.slf[:], [[0, 28], [16, 2]], 0, 0, ["slf"])
+    io(T.shf[:], [[1, 28], [0, 2]], 0, 0, ["shf"])
+    send(hwin(0, ub, ub + B), "mh0", ["hb0"], "hf0")
+
+    ms(BG[0][:, 0:X], 0.0, ["z0"])
+    dma("y", "dz0", [(BG[0][:, k * X:(k + 1) * X], BG[0][:, 0:X]) for k in (1, 2, 3)], ["z0"], ["cw0_0", "cw0_1", "cw0_2"])
+    dma("y", "dz1", [(BG[r][:, 0:4 * X], BG[0][:, 0:4 * X]) for r in range(1, RO)], ["z0", "cw0_0", "cw0_1", "cw0_2"],
+        ["z1", "z2", "cw1_0", "cw1_1", "cw1_2", "cw2_0", "cw2_1", "cw2_2"])
+    p, pm, pg = T.PF[:, 0:1], T.PF[:, 1:2], T.PF[:, 2:3]
+    c_b, c_y = T.PF[:, 3:4], T.PF[:, 4:5]
+    ts(T.PI[:, 1:2], T.PI[:, 0:1], 15, None, A.bitwise_and, None, ["PI0"], ["PI1"])
+    ms(T.DA[:], 0.0, ["DA0", "DA1", "DA2"])
+    cp(T.PF[:, 0:2], T.PI[:, 0:2], ["PI0", "PI1"], ["PF"])
+    ms(T.o16[:], 1.0, ["o16"])
+    tt(pg, p, pm, A.subtract, ["PF"], ["pg"])
+    ts(T.OH[:], T.J[:, 0:16], pm, None, A.is_equal, None, ["J", "PF"], ["OH"])
+    ts(T.QS[:], T.J[:], pg, 15.0, A.subtract, A.is_equal, ["J", "pg"], ["QS"])
+    ts(T.VW[:, 0, :], T.chh[:], pm, None, A.add, None, ["PF", "chh"], ["VW0"])
+    ts(T.ID[:], T.J[:, 0:128], p, None, A.is_equal, None, ["J", "PF"], ["ID"])
+    ts(T.cl[:], T.chh[:], 0.0, pm, A.mult, A.add, ["PF", "chh"], ["cl"])
+    for l in range(3):
+        ac(T.SF[:, l, 0:10], T.VW[:, 0, 0:10], I, ["VW0"], ["SFa%d" % l], bias=ub * SC, scale=SC)
+        ac(T.SF[:, l, 10:56], T.VW[:, 0, 10:56], I, ["VW0"], ["SFb%d" % l], scale=SC)
+    SF = ["SFa0", "SFa1", "SFa2", "SFb0", "SFb1", "SFb2"]
+    for i in range(16):
+        if i < 11:
+            ts(T.PT[:, i, :], T.QS[:], T.OH[:, i:i + 1], None, A.mult, None, ["QS", "OH"], [PT[i]])
+        else:
+            ac(T.PT[:, i, :], T.QS[:], I, ["QS", "OH"], [PT[i]], scale=T.OH[:, i:i + 1])
+    ac(T.NI[:], T.ID[:], I, ["ID"], ["NI"], scale=-1.0)
+    ac(T.QH[:], T.QS[:], I, ["QS"], ["QH"], scale=0.5)
+    for b in range(2):
+        c0, c1, _ = HV[b]
+        n = 16 * (c1 - c0)
+        lst = [(pH[b][:, 0:n], T.ID[:], BG[0][:, 0:n], True, False)]
+        for i in range(16):
+            lst += [(pH[b][:, i:n:16], sel(T.PT[:, i, :], 0), T.cl[:, c0:c1], False, False),
+                    (pH[b][:, i:n:16], sel(T.PT[:, i, :], 1), T.chh[:, c0:c1], False, i == 15)]
+        mms(lst, ["ID", "z0", "cl", "chh"] + PT, ["pH%d" % b], ["pH%d" % b])
+    ts(T.ia[:], T.nbi[:], 10, None, A.arith_shift_right, None, ["nbi"], ["ia"])
+    ts(T.ib[:], T.nbi[:], 1023, None, A.bitwise_and, None, ["nbi"], ["ib"])
+    ts(T.fa[:], T.ia[:], float(B), float(UB), A.mult, A.add, ["ia"], ["fa"])
+    ts(T.fb[:], T.ib[:], float(B), None, A.is_lt, None, ["ib"], ["fb"])
+    ts(T.ONE[:], T.JG[:], pg, 1.0 / FL, A.is_equal, A.mult, ["JG", "pg"], ["ONE"])
+    tt(T.fa[:], T.fa[:], T.fb[:], A.mult, ["fa", "fb"], ["fa"])
+    ts(T.tri0[:], T.J[:, 0:128], p, -1.0, A.is_lt, A.mult, ["J", "PF"], ["tri0"])
+    tt(T.fa[:], T.fa[:], T.ib[:], A.add, ["fa", "ib"], ["fa"])
+    for r in range(RO):
+        ms(hwin(r, V, X), 0.0, ["hc%d" % r])
+    ts(T.NF3[:], T.fa[:], SC, None, A.mult, None, ["fa"], ["NF0", "NF1"])
+    cp(T.NU[:], T.fa[:], ["fa"], ["NU0", "NU1"])
+    split_names(0)
+    split_names(1)
+    tt(T.RF[:], T.NF3[:], T.SF[:], A.subtract, ["NF0", "NF1"] + SF, ["RF0", "RF1"])
+    low_names(0)
+    table(0, 0, 0, 16)
+    ac(T.CT[:, 0:512], pH[0][:], Cp, ["pH0"], ["CT0"], ["pH0"])
+    ac(T.CT[:, 512:V], pH[1][:, 0:384], Cp, ["pH1"], ["CT1"], ["pH1"])
+    ts(T.EM[:], T.RF[:], 0.0, 16.0, A.is_equal, A.mult, ["RF0", "RF1"], ["EM0", "EM1"])
+    tt(T.TRI[:], T.tri0[:], T.ONE[:], A.mult, ["tri0", "ONE"], ["TRI"])
+    low_names(1)
+    ts(c_b, T.OH[:, 1:2], float(V + CAP * rk), None, A.mult, None, ["OH"], ["c_b"])
+    ts(c_y, pm, 3.0, (UB // 32) / 256.0, A.is_ge, A.mult, ["PF"], ["c_y"])
+    ts(T.c48[:, 0:10], T.VW[:, 0, 0:10], float(CAP), None, A.add, None, ["VW0"], ["c48"])
+    ms(T.LW[:], 0.0, ["LW"])
+    for r in range(RO):
+        ms(DW[r][:, 0:B], 0.0, ["dwz%d" % r])
+        ms(DW[r][:, V:X], 0.0, ["dwy%d" % r])
+    for l in range(3):
+        ms(T.PR[:, l * 56:(l + 1) * 56], 8192.0 * (2 - l), ["PR%d" % l])
+    ts(T.sl[:], T.slf[:], pm, SC, A.add, A.mult, ["slf", "PF"], ["sl"])
+    ts(T.bli[:], T.VW[:, 0, 0:14], -3.0, 1 / 7.0, A.add, A.mult, ["VW0"], ["bli"])
+    ms(T.TIE[:], -1.0, ["TIE"])
+    ms(T.RST[:], 0.0, ["RST"])
+    ms(T.n7[:, 0:8], 4.0, ["n7"])
+    ms(T.RB[:, :, 400:408], 0.0, ["RB01", "RB11", "RB21"])
+    ms(T.QB[:, :, 400:408], 0.0, ["QB01", "QB11", "QB21"])
+    ts(T.BL[:], T.bli[:], 7.0, 6.0, A.mult, A.add, ["bli"], ["BL"])
+    ms(T.RST[:, 0:400:7], 4.0, ["RST"])
+    TIE = ["TIE"] + ["TIE%d" % c for c in range(1, 6)]
+    for c in range(6):
+        op("v", lambda: v.memset(T.TIE[:, c:392:7], -(6 - c) / FL), ["TIE"] if c else [], [TIE[c]])
+    for l in range(3):
+        tt(T.QF[:, l, :], T.PT[:, l, :], T.PT[:, 3 + l, :], A.add, PT[:6], ["QF%d" % l])
+    ac(T.QK[:], T.QS[:], I, ["QS"], ["QK"], scale=-8.0 / FL)
+    ac(T.FM[:], T.PT[:, 2, :], I, ["PT2"], ["FM"], scale=0.5 / FL)
+    ac(T.HI[:], T.ID[:], I, ["ID"], ["HI"], scale=0.5)
+    ac(T.VW[:, 1, :], T.VW[:, 0, :], I, ["VW0"], ["VW1"])
+    ac(T.VW[:, 2, :], T.VW[:, 0, :], I, ["VW0"], ["VW2"])
+    ac(T.sh[:, 0:10], T.shf[:, 0:10], I, ["shf"], ["sha"], bias=(ub // 32) / 256.0, scale=1 / 256.0)
+    ac(T.sh[:, 10:56], T.shf[:, 10:56], I, ["shf"], ["shb"], scale=1 / 256.0)
+
+    def hall(r):
+        return ["hw%d" % r, "hb%d" % r, "hf%d" % r, "hc%d" % r]
+
+    def count_votes(k, tab):
+        c0, c1 = CH[k]
+        n, o = c1 - c0, 3 * c0
+        lst = [(T.pA[:, o:o + 3 * n], sel(tab, i), T.cmp[:, 48 * c0 + i:48 * c1:16], i == 0, False) for i in range(16)]
+        for l in range(3):
+            lst.append((T.pA[:, o + l * n:o + (l + 1) * n], T.ID[:], T.EM[:, l, c0:c1], False, False))
+            lst.append((T.pA[:, o + l * n:o + (l + 1) * n], T.NI[:], T.DA[:, c0:c1], False, l == 2))
+        mms(lst, ["QS", "QH", "ID", "NI", "DA%d" % k, "EM%d" % (k // 2)] + ["cmp%d%d" % (k, l) for l in range(3)],
+            ["vt%d" % k], ["pA"])
+
+    def votes(r, k, mid=()):
+        c0, c1 = CH[k]
+        n = c1 - c0
+        for l in range(3):
+            tt(T.cmp[:, 48 * c0 + 16 * n * l:48 * c0 + 16 * n * (l + 1)],
+               hwin(r, 0, HW).indirect(T.NU[:, l, c0:c1]), hown(r, 16 * c0, 16 * c1), A.is_lt,
+               hall(r) + ["h%d" % r, "NU%d" % (k // 2)], ["cmp%d%d" % (k, l)])
+            for f in mid[l] if mid else ():
+                f()
+        count_votes(k, T.QS)
+
+    def votes_scalar(r):
+        c0, c1 = CH[1]
+        n = 16 * (c1 - c0)
+
+        def ga(l):
+            ac(T.gI[:, l * n:(l + 1) * n], hwin(r, 0, HW).indirect(T.NU[:, l, c0:c1]), Cp, hall(r) + ["NU0"], ["gI%d" % l])
+            b = "pH%d" % (l % 2)
+            mms([(pH[l % 2][:, 0:n], T.ID[:], hown(r, 16 * c0, 16 * c1), True, False),
+                 (pH[l % 2][:, 0:n], T.NI[:], T.gI[:, l * n:(l + 1) * n], False, True)], ["ID", "NI", "h%d" % r, "gI%d" % l], [b], [b])
+
+        def sg(l):
+            b = "pH%d" % (l % 2)
+            ac(T.cmp[:, 48 * c0 + n * l:48 * c0 + n * (l + 1)], pH[l % 2][:, 0:n], F.Sign, [b], ["cmp1%d" % l], [b], bias=-0.5)
+        return [lambda: (ga(0), ga(1)), lambda: (sg(0), ga(2), sg(1)), lambda: (sg(2), count_votes(1, T.QH))]
+
+    def deaths_steps(r, k):
+        c0, c1 = CH[k]
+        n, o = c1 - c0, 3 * c0
+        st = [lambda: ts(T.ok[:, o:o + 3 * n], T.pA[:, o:o + 3 * n], 1.0 if k == 1 else 9.0, 32.0, A.is_ge, A.mult,
+                         ["vt%d" % k], ["ok%d" % k], ["pA"]),
+              lambda: tt(T.d01[:, c0:c1], T.ok[:, o:o + n], T.ok[:, o + n:o + 2 * n], A.mult, ["ok%d" % k], ["d01%d" % k]),
+              lambda: tt(T.die[:, c0:c1], T.d01[:, c0:c1], T.ok[:, o + 2 * n:o + 3 * n], A.mult, ["ok%d" % k, "d01%d" % k], ["die%d" % k])]
+        if k:
+            ps, pn = (T.pN, "pN") if k == 1 else (pH[1], "pH1")
+
+            def rows():
+                lst = [(ps[:, 0:16 * n], T.ID[:], T.CT[:, 16 * c0:16 * c1], True, False)]
+                lst += [(ps[:, i:16 * n:16], sel(T.PT[:, i, :], 2), T.die[:, c0:c1], False, i == 15) for i in range(16)]
+                mms(lst, ["ID", "CT0", "CT1", "die%d" % k] + PT, [pn], [pn])
+                tt(T.DA[:, c0:c1], T.DA[:, c0:c1], T.die[:, c0:c1], A.add, ["DA%d" % k, "die%d" % k], ["DA%d" % k])
+            return st + [rows, lambda: ac(DW[r][:, 16 * c0:16 * c1], ps[:, 0:16 * n], Cp, [pn], ["dw%d%d" % (r, k)], [pn])]
+        cn = T.pA[:, 200:210]
+
+        def count():
+            scan(T.cs[:, 0:10], T.o16[:, 0:10], T.die[:, 0:10], 0.0, A.mult, A.add, ["o16", "die0"], ["cs"])
+            mms([(cn, T.TRI[:], T.die[:, 0:10], True, False), (cn, T.ONE[:], T.cs[:, 0:10], False, True)],
+                ["TRI", "ONE", "die0", "cs"], ["cn"], ["pA"])
+
+        def cap():
+            ts(T.keep[:, 0:10], cn, float(CAP), None, A.is_le, None, ["cn"], ["keep"], ["pA"])
+            ts(T.pos[:, 0:10], cn, -1.0, CAP - 1.0, A.add, A.min, ["cn"], ["pos"], ["pA"])
+
+        def rows0():
+            tt(T.dieB[:, 0:10], T.die[:, 0:10], T.keep[:, 0:10], A.mult, ["die0", "keep"], ["dieB"])
+            lst = [(T.pV[:, 352:512], T.ID[:], BG[r][:, 0:B], True, False)]
+            for i in range(16):
+                lst.append((T.pV[:, 352 + i:512:16], sel(T.PT[:, i, :], 3), T.pos[:, 0:10], False, False))
+                lst.append((T.pV[:, 352 + i:512:16], sel(T.PT[:, i, :], 2), T.dieB[:, 0:10], False, i == 15))
+            mms(lst, ["ID", "z%d" % r, "pos", "dieB"] + PT, ["pVb"], ["pV"])
+            ac(DW[r][:, ub:ub + B], T.pV[:, 352:512], Re, ["pVb", "c_b"], ["dw%d0" % r], ["pV"], bias=c_b)
+            send(DW[r][:, ub:ub + B], "md%d" % r, ["dw%d0" % r], "dwf%d" % r)
+
+        def scat():
+            op("v", lambda: v.tensor_copy(T.LW[:].indirect(T.SU[:, 0:10]), T.CT[:, 0:B]), ["SU", "CT0"], ["LW"])
+            mms([(T.pV[:, 200:203], sel(T.QS, i), T.LW[:, i:CAP:16], i == 0, i == 15) for i in range(16)],
+                ["QS", "LW"], ["lc"], ["pV"])
+
+        def lists():
+            cp(T.LU[:, 0:3], T.pV[:, 200:203], ["lc"], ["LU"], ["pV"])
+            for b in range(4):
+                src = wblk(r, b, 0, B) if b < 3 else hown(r, 0, B)
+                ac(LA[r][:, rk, b * CAP:(b + 1) * CAP], src.indirect(T.LU[:, 0:3]), Cp,
+                   ["LU", "w%d_0" % r, "h%d" % r], ["la%d%d" % (r, b)])
+            send(LA[r][:, rk, :], "ma%d" % r, ["la%d%d" % (r, b) for b in range(4)], "laf%d" % r)
+        return st + [count, lambda: None, cap, rows0,
+                     lambda: ts(T.so1[:, 0:10], T.dieB[:, 0:10], -1000.0 / FL, 1000.0, A.mult, A.add, ["dieB"], ["so1"]),
+                     lambda: tt(T.so2[:, 0:10], T.so1[:, 0:10], T.pos[:, 0:10], A.add, ["so1", "pos"], ["so2"]),
+                     lambda: tt(T.so3[:, 0:10], T.so2[:, 0:10], T.c48[:, 0:10], A.min, ["so2", "c48"], ["so3"]),
+                     lambda: cp(T.SU[:, 0:10], T.so3[:, 0:10], ["so3"], ["SU"]), scat,
+                     lambda: tt(T.DA[:, 0:10], T.DA[:, 0:10], T.dieB[:, 0:10], A.add, ["DA0", "dieB"], ["DA0"]), lists]
+
+    def border_names():
+        ac(T.TB[:], pT[0][:], Cp, ["pT0"], ["TB"], ["pT0"])
+        ac(T.TC[:], T.TB[:, 0:B].indirect(T.LU[:, 0:3]), Cp, ["TB", "LU"], ["TC"])
+
+    def mark_names():
+        ts(T.tmp48[:], T.TC[:], c_y, 0.5, A.is_lt, A.mult, ["TC", "c_y"], ["tmp48"])
+        tt(T.TM[:], T.TC[:], T.tmp48[:], A.add, ["TC", "tmp48"], ["TM"])
+
+    def relay(r):
+        la = ["la%d%d" % (r, b) for b in range(4)] + ["laf%d" % r]
+        for b in range(4):
+            dst = wblk(r, b, V, X) if b < 3 else hwin(r, V, X)
+            cp(dst, LA[r][:, :, b * CAP:(b + 1) * CAP], la, ["wc%d%d" % (r, b) if b < 3 else "hc%d" % r])
+
+    def gone(r):
+        dwt = ["dw%d%d" % (r, k) for k in range(3)] + ["dwf%d" % r, "dwz%d" % r, "dwy%d" % r, "NU0", "NU1"]
+        for l in range(3):
+            ac(T.G[:, l * V:l * V + B], DW[r][:].indirect(T.NU[:, l, 0:10]), Cp, dwt, ["Gb%d" % l])
+        for l in range(3):
+            ac(T.Gc[:, l], T.G[:, l * V:l * V + B].indirect(T.LU[:, 0:3]), Cp, ["Gb%d" % l, "LU"], ["Gc%d" % l])
+        for l in range(2):
+            cp(T.G[:, l * V + B:(l + 1) * V], DW[r][:].indirect(T.NU[:, l, 10:56]), dwt, ["G%d" % l])
+        table(r, 1, 0, 4)
+        pc, pd = T.pA[:, 256:256 + CAP], T.pA[:, 304:304 + CAP]
+        mms([(o, a, b, j == 0, j == 3) for o, src in ((pd, T.TM), (pc, T.TC))
+             for j, (a, b) in enumerate([(T.ID[:], src[:])] + [(sel(T.FM, 3 + l), T.Gc[:, l]) for l in range(3)])],
+            ["ID", "FM", "TC", "TM", "Gc0", "Gc1", "Gc2"], ["pc"], ["pA"])
+        mine = twin(r, V + CAP * rk, V + CAP * (rk + 1))
+        ac(T.G[:, 2 * V + B:2 * V + 384], DW[r][:].indirect(T.NU[:, 2, 10:24]), Cp, dwt, ["G2a"])
+        ac(T.LS[:, r], pd, Cp, ["pc"], ["ls%d" % r], ["pA"])
+        send(mine, "mb%d" % r, ["ls%d" % r], "tf%d" % r, T.LS[:, r])
+        ac(T.G[:, 2 * V + 384:3 * V], DW[r][:].indirect(T.NU[:, 2, 24:56]), Cp, dwt + ["G2a"], ["G2"])
+        ac(mine, pc, Cp, ["pc"], ["tb%d" % r], ["pA"])
+        for a, b in ((0, 1), (1, 3)):
+            o = T.pV[:, 56 * a:56 * b]
+            lst = [(o, T.ID[:], T.PR[:, 56 * a:56 * b], True, False)]
+            lst += [(T.pV[:, 56 * l:56 * (l + 1)], T.NI[:], T.DA[:], False, False) for l in range(a, b)]
+            lst += [(o, sel(T.QS, i), T.G[:, a * V + i:b * V:16], False, i == 15) for i in range(16)]
+            mms(lst, ["QS", "ID", "NI", "PR0", "PR1", "PR2", "DA0", "DA1", "DA2"] + ["G%d" % l for l in range(a, b)] +
+                ["Gb%d" % l for l in range(a, b)], ["val%d" % a], ["pV"])
+            if a == 0:
+                table(r, 1, 4, 6)
+        relay(r)
+        cp(T.VI[:], T.pV[:, 0:168], ["val0", "val1"], ["VI"], ["pV"])
+        tt(T.m01[:], T.VI[:, 0], T.VI[:, 1], A.max, ["VI"], ["m01"])
+        ts(T.gm[:], T.VI[:], FL, 0.5, A.is_ge, A.mult, ["VI"], ["gm"])
+        tt(T.m[:], T.m01[:], T.VI[:, 2], A.max, ["VI", "m01"], ["m"])
+        ts(T.a1[:], T.m[:], 13, None, A.arith_shift_right, None, ["m"], ["a1"])
+        ts(T.hx[:], T.m[:], FL, float(X), A.is_ge, A.mult, ["m"], ["hx"])
+        ts(T.oi[:], T.m[:], 8191, None, A.bitwise_and, None, ["m"], ["oi"])
+        tt(T.a3[:], T.a1[:], T.hx[:], A.mult, ["a1", "hx"], ["a3"])
+        cp(T.OU[:], T.oi[:], ["oi"], ["OU"])
+        tt(T.a4[:], T.a3[:], T.VW[:, 0], A.add, ["a3", "VW0"], ["a4"])
+        cp(T.WU[:], T.a4[:], ["a4"], ["WU"])
+        table(r, 1, 6, 16)
+
+    def pool_tokens(r):
+        return ["z%d" % r, "w%d_0" % r, "w%d_1" % r] + ["cw%d_%d" % (r, l) for l in range(3)] + ["wc%d%d" % (r, b) for b in range(3)]
+
+    def splice(r):
+        w = ["w%d_0" % r, "w%d_1" % r]
+        od = T.OU[:]
+        kp = ["kp0", "kp1"]
+        ac(T.ws[:, 0:448], BG[r][:, 0:HB].indirect(T.WU[:, 0:28]), Cp, pool_tokens(r) + ["WU"], ["ws0"])
+        cp(T.ws[:, 448:V], BG[r][:, 0:HB].indirect(T.WU[:, 28:56]), pool_tokens(r) + ["WU"], ["ws1"])
+        for l in range(3):
+            ac(T.nh[:, l], T.hx[:], Re, ["hx"], ["nh%d" % l], bias=1.0, scale=-1.0)
+        pb = T.pA[:, 352:512]
+        if r + 1 < RO:
+            mms([(pb, T.ID[:], T.ws[:, 0:B], True, False), (pb, T.NI[:], hown(r, 0, B), False, True)],
+                ["ID", "NI", "ws0", "h%d" % r], ["pb"], ["pA"])
+        for h in range(2):
+            c0, c1, _ = HV[h]
+            mms(([] if h else [(pT[0][:], T.ID[:], T.TB[:], True, False)]) +
+                [(pT[h][:, 0:16 * (c1 - c0)], sel(T.FM, 3 + l), T.G[:, l * V + 16 * c0:l * V + 16 * c1], False, l == 2) for l in range(3)],
+                ["FM", "ID", "TB", "G0", "G1", "G2", "Gb0", "Gb1", "Gb2"], ["pT%d" % h], ["pT%d" % h])
+        ac(twin(r, 0, 512), pT[0][:], Cp, ["pT0"], ["TT0"], ["pT0"])
+        ac(twin(r, 512, V), pT[1][:, 0:384], Cp, ["pT1"], ["TT1"], ["pT1"])
+        for h in range(2):
+            tt(T.tt[:, 448 * h:448 * (h + 1)], hwin(r, 0, X).indirect(T.OU[:, 28 * h:28 * (h + 1)]),
+               T.ws[:, 448 * h:448 * (h + 1)], A.subtract, ["hw%d" % r, "hc%d" % r, "OU", "ws%d" % h], ["tt%d" % h])
+            if h == 0 and r + 1 < RO:
+                ts(T.hyb[:], pb, 0.0, 255.6, A.max, A.add, ["pb"], ["hyb"], ["pA"])
+                mms([(pb, T.ID[:], hown(r, 0, B), True, False), (pb, T.HI[:], T.hyb[:], False, True)],
+                    ["ID", "HI", "hyb", "h%d" % r], ["pb"], ["pA"])
+                ac(hwin(r + 1, ub, ub + B), pb, I, ["pb"], ["hb%d" % (r + 1)], ["pA"], bias=-128.0)
+                send(hwin(r + 1, ub, ub + B), "mh%d" % (r + 1), ["hb%d" % (r + 1)], "hf%d" % (r + 1))
+        tt(T.HIs[:], T.HP[:], T.gm[:], A.add, ["HP0", "HP1", "gm"], ["HIs"])
+        ac(T.Fg[:], twin(r).indirect(od), Cp, ["TT0", "TT1", "tb%d" % r, "tf%d" % r, "OU"], ["Fg"])
+        ac(T.wd2[:], wblk(r, 2, 0, X).indirect(od), Cp, w + ["wc%d2" % r, "OU"], ["wd2"])
+        lst = [(T.pK[:, 0:400], T.ID[:], T.TIE[:], True, False)]
+        for c in range(3):
+            lst += [(T.pK[:, c:392:7], sel(T.QK, i), BG[r][:, (6 - c) * X + i:(6 - c) * X + V:16], False, False) for i in range(16)]
+        lst += [(T.pK[:, c:392:7], T.ID[:], T.nh[:, 0], False, False) for c in range(6)]
+        mms(lst, ["ID", "QK", "nh0"] + w + TIE, kp, ["pK"])
+        lst = [(T.pN[:, 0:400], T.ID[:], BG[r][:, 0:400], True, False)]
+        for c in range(6):
+            o = T.pN[:, c:392:7]
+            lst += [(o, T.NI[:], T.sl[:], False, False), (o, T.NI[:], T.sh[:], False, False)]
+            if c < 3:
+                lst += [(o, T.ID[:], T.LOs[:, c], False, False), (o, T.ID[:], T.HIs[:, c], False, False)]
+        mms(lst, ["ID", "NI", "sl", "sha", "shb", "LOs0", "LOs1", "HIs", "z%d" % r], ["pN"], ["pN"])
+
+        def cw(l, a=0, b=V):
+            return BG[r][:, (3 - l) * X + a:(3 - l) * X + b]
+
+        def sums(l, last=False):
+            mms([(T.pK[:, 3 + l:392:7], sel(T.QK, i), BG[r][:, (3 - l) * X + i:(3 - l) * X + V:16], False, last and i == 15)
+                 for i in range(16)], ["QK", "cw%d_%d" % (r, l)], kp, ["pK"])
+        for l in range(2):
+            tt(cw(l), wblk(r, l, 0, X).indirect(od), T.tt[:], A.subtract, w + ["wc%d%d" % (r, l), "OU", "tt0", "tt1"], ["cw%d_%d" % (r, l)])
+            if l == 0:
+                tt(T.ON[:], T.RF[:], T.nh[:], A.mult, ["RF0", "RF1", "nh0", "nh1", "nh2"], ["ON"])
+            ts(cw(l), cw(l), 0.0, 255.0, A.max, A.min, ["cw%d_%d" % (r, l)], ["cw%d_%d" % (r, l)])
+        mms([(T.pN[:, 3 + l:392:7], sel(T.QF[:, l, :], i), T.Fg[:, i:V:16], False, l == 2 and i == 15)
+             for l in range(3) for i in range(16)], ["QF0", "QF1", "QF2", "Fg"], ["pN"], ["pN"])
+        sums(0)
+        for h in range(2):
+            mms([(pH[h][:, 0:448], T.ID[:], T.wd2[:, 448 * h:448 * (h + 1)], True, False),
+                 (pH[h][:, 0:448], T.NI[:], T.tt[:, 448 * h:448 * (h + 1)], False, True)],
+                ["ID", "NI", "wd2", "tt%d" % h], ["pH%d" % h], ["pH%d" % h])
+        sums(1)
+        ts(T.P1[:], T.pN[:, 0:400], 0.0, None, A.is_equal, None, ["pN"], ["P1"], ["pN"])
+        ac(T.P2[:], T.pN[:, 0:400], Re, ["pN"], ["P2"], ["pN"], bias=-64.0, scale=256.0)
+        ac(T.n7[:, 1:401], T.pN[:, 0:400], Cp, ["pN"], ["n7"], ["pN"])
+        ac(T.n7[:, 7:401:7], T.RST[:, 0:399:7], Cp, ["RST", "n7"], ["n7"])
+        for h in range(2):
+            ts(cw(2, 448 * h, 448 * (h + 1)), pH[h][:, 0:448], 0.0, 255.0, A.max, A.min, ["pH%d" % h],
+               ["cw%d_2" % r], ["pH%d" % h])
+        mms([(T.pK[:, 0:400], T.ID[:], a[:], False, False) for a in (T.P1, T.P2)], ["ID", "P1", "P2"], kp, ["pK"])
+        sums(2, True)
+        tt(T.dn[:], T.n7[:, 0:400], T.pN[:, 0:400], A.subtract, ["n7", "pN"], ["dn"], ["pN"])
+        for l in range(3):
+            ac(T.vbp[:, 56 * l:56 * (l + 1)], T.hx[:], I, ["hx"], ["vbp%d" % l], bias=float((6 - l) * X), scale=-float(6 - l))
+        ac(T.k0[:, 0:224], T.pK[:, 0:224], Cp, kp, ["k00"], ["pK"])
+
+    def heights(r):
+        for h in range(2):
+            mms([(pH[h][:, 0:448], T.ID[:], T.ws[:, 448 * h:448 * (h + 1)], True, False),
+                 (pH[h][:, 0:448], T.NI[:], hown(r, 448 * h, 448 * (h + 1)), False, True)],
+                ["ID", "NI", "ws%d" % h, "h%d" % r], ["pH%d" % h], ["pH%d" % h])
+            ac(T.hr[:, 448 * h:448 * (h + 1)], pH[h][:, 0:448], Re, ["pH%d" % h], ["hr%d" % h], ["pH%d" % h])
+        for h in range(2):
+            ac(T.hy[:, 448 * h:448 * (h + 1)], T.hr[:, 448 * h:448 * (h + 1)], I, ["hr%d" % h], ["hy%d" % h], bias=255.6)
+            mms([(pH[h][:, 0:448], T.ID[:], hown(r, 448 * h, 448 * (h + 1)), True, False),
+                 (pH[h][:, 0:448], T.HI[:], T.hy[:, 448 * h:448 * (h + 1)], False, True)],
+                ["ID", "HI", "hy%d" % h, "h%d" % r], ["pH%d" % h], ["pH%d" % h])
+        for h in range(2):
+            ac(hown(r + 1, 448 * h, 448 * (h + 1)), pH[h][:, 0:448], I, ["pH%d" % h], ["h%d" % (r + 1)], ["pH%d" % h], bias=-128.0)
+        if r + 1 < RO:
+            ac(hwin(r + 1), hown(r + 1), Cp, ["h%d" % (r + 1)], ["hw%d" % (r + 1)])
+        else:
+            dma("y", "dout", [(T.yh[:], hown(RO))], ["h%d" % RO], [])
+
+    def choose_steps(r, h):
+        c0, c1, n = HV[h]
+        a, b = 7 * c0, 7 * c0 + n
+        bl = T.BL[:, 0:n // 16]
+        k = str(h)
+        kp = "kp" + k
+        st = []
+        for t in range(3):
+            st.append(lambda t=t: scan(T.RB[:, t, a:b], T.RST[:, a:b], T.pK[:, a:b], 0.0, A.add, A.min,
+                                       ["RST", kp], ["RB%d%d" % (t, h)], ["pK"]))
+            st.append(lambda t=t: tt(T.nq[:, a:b], T.RB[:, t, a:b + 8 * h].indirect(bl), T.k0[:, a:b], A.not_equal,
+                                     ["RB%d%d" % (t, h), "k0" + k, "BL"], ["nq" + k]))
+            st.append(lambda t=t: scan(T.QB[:, t, a:b], T.dn[:, a:b], T.nq[:, a:b], 4.0, A.add, A.min,
+                                       ["dn", "nq" + k], ["QB%d%d" % (t, h)]))
+            if t < 2:
+                st.append(lambda t=t: tt(T.pen[:, a:b], T.QB[:, t, a:b + 8 * h].indirect(bl), T.n7[:, 1 + a:1 + b], A.is_equal,
+                                         ["QB%d%d" % (t, h), "n7", "BL"], ["pen" + k]))
+                st.append(lambda: tt(T.pK[:, a:b], T.pK[:, a:b], T.pen[:, a:b], A.add, [kp, "pen" + k], [kp], ["pK"]))
+        rb = ["RB%d%d" % (t, h) for t in range(3)]
+        qb = ["QB%d%d" % (t, h) for t in range(3)]
+        ki = lambda: ts(T.Ki[:, :, c0:c1], T.RB[:, :, a + 6:7 * c1:7], -FL, None, A.mult, None, rb, ["Ki" + k])
+        xi = lambda: ts(T.xi[:, :, c0:c1], T.Ki[:, :, c0:c1], 7, None, A.bitwise_and, None, ["Ki" + k], ["xi" + k])
+        st = st[:-1] + [lambda f=st[-1]: (ki(), f(), xi())]
+        st += [
+            lambda: tt(T.RF[:, :, c0:c1], T.QB[:, :, a + 6:7 * c1:7], T.ON[:, :, c0:c1], A.add, qb + ["ON"], ["RF" + k]),
+            lambda: ts(T.xf[:, :, c0:c1], T.xi[:, :, c0:c1], float(X), None, A.mult, None, ["xi" + k], ["xf" + k]),
+            lambda: tt(T.NF3[:, :, c0:c1], T.RF[:, :, c0:c1], T.SF[:, :, c0:c1], A.add, ["RF" + k] + SF, ["NF" + k]),
+            lambda: tt(T.ef[:, :, c0:c1], T.xf[:, :, c0:c1], T.vb[:, :, c0:c1], A.add, ["xf" + k, "vb"], ["ef" + k]),
+            lambda: cp(T.EU[:, :, c0:c1], T.ef[:, :, c0:c1], ["ef" + k], ["EU" + k]),
+        ]
+        if r + 1 < RO:
+            st.insert(-1, lambda: ts(T.NU[:, :, c0:c1], T.NF3[:, :, c0:c1], 1 / SC, None, A.mult, None, ["NF" + k], ["NU" + k]))
+            st.append(lambda: ts(T.EM[:, :, c0:c1], T.RF[:, :, c0:c1], 0.0, 16.0, A.is_equal, A.mult, ["RF" + k], ["EM" + k]))
+        return st
+
+    def new_weights(r, h, eng="sss", which=(0, 1, 2)):
+        c0, c1, _ = HV[h]
+        for t in which:
+            src = BG[r][:, 0:HB].indirect(T.EU[:, t, c0:c1])
+            R = pool_tokens(r) + ["EU%d" % h]
+            if r + 1 < RO:
+                ac(wblk(r + 1, t, 16 * c0, 16 * c1), src, Cp, R, ["w%d_%d" % (r + 1, h)])
+            else:
+                o = T.WF[:, t * V + 16 * c0:t * V + 16 * c1]
+                tok = "wf%d%d" % (t, h)
+                if eng[t] == "s":
+                    ac(o, src, Cp, R, [tok])
+                else:
+                    cp(o, src, R, [tok])
+                dma("y", "dout", [(T.yw[:, t * V + 16 * c0:t * V + 16 * c1], o)], [tok], [])
+
+    def run(*lists):
+        for k in range(max(len(x) for x in lists)):
+            for x in lists:
+                if k < len(x):
+                    x[k]()
+
+    nop = [lambda: None]
+
+    def tb(r, a, b):
+        return lambda: table(r, 0, a, b)
+
+    votes(0, 0)
+    vs = votes_scalar(0)
+    db = deaths_steps(0, 0)
+    run(db[:7], nop * 4 + vs[:1] + nop + vs[1:2])
+    vs[2]()
+    for r in range(RO):
+        d1, d2 = deaths_steps(r, 1), deaths_steps(r, 2)
+        if r == 0:
+            votes(r, 2, [db[7:12], db[12:14], d1[:4]])
+            d1[4]()
+            border_names()
+        else:
+            new_weights(r - 1, 1, which=(0, 1))
+            votes(r, 2, [d1[:1], d1[1:2] + [lambda: low_names(1)], d1[2:4]])
+            d1[4]()
+            new_weights(r - 1, 1, which=(2,))
+            border_names()
+        run(d2)
+        mark_names()
+        gone(r)
+        splice(r)
+        run(choose_steps(r, 0),
+            [lambda: ac(T.k0[:, 224:400], T.pK[:, 224:400], Cp, ["kp1"], ["k01"], ["pK"]),
+             lambda: tt(T.vb[:], T.vbp[:], T.VW[:], A.add, ["vbp0", "vbp1", "vbp2", "VW0", "VW1", "VW2"], ["vb"]),
+             lambda: heights(r)])
+        if r + 1 < RO:
+            split_names(0)
+            new_weights(r, 0)
+            votes(r + 1, 0)
+            db = deaths_steps(r + 1, 0)
+            vs = votes_scalar(r + 1)
+            run(choose_steps(r, 1),
+                [lambda: (low_names(0), table(r + 1, 0, 0, 4)), nop[0]] + db[:4] + [tb(r + 1, 4, 7), db[5], vs[0]] + db[6:13],
+                nop * 9 + [vs[1], tb(r + 1, 7, 9)] + nop * 3 + [vs[2], tb(r + 1, 9, 16)])
+            db[13]()
+            split_names(1)
+        else:
+            new_weights(r, 0)
+            run(choose_steps(r, 1))
+            ac(T.q128[:], T.NF3[:], I, ["NF0", "NF1"], ["q128"], bias=192.0 - (UB + 79.5) / B, scale=1 / (SC * B))
+            ac(T.fa[:], T.q128[:], I, ["q128"], ["fa"], bias=-192.0 * 864 - UB - 1024.0 * rk, scale=864.0)
+            ts(T.fb[:], T.NF3[:], UB * SC, None, A.is_ge, None, ["NF0", "NF1"], ["fb"])
+            ts(T.h32[:], T.NF3[:], 1 / SC, 1024.0 * rk, A.mult, A.add, ["NF0", "NF1"], ["h320", "h321"])
+            tt(T.fa[:], T.fa[:], T.fb[:], A.mult, ["fa", "fb"], ["fa"])
+            tt(T.YN[:], T.fa[:], T.h32[:], A.add, ["fa", "h320"], ["YN"])
+            dma("y", "dout", [(T.yn[:], T.YN[:])], ["YN"], [])
+            new_weights(r, 1, "svv")
+    for k, n in cnt.items():
+        g.wait_ge(T.sem[k], n)

@@ -186,21 +186,36 @@ def rank_program(g, core, T, topo):
         tt(T.LOs[:, :, c0:c1], T.NF3[:, :, c0:c1], T.h32[:, :, c0:c1], A.add, ["NF%d" % h, "h32%d" % h], ["LOs%d" % h])
 
     PT = ["PT%d" % i for i in range(16)]
+    TIE = ["TIE"] + ["TIE%d" % c for c in range(1, 6)]
 
-    def table(r, h, i0, i1):
-        c0, c1, _ = HV[h]
+    def table(r, i0, i1):
+        c0, c1, _ = HV[0]
         n = 16 * (c1 - c0)
-        lst = [(pT[h][:, 0:n], T.ID[:], BG[r][:, 0:n], True, False)] if i0 == 0 else []
+        lst = [(pT[0][:, 0:n], T.ID[:], BG[r][:, 0:n], True, False)] if i0 == 0 else []
         for i in range(i0, i1):
             for l in range(3):
-                lst += [(pT[h][:, i:n:16], sel(T.PT[:, i, :], l), T.LOs[:, l, c0:c1], False, False),
-                        (pT[h][:, i:n:16], sel(T.PT[:, i, :], 3 + l), T.HP[:, l, c0:c1], False, h == 0 and i == 15 and l == 2)]
-        mms(lst, ["ID", "z%d" % r, "LOs%d" % h, "HP%d" % h] + PT, ["pT%d" % h], ["pT%d" % h])
+                lst += [(pT[0][:, i:n:16], sel(T.PT[:, i, :], l), T.LOs[:, l, c0:c1], False, False),
+                        (pT[0][:, i:n:16], sel(T.PT[:, i, :], 3 + l), T.HP[:, l, c0:c1], False, i == 15 and l == 2)]
+        mms(lst, ["ID", "z%d" % r, "LOs0", "HP0"] + PT, ["pT0"], ["pT0"])
+
+    def table1(r, hi):
+        c0, c1, _ = HV[1]
+        n = 16 * (c1 - c0)
+        lst = [] if hi else [(pT[1][:, 0:n], T.ID[:], BG[r][:, 0:n], True, False)]
+        lst += [(pT[1][:, i:n:16], sel(T.PT[:, i, :], 3 * hi + l), (T.HIs if hi else T.LOs)[:, l, c0:c1], False,
+                 hi == 1 and i == 15 and l == 2) for i in range(16) for l in range(3)]
+        mms(lst, ["ID", "z%d" % r, "HIs1" if hi else "LOs1"] + PT, ["pT1"], ["pT1"])
+
+    def own_sums(r, cs):
+        lst = [(T.pK[:, 0:400], T.ID[:], T.TIE[:], True, False)] if cs[0] == 0 else []
+        for c in cs:
+            lst += [(T.pK[:, c:392:7], sel(T.QK, i), BG[r][:, (6 - c) * X + i:(6 - c) * X + V:16], False, False) for i in range(16)]
+        mms(lst, ["ID", "QK"] + ["w%d_%d" % (r, k) for k in range(3)] + TIE, ["kp0", "kp1"], ["pK"])
 
     dma("y", "dhb", [(hwin(0, ub, ub + B), T.h0[:, 0:B])], [], ["hb0"])
     dma("s", "dnb", [(T.nbi[:], T.nb[:])], [], ["nbi"])
     dma("y", "dh", [(hown(0), T.h0[:]), (hwin(0), T.h0[:])], [], ["h0", "hw0"])
-    dma("s", "dw", [(wblk(0, l), T.w0[:, l * V:(l + 1) * V]) for l in range(3)], [], ["w0_0", "w0_1"])
+    dma("s", "dw", [(wblk(0, l), T.w0[:, l * V:(l + 1) * V]) for l in range(3)], [], ["w0_0", "w0_1", "w0_2"])
     io(T.PI[:, 0:1], [[0, 1]], 0, 1, ["PI0"], False)
     io(T.J[:], [[1, 144]], 0, 0, ["J"])
     io(T.chh[:], [[16, 56]], 0, 0, ["chh"])
@@ -260,7 +275,7 @@ def rank_program(g, core, T, topo):
     split_names(1)
     tt(T.RF[:], T.NF3[:], T.SF[:], A.subtract, ["NF0", "NF1"] + SF, ["RF0", "RF1"])
     low_names(0)
-    table(0, 0, 0, 16)
+    table(0, 0, 16)
     ac(T.CT[:, 0:512], pH[0][:], Cp, ["pH0"], ["CT0"], ["pH0"])
     ac(T.CT[:, 512:V], pH[1][:, 0:384], Cp, ["pH1"], ["CT1"], ["pH1"])
     ts(T.EM[:], T.RF[:], 0.0, 16.0, A.is_equal, A.mult, ["RF0", "RF1"], ["EM0", "EM1"])
@@ -284,11 +299,12 @@ def rank_program(g, core, T, topo):
     ms(T.QB[:, :, 400:408], 0.0, ["QB01", "QB11", "QB21"])
     ts(T.BL[:], T.bli[:], 7.0, 6.0, A.mult, A.add, ["bli"], ["BL"])
     ms(T.RST[:, 0:400:7], 4.0, ["RST"])
-    TIE = ["TIE"] + ["TIE%d" % c for c in range(1, 6)]
-    for c in range(6):
-        op("v", lambda: v.memset(T.TIE[:, c:392:7], -(6 - c) / FL), ["TIE"] if c else [], [TIE[c]])
-    for l in range(3):
-        tt(T.QF[:, l, :], T.PT[:, l, :], T.PT[:, 3 + l, :], A.add, PT[:6], ["QF%d" % l])
+
+    def late_consts():
+        for c in range(6):
+            op("v", lambda: v.memset(T.TIE[:, c:392:7], -(6 - c) / FL), ["TIE"] if c else [], [TIE[c]])
+        for l in range(3):
+            tt(T.QF[:, l, :], T.PT[:, l, :], T.PT[:, 3 + l, :], A.add, PT[:6], ["QF%d" % l])
     ac(T.QK[:], T.QS[:], I, ["QS"], ["QK"], scale=-8.0 / FL)
     ac(T.FM[:], T.PT[:, 2, :], I, ["PT2"], ["FM"], scale=0.5 / FL)
     ac(T.HI[:], T.ID[:], I, ["ID"], ["HI"], scale=0.5)
@@ -321,12 +337,14 @@ def rank_program(g, core, T, topo):
                 f()
         count_votes(k, T.QS)
 
-    def votes_scalar(r):
+    def votes_scalar(r, mid=lambda: None):
         c0, c1 = CH[1]
         n = 16 * (c1 - c0)
 
         def ga(l):
             ac(T.gI[:, l * n:(l + 1) * n], hwin(r, 0, HW).indirect(T.NU[:, l, c0:c1]), Cp, hall(r) + ["NU0"], ["gI%d" % l])
+
+        def df(l):
             b = "pH%d" % (l % 2)
             mms([(pH[l % 2][:, 0:n], T.ID[:], hown(r, 16 * c0, 16 * c1), True, False),
                  (pH[l % 2][:, 0:n], T.NI[:], T.gI[:, l * n:(l + 1) * n], False, True)], ["ID", "NI", "h%d" % r, "gI%d" % l], [b], [b])
@@ -334,7 +352,8 @@ def rank_program(g, core, T, topo):
         def sg(l):
             b = "pH%d" % (l % 2)
             ac(T.cmp[:, 48 * c0 + n * l:48 * c0 + n * (l + 1)], pH[l % 2][:, 0:n], F.Sign, [b], ["cmp1%d" % l], [b], bias=-0.5)
-        return [lambda: (ga(0), ga(1)), lambda: (sg(0), ga(2), sg(1)), lambda: (sg(2), count_votes(1, T.QH))]
+        return [lambda: (ga(0), ga(1)), lambda: (df(0), df(1), ga(2), sg(0)),
+                lambda: (df(2), sg(1), sg(2), mid(), count_votes(1, T.QH))]
 
     def deaths_steps(r, k):
         c0, c1 = CH[k]
@@ -351,6 +370,8 @@ def rank_program(g, core, T, topo):
                 lst += [(ps[:, i:16 * n:16], sel(T.PT[:, i, :], 2), T.die[:, c0:c1], False, i == 15) for i in range(16)]
                 mms(lst, ["ID", "CT0", "CT1", "die%d" % k] + PT, [pn], [pn])
                 tt(T.DA[:, c0:c1], T.DA[:, c0:c1], T.die[:, c0:c1], A.add, ["DA%d" % k, "die%d" % k], ["DA%d" % k])
+            if k == 2:
+                return st + [rows, lambda: cp(DW[r][:, 16 * c0:16 * c1], ps[:, 0:16 * n], [pn], ["dw%d%d" % (r, k)], [pn])]
             return st + [rows, lambda: ac(DW[r][:, 16 * c0:16 * c1], ps[:, 0:16 * n], Cp, [pn], ["dw%d%d" % (r, k)], [pn])]
         cn = T.pA[:, 200:210]
 
@@ -414,7 +435,9 @@ def rank_program(g, core, T, topo):
             ac(T.Gc[:, l], T.G[:, l * V:l * V + B].indirect(T.LU[:, 0:3]), Cp, ["Gb%d" % l, "LU"], ["Gc%d" % l])
         for l in range(2):
             cp(T.G[:, l * V + B:(l + 1) * V], DW[r][:].indirect(T.NU[:, l, 10:56]), dwt, ["G%d" % l])
-        table(r, 1, 0, 4)
+            if l == 0:
+                mark_names()
+        table1(r, 0)
         pc, pd = T.pA[:, 256:256 + CAP], T.pA[:, 304:304 + CAP]
         mms([(o, a, b, j == 0, j == 3) for o, src in ((pd, T.TM), (pc, T.TC))
              for j, (a, b) in enumerate([(T.ID[:], src[:])] + [(sel(T.FM, 3 + l), T.Gc[:, l]) for l in range(3)])],
@@ -425,34 +448,42 @@ def rank_program(g, core, T, topo):
         send(mine, "mb%d" % r, ["ls%d" % r], "tf%d" % r, T.LS[:, r])
         ac(T.G[:, 2 * V + 384:3 * V], DW[r][:].indirect(T.NU[:, 2, 24:56]), Cp, dwt + ["G2a"], ["G2"])
         ac(mine, pc, Cp, ["pc"], ["tb%d" % r], ["pA"])
-        for a, b in ((0, 1), (1, 3)):
-            o = T.pV[:, 56 * a:56 * b]
-            lst = [(o, T.ID[:], T.PR[:, 56 * a:56 * b], True, False)]
-            lst += [(T.pV[:, 56 * l:56 * (l + 1)], T.NI[:], T.DA[:], False, False) for l in range(a, b)]
-            lst += [(o, sel(T.QS, i), T.G[:, a * V + i:b * V:16], False, i == 15) for i in range(16)]
-            mms(lst, ["QS", "ID", "NI", "PR0", "PR1", "PR2", "DA0", "DA1", "DA2"] + ["G%d" % l for l in range(a, b)] +
-                ["Gb%d" % l for l in range(a, b)], ["val%d" % a], ["pV"])
-            if a == 0:
-                table(r, 1, 4, 6)
-        relay(r)
-        cp(T.VI[:], T.pV[:, 0:168], ["val0", "val1"], ["VI"], ["pV"])
-        tt(T.m01[:], T.VI[:, 0], T.VI[:, 1], A.max, ["VI"], ["m01"])
-        ts(T.gm[:], T.VI[:], FL, 0.5, A.is_ge, A.mult, ["VI"], ["gm"])
-        tt(T.m[:], T.m01[:], T.VI[:, 2], A.max, ["VI", "m01"], ["m"])
+        pv, bv = [T.pV, T.pN, T.pV], ["pV", "pN", "pV"]
+        for l in range(3):
+            o = pv[l][:, 56 * l:56 * (l + 1)]
+            lst = [(o, T.ID[:], T.PR[:, 56 * l:56 * (l + 1)], True, False)]
+            lst += [(o, sel(T.QS, i), T.G[:, l * V + i:(l + 1) * V:16], False, i == 15) for i in range(16)]
+            mms(lst, ["QS", "ID", "PR%d" % l, "G%d" % l, "Gb%d" % l], ["val%d" % l, bv[l]], [bv[l]])
+            if l == 0:
+                own_sums(r, (0,))
+                cp(T.VI[:, 0], o, ["val0"], ["VI0"], ["pV"])
+                relay(r)
+                ts(T.gm[:, 0], T.VI[:, 0], FL, 0.5, A.is_ge, A.mult, ["VI0"], ["gm0"])
+            if l == 1:
+                tt(T.m01[:], T.VI[:, 0], o, A.max, ["VI0", "val1"], ["m01"], ["pN"])
+                ts(T.gm[:, 1], o, FL, 0.5, A.is_ge, A.mult, ["val1", "pN"], ["gm1"], ["pN"])
+        tt(T.m[:], T.m01[:], o, A.max, ["val2", "m01"], ["m"], ["pV"])
+        ts(T.gm[:, 2], o, FL, 0.5, A.is_ge, A.mult, ["val2"], ["gm2"], ["pV"])
+        tt(T.a4[:], T.m[:], T.DA[:], A.subtract, ["m", "DA0", "DA1", "DA2"], ["a4"])
         ts(T.a1[:], T.m[:], 13, None, A.arith_shift_right, None, ["m"], ["a1"])
-        ts(T.hx[:], T.m[:], FL, float(X), A.is_ge, A.mult, ["m"], ["hx"])
+        ts(T.hx[:], T.a4[:], FL, float(X), A.is_ge, A.mult, ["a4"], ["hx"])
         ts(T.oi[:], T.m[:], 8191, None, A.bitwise_and, None, ["m"], ["oi"])
         tt(T.a3[:], T.a1[:], T.hx[:], A.mult, ["a1", "hx"], ["a3"])
         cp(T.OU[:], T.oi[:], ["oi"], ["OU"])
         tt(T.a4[:], T.a3[:], T.VW[:, 0], A.add, ["a3", "VW0"], ["a4"])
+        tt(T.HIs[:, :, 32:56], T.HP[:, :, 32:56], T.gm[:, :, 32:56], A.add, ["HP1", "gm0", "gm1", "gm2"], ["HIs1"])
         cp(T.WU[:], T.a4[:], ["a4"], ["WU"])
-        table(r, 1, 6, 16)
+        mms([(pT[0][:], T.ID[:], T.TB[:], True, False)] +
+            [(pT[0][:], sel(T.FM, 3 + l), T.G[:, l * V:l * V + 512], False, l == 2) for l in range(3)],
+            ["FM", "ID", "TB", "G0", "G1", "G2", "Gb0", "Gb1", "Gb2"], ["pT0"], ["pT0"])
+        table1(r, 1)
 
     def pool_tokens(r):
-        return ["z%d" % r, "w%d_0" % r, "w%d_1" % r] + ["cw%d_%d" % (r, l) for l in range(3)] + ["wc%d%d" % (r, b) for b in range(3)]
+        return ["z%d" % r] + ["w%d_%d" % (r, k) for k in range(3)] + ["cw%d_%d" % (r, l) for l in range(3)] + \
+            ["wc%d%d" % (r, b) for b in range(3)]
 
     def splice(r):
-        w = ["w%d_0" % r, "w%d_1" % r]
+        w = ["w%d_%d" % (r, k) for k in range(3)]
         od = T.OU[:]
         kp = ["kp0", "kp1"]
         ac(T.ws[:, 0:448], BG[r][:, 0:HB].indirect(T.WU[:, 0:28]), Cp, pool_tokens(r) + ["WU"], ["ws0"])
@@ -463,37 +494,29 @@ def rank_program(g, core, T, topo):
         if r + 1 < RO:
             mms([(pb, T.ID[:], T.ws[:, 0:B], True, False), (pb, T.NI[:], hown(r, 0, B), False, True)],
                 ["ID", "NI", "ws0", "h%d" % r], ["pb"], ["pA"])
-        for h in range(2):
-            c0, c1, _ = HV[h]
-            mms(([] if h else [(pT[0][:], T.ID[:], T.TB[:], True, False)]) +
-                [(pT[h][:, 0:16 * (c1 - c0)], sel(T.FM, 3 + l), T.G[:, l * V + 16 * c0:l * V + 16 * c1], False, l == 2) for l in range(3)],
-                ["FM", "ID", "TB", "G0", "G1", "G2", "Gb0", "Gb1", "Gb2"], ["pT%d" % h], ["pT%d" % h])
         ac(twin(r, 0, 512), pT[0][:], Cp, ["pT0"], ["TT0"], ["pT0"])
         ac(twin(r, 512, V), pT[1][:, 0:384], Cp, ["pT1"], ["TT1"], ["pT1"])
         for h in range(2):
             tt(T.tt[:, 448 * h:448 * (h + 1)], hwin(r, 0, X).indirect(T.OU[:, 28 * h:28 * (h + 1)]),
                T.ws[:, 448 * h:448 * (h + 1)], A.subtract, ["hw%d" % r, "hc%d" % r, "OU", "ws%d" % h], ["tt%d" % h])
-            if h == 0 and r + 1 < RO:
-                ts(T.hyb[:], pb, 0.0, 255.6, A.max, A.add, ["pb"], ["hyb"], ["pA"])
-                mms([(pb, T.ID[:], hown(r, 0, B), True, False), (pb, T.HI[:], T.hyb[:], False, True)],
-                    ["ID", "HI", "hyb", "h%d" % r], ["pb"], ["pA"])
-                ac(hwin(r + 1, ub, ub + B), pb, I, ["pb"], ["hb%d" % (r + 1)], ["pA"], bias=-128.0)
-                send(hwin(r + 1, ub, ub + B), "mh%d" % (r + 1), ["hb%d" % (r + 1)], "hf%d" % (r + 1))
-        tt(T.HIs[:], T.HP[:], T.gm[:], A.add, ["HP0", "HP1", "gm"], ["HIs"])
         ac(T.Fg[:], twin(r).indirect(od), Cp, ["TT0", "TT1", "tb%d" % r, "tf%d" % r, "OU"], ["Fg"])
+        if r + 1 < RO:
+            ts(T.hyb[:], pb, 0.0, 255.6, A.max, A.add, ["pb"], ["hyb"], ["pA"])
+            mms([(pb, T.ID[:], hown(r, 0, B), True, False), (pb, T.HI[:], T.hyb[:], False, True)],
+                ["ID", "HI", "hyb", "h%d" % r], ["pb"], ["pA"])
+            ac(hwin(r + 1, ub, ub + B), pb, I, ["pb"], ["hb%d" % (r + 1)], ["pA"], bias=-128.0)
+            send(hwin(r + 1, ub, ub + B), "mh%d" % (r + 1), ["hb%d" % (r + 1)], "hf%d" % (r + 1))
+        tt(T.HIs[:, :, 0:32], T.HP[:, :, 0:32], T.gm[:, :, 0:32], A.add, ["HP0", "gm0", "gm1", "gm2"], ["HIs0"])
         ac(T.wd2[:], wblk(r, 2, 0, X).indirect(od), Cp, w + ["wc%d2" % r, "OU"], ["wd2"])
-        lst = [(T.pK[:, 0:400], T.ID[:], T.TIE[:], True, False)]
-        for c in range(3):
-            lst += [(T.pK[:, c:392:7], sel(T.QK, i), BG[r][:, (6 - c) * X + i:(6 - c) * X + V:16], False, False) for i in range(16)]
-        lst += [(T.pK[:, c:392:7], T.ID[:], T.nh[:, 0], False, False) for c in range(6)]
-        mms(lst, ["ID", "QK", "nh0"] + w + TIE, kp, ["pK"])
+        own_sums(r, (1, 2))
+        mms([(T.pK[:, c:392:7], T.ID[:], T.nh[:, 0], False, False) for c in range(6)], ["ID", "nh0"], kp, ["pK"])
         lst = [(T.pN[:, 0:400], T.ID[:], BG[r][:, 0:400], True, False)]
         for c in range(6):
             o = T.pN[:, c:392:7]
             lst += [(o, T.NI[:], T.sl[:], False, False), (o, T.NI[:], T.sh[:], False, False)]
             if c < 3:
                 lst += [(o, T.ID[:], T.LOs[:, c], False, False), (o, T.ID[:], T.HIs[:, c], False, False)]
-        mms(lst, ["ID", "NI", "sl", "sha", "shb", "LOs0", "LOs1", "HIs", "z%d" % r], ["pN"], ["pN"])
+        mms(lst, ["ID", "NI", "sl", "sha", "shb", "LOs0", "LOs1", "HIs0", "HIs1", "z%d" % r], ["pN"], ["pN"])
 
         def cw(l, a=0, b=V):
             return BG[r][:, (3 - l) * X + a:(3 - l) * X + b]
@@ -503,8 +526,6 @@ def rank_program(g, core, T, topo):
                  for i in range(16)], ["QK", "cw%d_%d" % (r, l)], kp, ["pK"])
         for l in range(2):
             tt(cw(l), wblk(r, l, 0, X).indirect(od), T.tt[:], A.subtract, w + ["wc%d%d" % (r, l), "OU", "tt0", "tt1"], ["cw%d_%d" % (r, l)])
-            if l == 0:
-                tt(T.ON[:], T.RF[:], T.nh[:], A.mult, ["RF0", "RF1", "nh0", "nh1", "nh2"], ["ON"])
             ts(cw(l), cw(l), 0.0, 255.0, A.max, A.min, ["cw%d_%d" % (r, l)], ["cw%d_%d" % (r, l)])
         mms([(T.pN[:, 3 + l:392:7], sel(T.QF[:, l, :], i), T.Fg[:, i:V:16], False, l == 2 and i == 15)
              for l in range(3) for i in range(16)], ["QF0", "QF1", "QF2", "Fg"], ["pN"], ["pN"])
@@ -514,19 +535,21 @@ def rank_program(g, core, T, topo):
                  (pH[h][:, 0:448], T.NI[:], T.tt[:, 448 * h:448 * (h + 1)], False, True)],
                 ["ID", "NI", "wd2", "tt%d" % h], ["pH%d" % h], ["pH%d" % h])
         sums(1)
-        ts(T.P1[:], T.pN[:, 0:400], 0.0, None, A.is_equal, None, ["pN"], ["P1"], ["pN"])
         ac(T.P2[:], T.pN[:, 0:400], Re, ["pN"], ["P2"], ["pN"], bias=-64.0, scale=256.0)
         ac(T.n7[:, 1:401], T.pN[:, 0:400], Cp, ["pN"], ["n7"], ["pN"])
         ac(T.n7[:, 7:401:7], T.RST[:, 0:399:7], Cp, ["RST", "n7"], ["n7"])
-        for h in range(2):
-            ts(cw(2, 448 * h, 448 * (h + 1)), pH[h][:, 0:448], 0.0, 255.0, A.max, A.min, ["pH%d" % h],
-               ["cw%d_2" % r], ["pH%d" % h])
-        mms([(T.pK[:, 0:400], T.ID[:], a[:], False, False) for a in (T.P1, T.P2)], ["ID", "P1", "P2"], kp, ["pK"])
-        sums(2, True)
-        tt(T.dn[:], T.n7[:, 0:400], T.pN[:, 0:400], A.subtract, ["n7", "pN"], ["dn"], ["pN"])
         for l in range(3):
             ac(T.vbp[:, 56 * l:56 * (l + 1)], T.hx[:], I, ["hx"], ["vbp%d" % l], bias=float((6 - l) * X), scale=-float(6 - l))
+        ts(cw(2, 0, 448), pH[0][:, 0:448], 0.0, 255.0, A.max, A.min, ["pH0"], ["cw%d_2" % r], ["pH0"])
+        ts(T.P1[:], T.pN[:, 0:400], 0.0, None, A.is_equal, None, ["pN"], ["P1"], ["pN"])
+        ts(cw(2, 448, V), pH[1][:, 0:448], 0.0, 255.0, A.max, A.min, ["pH1"], ["cw%d_2" % r], ["pH1"])
+        mms([(T.pK[:, 0:400], T.ID[:], a[:], False, False) for a in (T.P2, T.P1)], ["ID", "P1", "P2"], kp, ["pK"])
+        sums(2, True)
+        tt(T.dn[:], T.n7[:, 0:400], T.pN[:, 0:400], A.subtract, ["n7", "pN"], ["dn"], ["pN"])
+        tt(T.ON[:], T.RF[:], T.nh[:], A.mult, ["RF0", "RF1", "nh0", "nh1", "nh2"], ["ON"])
+        tt(T.vb[:], T.vbp[:], T.VW[:], A.add, ["vbp0", "vbp1", "vbp2", "VW0", "VW1", "VW2"], ["vb"])
         ac(T.k0[:, 0:224], T.pK[:, 0:224], Cp, kp, ["k00"], ["pK"])
+        ac(T.k0[:, 224:400], T.pK[:, 224:400], Cp, kp, ["k01"], ["pK"])
 
     def heights(r):
         for h in range(2):
@@ -546,26 +569,40 @@ def rank_program(g, core, T, topo):
         else:
             dma("y", "dout", [(T.yh[:], hown(RO))], ["h%d" % RO], [])
 
-    def choose_steps(r, h):
-        c0, c1, n = HV[h]
-        a, b = 7 * c0, 7 * c0 + n
+    def extract(a, n, k, pad=0):
+        b = a + n
         bl = T.BL[:, 0:n // 16]
-        k = str(h)
-        kp = "kp" + k
+        h = k[0]
+        kp = "kq" + k
         st = []
         for t in range(3):
             st.append(lambda t=t: scan(T.RB[:, t, a:b], T.RST[:, a:b], T.pK[:, a:b], 0.0, A.add, A.min,
-                                       ["RST", kp], ["RB%d%d" % (t, h)], ["pK"]))
-            st.append(lambda t=t: tt(T.nq[:, a:b], T.RB[:, t, a:b + 8 * h].indirect(bl), T.k0[:, a:b], A.not_equal,
-                                     ["RB%d%d" % (t, h), "k0" + k, "BL"], ["nq" + k]))
+                                       ["RST", kp, "kp" + h], ["RB%d%s" % (t, k)], ["pK"]))
+            st.append(lambda t=t: tt(T.nq[:, a:b], T.RB[:, t, a:b + pad].indirect(bl), T.k0[:, a:b], A.not_equal,
+                                     ["RB%d%s" % (t, k), "k0" + h, "BL"], ["nq" + k]))
             st.append(lambda t=t: scan(T.QB[:, t, a:b], T.dn[:, a:b], T.nq[:, a:b], 4.0, A.add, A.min,
-                                       ["dn", "nq" + k], ["QB%d%d" % (t, h)]))
+                                       ["dn", "nq" + k], ["QB%d%s" % (t, k)]))
             if t < 2:
-                st.append(lambda t=t: tt(T.pen[:, a:b], T.QB[:, t, a:b + 8 * h].indirect(bl), T.n7[:, 1 + a:1 + b], A.is_equal,
-                                         ["QB%d%d" % (t, h), "n7", "BL"], ["pen" + k]))
-                st.append(lambda: tt(T.pK[:, a:b], T.pK[:, a:b], T.pen[:, a:b], A.add, [kp, "pen" + k], [kp], ["pK"]))
-        rb = ["RB%d%d" % (t, h) for t in range(3)]
-        qb = ["QB%d%d" % (t, h) for t in range(3)]
+                st.append(lambda t=t: tt(T.pen[:, a:b], T.QB[:, t, a:b + pad].indirect(bl), T.n7[:, 1 + a:1 + b], A.is_equal,
+                                         ["QB%d%s" % (t, k), "n7", "BL"], ["pen" + k]))
+                st.append(lambda: tt(T.pK[:, a:b], T.pK[:, a:b], T.pen[:, a:b], A.add, [kp, "kp" + h, "pen" + k], [kp], ["pK"]))
+        return st
+
+    def both(x, y):
+        return [(lambda f=f, e=e: (f(), e())) for f, e in zip(x, y)]
+
+    def choose_steps(r, h):
+        c0, c1, n = HV[h]
+        a = 7 * c0
+        k = str(h)
+        if h == 0:
+            st, ks = both(extract(0, 112, "0a"), extract(112, 112, "0b")), ["0a", "0b"]
+        elif r + 1 == RO:
+            st, ks = both(extract(a, 112, "1a"), extract(a + 112, 64, "1", 8)), ["1a", "1"]
+        else:
+            st, ks = extract(a, n, "1", 8), ["1"]
+        rb = ["RB%d%s" % (t, x) for t in range(3) for x in ks]
+        qb = ["QB%d%s" % (t, x) for t in range(3) for x in ks]
         ki = lambda: ts(T.Ki[:, :, c0:c1], T.RB[:, :, a + 6:7 * c1:7], -FL, None, A.mult, None, rb, ["Ki" + k])
         xi = lambda: ts(T.xi[:, :, c0:c1], T.Ki[:, :, c0:c1], 7, None, A.bitwise_and, None, ["Ki" + k], ["xi" + k])
         st = st[:-1] + [lambda f=st[-1]: (ki(), f(), xi())]
@@ -587,14 +624,14 @@ def rank_program(g, core, T, topo):
             src = BG[r][:, 0:HB].indirect(T.EU[:, t, c0:c1])
             R = pool_tokens(r) + ["EU%d" % h]
             if r + 1 < RO:
-                ac(wblk(r + 1, t, 16 * c0, 16 * c1), src, Cp, R, ["w%d_%d" % (r + 1, h)])
+                o, tok = wblk(r + 1, t, 16 * c0, 16 * c1), "w%d_%d" % (r + 1, h if eng[t] == "s" else 2)
             else:
-                o = T.WF[:, t * V + 16 * c0:t * V + 16 * c1]
-                tok = "wf%d%d" % (t, h)
-                if eng[t] == "s":
-                    ac(o, src, Cp, R, [tok])
-                else:
-                    cp(o, src, R, [tok])
+                o, tok = T.WF[:, t * V + 16 * c0:t * V + 16 * c1], "wf%d%d" % (t, h)
+            if eng[t] == "s":
+                ac(o, src, Cp, R, [tok])
+            else:
+                cp(o, src, R, [tok])
+            if r + 1 == RO:
                 dma("y", "dout", [(T.yw[:, t * V + 16 * c0:t * V + 16 * c1], o)], [tok], [])
 
     def run(*lists):
@@ -606,47 +643,48 @@ def rank_program(g, core, T, topo):
     nop = [lambda: None]
 
     def tb(r, a, b):
-        return lambda: table(r, 0, a, b)
+        return lambda: table(r, a, b)
 
     votes(0, 0)
     vs = votes_scalar(0)
+    vs[0]()
+    vs[1]()
     db = deaths_steps(0, 0)
-    run(db[:7], nop * 4 + vs[:1] + nop + vs[1:2])
+    run(db[:7])
     vs[2]()
     for r in range(RO):
         d1, d2 = deaths_steps(r, 1), deaths_steps(r, 2)
         if r == 0:
-            votes(r, 2, [db[7:12], db[12:14], d1[:4]])
-            d1[4]()
+            votes(r, 2, [db[7:12], db[12:14], d1])
+            late_consts()
             border_names()
         else:
-            new_weights(r - 1, 1, which=(0, 1))
-            votes(r, 2, [d1[:1], d1[1:2] + [lambda: low_names(1)], d1[2:4]])
-            d1[4]()
-            new_weights(r - 1, 1, which=(2,))
+            votes(r, 2, [db[13:] + [lambda: split_names(1), lambda: new_weights(r - 1, 1, which=(0, 1))], [], []])
+            run(d1[:3], [lambda: low_names(1)])
+            table(r, 13, 16)
+            run(d1[3:])
             border_names()
-        run(d2)
-        mark_names()
+        run(d2[:4])
+        if r:
+            new_weights(r - 1, 1, "vvv", which=(2,))
+        d2[4]()
         gone(r)
         splice(r)
-        run(choose_steps(r, 0),
-            [lambda: ac(T.k0[:, 224:400], T.pK[:, 224:400], Cp, ["kp1"], ["k01"], ["pK"]),
-             lambda: tt(T.vb[:], T.vbp[:], T.VW[:], A.add, ["vbp0", "vbp1", "vbp2", "VW0", "VW1", "VW2"], ["vb"]),
-             lambda: heights(r)])
+        heights(r)
+        run(choose_steps(r, 0))
         if r + 1 < RO:
             split_names(0)
             new_weights(r, 0)
             votes(r + 1, 0)
             db = deaths_steps(r + 1, 0)
-            vs = votes_scalar(r + 1)
+            vs = votes_scalar(r + 1, tb(r + 1, 9, 13))
             run(choose_steps(r, 1),
-                [lambda: (low_names(0), table(r + 1, 0, 0, 4)), nop[0]] + db[:4] + [tb(r + 1, 4, 7), db[5], vs[0]] + db[6:13],
-                nop * 9 + [vs[1], tb(r + 1, 7, 9)] + nop * 3 + [vs[2], tb(r + 1, 9, 16)])
-            db[13]()
-            split_names(1)
+                [lambda: (low_names(0), table(r + 1, 0, 4), vs[0]()), nop[0]] + db[:4] + [tb(r + 1, 4, 6), db[5]] + db[6:13],
+                nop * 8 + [vs[1], tb(r + 1, 6, 9)] + nop * 3 + [vs[2]])
         else:
             new_weights(r, 0)
             run(choose_steps(r, 1))
+            new_weights(r, 1, "svv")
             ac(T.q128[:], T.NF3[:], I, ["NF0", "NF1"], ["q128"], bias=192.0 - (UB + 79.5) / B, scale=1 / (SC * B))
             ac(T.fa[:], T.q128[:], I, ["q128"], ["fa"], bias=-192.0 * 864 - UB - 1024.0 * rk, scale=864.0)
             ts(T.fb[:], T.NF3[:], UB * SC, None, A.is_ge, None, ["NF0", "NF1"], ["fb"])
@@ -654,6 +692,5 @@ def rank_program(g, core, T, topo):
             tt(T.fa[:], T.fa[:], T.fb[:], A.mult, ["fa", "fb"], ["fa"])
             tt(T.YN[:], T.fa[:], T.h32[:], A.add, ["fa", "h320"], ["YN"])
             dma("y", "dout", [(T.yn[:], T.YN[:])], ["YN"], [])
-            new_weights(r, 1, "svv")
     for k, n in cnt.items():
         g.wait_ge(T.sem[k], n)

@@ -2,16 +2,21 @@ from concourse.bass import DstId, RemoteDMATransfer
 from concourse.mybir import AluOpType as A, ActivationFunctionType as F
 
 V, B, CAP, NR, RO = 896, 160, 48, 6, 3
-X = V + NR * CAP
-UB = X
-HW = UB + NR * B
-HB = 7 * X
+UB = V
+X = UB + NR * B
+U = X // 2
+U16 = U // 16
+W0 = 4 * U - 16
 FL = 32768.0
+GF = 8192.0
+DS = GF / FL
 SC = 2.0 ** -13
+BIG = 2.0 ** 23
 CH = [(0, 10), (10, 32), (32, 56)]
 HV = [(0, 32, 224), (32, 56, 176)]
+HS = [(0, 512), (512, V)]
 
-bf, f4, i4, u2 = "bfloat16", "float32", "int32", "uint16"
+bf, f2, f4, i4, u2 = "bfloat16", "float16", "float32", "int32", "uint16"
 
 
 def _s(n, d):
@@ -19,47 +24,89 @@ def _s(n, d):
 
 
 SCRATCH = {
+    "BG": _s([(4 + 6 * RO) * U], bf),
     "nbi": _s([168], i4), "ia": _s([168], i4), "ib": _s([168], i4), "fa": _s([168], f4), "fb": _s([168], f4),
-    "NU": _s([3, 56], u2), "RF": _s([3, 56], f4), "ON": _s([3, 56], f4), "EM": _s([3, 56], bf),
-    "H128": _s([3, 56], bf), "h32": _s([3, 56], f4), "LOs": _s([3, 56], bf), "HIs": _s([3, 56], bf),
-    "gm": _s([3, 56], bf), "HP": _s([3, 56], bf), "DA": _s([56], bf), "cmp": _s([2688], bf),
+    "NU": _s([3, 56], u2), "RF": _s([3, 56], f2), "NF": _s([3, 56], f2), "ON": _s([3, 56], f2), "EM": _s([3, 56], bf),
+    "PN": _s([3, 56], f4), "VA": _s([56], f4), "PA": _s([3, 56], f4), "AB": _s([2, 3, 56], f4), "m1": _s([2, 56], f4),
+    "m": _s([2, 56], i4), "oi": _s([56], i4), "OU": _s([56], u2), "WU": _s([56], u2), "nh": _s([56], bf),
+    "NH": _s([3, 56], f4), "gm": _s([3, 56], bf), "DA": _s([56], bf), "cmp": _s([2688], bf), "gI": _s([1056], bf),
     "ok": _s([176], bf), "d01": _s([56], bf), "die": _s([56], bf), "dieB": _s([16], bf), "cs": _s([16], bf),
-    "keep": _s([16], bf), "pos": _s([16], bf), "so1": _s([16], f4), "so2": _s([16], f4), "so3": _s([16], f4),
-    "SU": _s([16], u2), "LW": _s([208], bf), "LU": _s([4], u2), "tmp48": _s([48], bf), "LS": _s([3, 48], bf),
-    "G": _s([2688], bf), "Gc": _s([3, 48], bf), "TB": _s([512], bf), "TC": _s([48], bf), "TM": _s([48], bf),
-    "gI": _s([1056], bf),
-    "VI": _s([3, 56], i4), "m01": _s([56], i4), "m": _s([56], i4), "oi": _s([56], i4), "OU": _s([56], u2),
-    "hx": _s([56], f4), "a1": _s([56], i4), "a3": _s([56], f4), "a4": _s([56], f4), "WU": _s([56], u2),
-    "nh": _s([3, 56], bf), "vbp": _s([168], f4), "vb": _s([3, 56], f4), "ws": _s([V], bf), "tt": _s([V], bf),
-    "wd2": _s([V], bf), "Fg": _s([V], bf), "hr": _s([V], bf), "hy": _s([V], bf), "hyb": _s([B], bf),
-    "TT": _s([RO * X], bf), "P1": _s([400], bf), "P2": _s([400], bf), "n7": _s([408], f4), "dn": _s([400], f4),
-    "k0": _s([400], f4), "RB": _s([3, 408], f4), "QB": _s([3, 408], f4), "nq": _s([400], bf), "pen": _s([400], bf),
-    "Ki": _s([3, 56], i4), "xi": _s([3, 56], i4), "xf": _s([3, 56], f4), "ef": _s([3, 56], f4),
-    "EU": _s([3, 56], u2), "NF3": _s([3, 56], f4), "WF": _s([2688], bf), "HO": _s([4 * V], bf),
-    "YN": _s([168], f4), "q128": _s([168], bf),
+    "keep": _s([16], bf), "G": _s([2688], bf), "TB": _s([512], bf), "H8": _s([3, 56], bf), "mk": _s([B], bf), "LS": _s([RO, B], bf),
+    "ws": _s([V], bf), "tt": _s([V], bf), "wd2": _s([V], bf), "Fg": _s([V], bf), "hr": _s([V], bf), "hy": _s([V], bf),
+    "hyb": _s([B], bf), "P1": _s([3, 56], bf), "P2": _s([3, 56], bf), "n7": _s([408], f4), "dn": _s([400], f4),
+    "RB": _s([3, 400], f4), "QB": _s([3, 408], f4), "nq": _s([400], bf), "kp": _s([400], bf),
+    "Ki": _s([3, 56], i4), "xi": _s([3, 56], i4), "EU": _s([3, 56], u2), "EB": _s([30], u2),
+    "WF": _s([2688], bf), "HO": _s([4 * V], bf), "NA": _s([168], f4), "YN": _s([168], f4), "q128": _s([168], bf),
     "PI": _s([2], i4), "PF": _s([16], f4), "J": _s([144], f4), "JG": _s([128], f4), "QS": _s([144], bf),
-    "QK": _s([144], bf), "QH": _s([144], bf), "FM": _s([144], bf), "QF": _s([3, 144], bf), "PT": _s([16, 144], bf),
-    "OH": _s([16], f4), "ID": _s([128], bf), "NI": _s([128], bf), "HI": _s([128], bf), "ONE": _s([128], bf),
-    "TRI": _s([128], bf), "tri0": _s([128], bf), "CT": _s([V], bf), "cl": _s([56], bf), "chh": _s([56], bf),
-    "VW": _s([3, 56], f4), "SF": _s([3, 56], f4), "sl": _s([56], bf), "sh": _s([56], bf), "slf": _s([56], f4),
-    "shf": _s([56], f4), "PR": _s([168], bf), "TIE": _s([400], bf), "RST": _s([400], f4), "BL": _s([14], u2),
-    "bli": _s([14], i4), "c48": _s([16], f4), "o16": _s([16], bf),
+    "Q3": _s([144], bf), "Q2": _s([144], bf), "QK": _s([144], bf), "QH": _s([144], bf), "FM": _s([144], bf),
+    "QF": _s([3, 144], bf), "PT": _s([16, 144], bf), "PB": _s([16, 144], bf), "OH": _s([16], f4), "O3": _s([6], f4),
+    "ID": _s([128], bf), "NI": _s([128], bf), "HI": _s([128], bf), "IB": _s([128], bf), "IU": _s([128], bf),
+    "S6": _s([128], bf), "CZ": _s([512], bf), "ONE": _s([128], bf), "TRI": _s([128], bf), "tri0": _s([128], bf),
+    "c16": _s([56], f4), "VW": _s([56], f4), "SF": _s([3, 56], f2), "T7": _s([406], bf), "POS": _s([400], bf),
+    "RST": _s([400], f4), "BL": _s([14], u2), "bli": _s([14], i4), "o16": _s([16], bf), "k6": _s([2, 56], bf),
     "pA": ("psum", [128, 512], f4), "pV": ("psum", [128, 512], f4), "pN": ("psum", [128, 512], f4),
     "pK": ("psum", [128, 512], f4), "pT0": ("psum", [128, 512], f4), "pT1": ("psum", [128, 512], f4),
     "pH0": ("psum", [128, 512], f4), "pH1": ("psum", [128, 512], f4),
 }
 for _r in range(RO):
-    SCRATCH["BG%d" % _r] = _s([HB + HW], bf)
-    SCRATCH["DW%d" % _r] = _s([HW], bf)
-    SCRATCH["LA%d" % _r] = _s([NR, 4 * CAP], bf)
+    SCRATCH["HW%d" % _r] = _s([X], bf)
+    SCRATCH["DW%d" % _r] = _s([X], bf)
+    SCRATCH["TT%d" % _r] = _s([X], bf)
+    SCRATCH["SB%d" % _r] = _s([3 * B], bf)
 
-SEMAPHORES = ["cv", "cs", "ct", "cg", "snt", "dnb", "dhb", "dh", "dw", "dz0", "dz1", "dout"] + \
-    ["%s%d" % (k, r) for k in ("mh", "md", "ma", "mb") for r in range(RO)]
+SEMAPHORES = ["cv", "cs", "ct", "cg", "snt", "dnb", "dhb", "dh", "dw", "dsb", "dout"] + \
+    ["%s%d" % (k, r) for k in ("mh", "md", "mb", "mw", "ho", "dc") for r in range(RO)]
+
+
+def unit(r, l):
+    return 8 + 6 * r - 2 * l
+
+
+def peers_of(core, T, turn=0):
+    k = T.rank_of(core)
+    p = list(T.cores[k + 1:]) + list(T.cores[:k])
+    return p[turn:] + p[:turn]
+
+
+def carriers(core, peers, topo):
+    return [c for c in topo.cores_of(core) if topo.die(c) != topo.die(core) and all(topo.may_write(c, p) for p in peers)][:2]
+
+
+def common_mask(core, dsts, topo):
+    mask = -1
+    for c in dsts:
+        mask &= topo.mask(core, c)
+    return mask, len([e for e in topo.engines(core, dsts[0]) if mask >> e & 1])
+
+
+def ids_of(core, dsts, topo):
+    return [DstId(rid=topo.addr(c, core)[0], pnc=topo.addr(c, core)[1]) for c in dsts]
+
+
+def spare(core, near, peers, topo):
+    return [e for e in topo.engines(core, near) if not common_mask(core, peers, topo)[0] >> e & 1]
+
+
+def carrier_program(g, core, owner, k, T, topo):
+    peers = peers_of(owner, T, 2 * k)
+    mask, ne = common_mask(core, peers, topo)
+    ub = UB + B * T.rank_of(owner)
+    for r in range(RO):
+        g.wait_ge(T.sem["ho%d" % r], len(spare(owner, core, peers, topo)) // 2)
+        o = unit(r, k) * U + ub
+        g.remote_dma_fused([RemoteDMATransfer(dst_ids=ids_of(core, peers, topo), dma_engine_mask=mask, remote_sem=T.sem["mw%d" % r],
+                                              src=T["SB%d" % r][:, k * B:(k + 1) * B], dsts=[T.BG[:, o:o + B]] * len(peers))],
+                           local_sem=T.sem.snt)
+    g.wait_ge(T.sem.snt, RO * ne)
 
 
 def rank_program(g, core, T, topo):
     rk = T.rank_of(core)
     if rk is None:
+        for owner in T.cores:
+            cs = carriers(owner, peers_of(owner, T), topo)
+            if core in cs:
+                carrier_program(g, core, owner, cs.index(core), T, topo)
         return
     Q = {"v": g.vector, "s": g.scalar, "t": g.tensor, "g": g, "y": g.sync}
     cnt = {"cv": 0, "cs": 0, "ct": 0, "cg": 0}
@@ -112,12 +159,11 @@ def rank_program(g, core, T, topo):
             cnt[sem] = cnt.get(sem, 0) + 16
         note((sem, cnt[sem]), R, W, ())
 
-    peers = [c for c in T.cores if c != core]
-    mask = -1
-    for c in peers:
-        mask &= topo.mask(core, c)
-    ne = len([e for e in topo.engines(core, peers[0]) if mask >> e & 1])
-    ids = [DstId(rid=topo.addr(c, core)[0], pnc=topo.addr(c, core)[1]) for c in peers]
+    peers = peers_of(core, T)
+    mask, ne = common_mask(core, peers, topo)
+    ids = ids_of(core, peers, topo)
+    cars = carriers(core, peers, topo)
+    on = spare(core, cars[0], peers, topo)
 
     def send(ap, sem, R, tok, src=None):
         need("g", R, [], ())
@@ -126,6 +172,18 @@ def rank_program(g, core, T, topo):
         cnt["snt"] = cnt.get("snt", 0) + ne
         cnt[sem] = ne * len(ids)
         wr[tok] = (sem, cnt[sem])
+
+    def hand_over(r):
+        sb = T["SB%d" % r]
+        need("g", ["sb%d" % r], [], ())
+        g.remote_dma_fused([RemoteDMATransfer(dst_ids=ids_of(core, [c], topo), dma_engine_mask=sum(1 << e for e in on[k::2]),
+                                              remote_sem=T.sem["ho%d" % r], src=sb[:, k * B:(k + 1) * B], dsts=[sb[:, k * B:(k + 1) * B]])
+                            for k, c in enumerate(cars)], local_sem=T.sem.snt)
+        cnt["snt"] += len(on)
+        o = unit(r, 2) * U + UB + B * rk
+        send(T.BG[:, o:o + B], "mw%d" % r, [], "wf%d" % r, sb[:, 2 * B:3 * B])
+        cnt["mw%d" % r] = 3 * ne * len(ids)
+        wr["wf%d" % r] = ("mw%d" % r, cnt["mw%d" % r])
 
     v, s = g.vector, g.scalar
 
@@ -152,84 +210,93 @@ def rank_program(g, core, T, topo):
         op("g", (lambda: g.iota(o, pat, base, cm, allow_small_or_imprecise_dtypes=True)) if fl else
            (lambda: g.iota(o, pat, base, cm)), [], W)
 
-    BG = [T["BG%d" % r] for r in range(RO)]
+    BG = T.BG
+    HW = [T["HW%d" % r] for r in range(RO)]
     DW = [T["DW%d" % r] for r in range(RO)]
-    LA = [T["LA%d" % r] for r in range(RO)]
+    TT = [T["TT%d" % r] for r in range(RO)]
+    SB = [T["SB%d" % r] for r in range(RO)]
     ub = UB + B * rk
     pT, pH = [T.pT0, T.pT1], [T.pH0, T.pH1]
+    pv, bv = [T.pV, T.pN], ["pV", "pN"]
     I, Re, Cp = F.Identity, F.Relu, F.Copy
 
     def wblk(r, l, a=0, b=V):
-        return BG[r][:, (6 - l) * X + a:(6 - l) * X + b]
+        return BG[:, unit(r, l) * U + a:unit(r, l) * U + b]
 
-    def hwin(r, a=0, b=V):
-        return BG[r][:, HB + a:HB + b]
+    def cw(l, a=0, b=V):
+        return BG[:, (3 - l) * U + a:(3 - l) * U + b]
 
     def hown(r, a=0, b=V):
         return T.HO[:, r * V + a:r * V + b]
 
-    def twin(r, a=0, b=X):
-        return T.TT[:, r * X + a:r * X + b]
-
     def sel(tab, i):
         return tab[:, 15 - i:143 - i]
 
-    def split_names(h):
-        c0, c1, _ = HV[h]
-        k = str(h)
-        ac(T.H128[:, :, c0:c1], T.NF3[:, :, c0:c1], I, ["NF" + k], ["H128" + k], bias=127.516, scale=256.0)
-        ac(T.h32[:, :, c0:c1], T.H128[:, :, c0:c1], I, ["H128" + k], ["h32" + k], bias=0.5, scale=-1 / 256.0)
-        ac(T.HP[:, :, c0:c1], T.H128[:, :, c0:c1], I, ["H128" + k], ["HP" + k], bias=-0.5, scale=1 / 256.0)
-
-    def low_names(h):
-        c0, c1, _ = HV[h]
-        tt(T.LOs[:, :, c0:c1], T.NF3[:, :, c0:c1], T.h32[:, :, c0:c1], A.add, ["NF%d" % h, "h32%d" % h], ["LOs%d" % h])
-
     PT = ["PT%d" % i for i in range(16)]
-    TIE = ["TIE"] + ["TIE%d" % c for c in range(1, 6)]
+    PB = ["PB%d" % i for i in range(16)]
+    POS = ["POS%d" % c for c in range(6)]
+    SF = ["SFa", "SFb"]
 
-    def table(r, i0, i1):
-        c0, c1, _ = HV[0]
+    def wown(r):
+        return ["w%d_%d" % (r, k) for k in range(4)]
+
+    def wall(r):
+        return wown(r) + ["wb%d" % r, "wf%d" % r]
+
+    def hall(r):
+        return ["hw%d" % r, "hb%d" % r, "hf%d" % r]
+
+    def run(*lists):
+        for k in range(max(len(x) for x in lists)):
+            for x in lists:
+                if k < len(x):
+                    x[k]()
+
+    def table(h, i0, i1):
+        c0, c1, _ = HV[h]
         n = 16 * (c1 - c0)
-        lst = [(pT[0][:, 0:n], T.ID[:], BG[r][:, 0:n], True, False)] if i0 == 0 else []
+        b = "pT%d" % h
+        lst = [(pT[h][:, 0:n], T.ID[:], T.CZ[:, 0:n], True, False)] if i0 == 0 else []
         for i in range(i0, i1):
             for l in range(3):
-                lst += [(pT[0][:, i:n:16], sel(T.PT[:, i, :], l), T.LOs[:, l, c0:c1], False, False),
-                        (pT[0][:, i:n:16], sel(T.PT[:, i, :], 3 + l), T.HP[:, l, c0:c1], False, i == 15 and l == 2)]
-        mms(lst, ["ID", "z%d" % r, "LOs0", "HP0"] + PT, ["pT0"], ["pT0"])
+                lst += [(pT[h][:, i:n:16], sel(T.PT[:, i, :], 3 + l), T.NF[:, l, c0:c1], False, False),
+                        (pT[h][:, i:n:16], sel(T.PB[:, i, :], l), T.H8[:, l, c0:c1], False, h == 0 and i == 15 and l == 2)]
+        mms(lst, ["ID", "CZ", "NF%d" % h, "H8%d" % h] + PT + PB, [b], [b])
 
-    def table1(r, hi):
-        c0, c1, _ = HV[1]
-        n = 16 * (c1 - c0)
-        lst = [] if hi else [(pT[1][:, 0:n], T.ID[:], BG[r][:, 0:n], True, False)]
-        lst += [(pT[1][:, i:n:16], sel(T.PT[:, i, :], 3 * hi + l), (T.HIs if hi else T.LOs)[:, l, c0:c1], False,
-                 hi == 1 and i == 15 and l == 2) for i in range(16) for l in range(3)]
-        mms(lst, ["ID", "z%d" % r, "HIs1" if hi else "LOs1"] + PT, ["pT1"], ["pT1"])
+    def high_names(h):
+        c0, c1, _ = HV[h]
+        ts(T.H8[:, :, c0:c1], T.NF[:, :, c0:c1], 256.0, 127.516, A.mult, A.add, ["NF%d" % h], ["H8%d" % h])
 
-    def own_sums(r, cs):
-        lst = [(T.pK[:, 0:400], T.ID[:], T.TIE[:], True, False)] if cs[0] == 0 else []
-        for c in cs:
-            lst += [(T.pK[:, c:392:7], sel(T.QK, i), BG[r][:, (6 - c) * X + i:(6 - c) * X + V:16], False, False) for i in range(16)]
-        mms(lst, ["ID", "QK"] + ["w%d_%d" % (r, k) for k in range(3)] + TIE, ["kp0", "kp1"], ["pK"])
+    def keep_table():
+        ac(T.TB[:], pT[0][:], Cp, ["pT0"], ["TB"], ["pT0"])
 
-    dma("y", "dhb", [(hwin(0, ub, ub + B), T.h0[:, 0:B])], [], ["hb0"])
+    def mark_inner():
+        ts(T.mk[:], T.TB[:, 0:B], T.O3[:, 3:4], 0.5, A.is_lt, A.mult, ["TB", "O33"], ["mk"])
+
+    def own_sums(r):
+        lst = [(T.pK[:, 0:400], T.NI[:], T.T7[:, 0:400], True, False), (T.pK[:, 0:400], T.IU[:], T.POS[:], False, False)]
+        if r:
+            lst += [(T.pK[:, c:392:7], T.IU[:], T.k6[:, r - 1], False, False) for c in range(3)]
+        for c in range(3):
+            lst += [(T.pK[:, c:392:7], sel(T.QK, i), BG[:, unit(r, c) * U + i:unit(r, c) * U + V:16], False, False) for i in range(16)]
+        mms(lst, ["NI", "IU", "QK", "T7", "k6"] + POS + wown(r), ["kp0", "kp1"], ["pK"])
+
+    dma("y", "dhb", [(HW[0][:, ub:ub + B], T.h0[:, 0:B])], [], ["hb0"])
     dma("s", "dnb", [(T.nbi[:], T.nb[:])], [], ["nbi"])
-    dma("y", "dh", [(hown(0), T.h0[:]), (hwin(0), T.h0[:])], [], ["h0", "hw0"])
-    dma("s", "dw", [(wblk(0, l), T.w0[:, l * V:(l + 1) * V]) for l in range(3)], [], ["w0_0", "w0_1", "w0_2"])
+    dma("y", "dsb", [(SB[0][:, l * B:(l + 1) * B], T.w0[:, l * V:l * V + B]) for l in range(3)], [], ["sb0"])
+    dma("s", "dh", [(hown(0), T.h0[:]), (HW[0][:, 0:V], T.h0[:])], [], ["h0", "hw0"])
+    dma("y", "dw", [(wblk(0, l), T.w0[:, l * V:(l + 1) * V]) for l in range(3)], [], wown(0))
+    dma("y", "dc0", [(wblk(0, l, ub, ub + B), T.w0[:, l * V:l * V + B]) for l in range(3)], [], ["wb0"])
     io(T.PI[:, 0:1], [[0, 1]], 0, 1, ["PI0"], False)
     io(T.J[:], [[1, 144]], 0, 0, ["J"])
-    io(T.chh[:], [[16, 56]], 0, 0, ["chh"])
+    io(T.c16[:], [[16, 56]], 0, 0, ["c16"])
     io(T.JG[:], [[16, 8], [0, 16]], 0, 0, ["JG"])
-    io(T.slf[:], [[0, 28], [16, 2]], 0, 0, ["slf"])
-    io(T.shf[:], [[1, 28], [0, 2]], 0, 0, ["shf"])
-    send(hwin(0, ub, ub + B), "mh0", ["hb0"], "hf0")
+    send(HW[0][:, ub:ub + B], "mh0", ["hb0"], "hf0")
+    hand_over(0)
+    io(T.T7[:], [[1, 58], [0, 7]], 0, 0, ["T7"])
 
-    ms(BG[0][:, 0:X], 0.0, ["z0"])
-    dma("y", "dz0", [(BG[0][:, k * X:(k + 1) * X], BG[0][:, 0:X]) for k in (1, 2, 3)], ["z0"], ["cw0_0", "cw0_1", "cw0_2"])
-    dma("y", "dz1", [(BG[r][:, 0:4 * X], BG[0][:, 0:4 * X]) for r in range(1, RO)], ["z0", "cw0_0", "cw0_1", "cw0_2"],
-        ["z1", "z2", "cw1_0", "cw1_1", "cw1_2", "cw2_0", "cw2_1", "cw2_2"])
     p, pm, pg = T.PF[:, 0:1], T.PF[:, 1:2], T.PF[:, 2:3]
-    c_b, c_y = T.PF[:, 3:4], T.PF[:, 4:5]
+    ms(BG[:, 0:U], 0.0, ["z"])
     ts(T.PI[:, 1:2], T.PI[:, 0:1], 15, None, A.bitwise_and, None, ["PI0"], ["PI1"])
     ms(T.DA[:], 0.0, ["DA0", "DA1", "DA2"])
     cp(T.PF[:, 0:2], T.PI[:, 0:2], ["PI0", "PI1"], ["PF"])
@@ -237,28 +304,19 @@ def rank_program(g, core, T, topo):
     tt(pg, p, pm, A.subtract, ["PF"], ["pg"])
     ts(T.OH[:], T.J[:, 0:16], pm, None, A.is_equal, None, ["J", "PF"], ["OH"])
     ts(T.QS[:], T.J[:], pg, 15.0, A.subtract, A.is_equal, ["J", "pg"], ["QS"])
-    ts(T.VW[:, 0, :], T.chh[:], pm, None, A.add, None, ["PF", "chh"], ["VW0"])
+    ts(T.VW[:], T.c16[:], pm, None, A.add, None, ["PF", "c16"], ["VW"])
+    ts(T.Q3[:], T.J[:], pg, 18.0, A.subtract, A.is_equal, ["J", "pg"], ["Q3"])
     ts(T.ID[:], T.J[:, 0:128], p, None, A.is_equal, None, ["J", "PF"], ["ID"])
-    ts(T.cl[:], T.chh[:], 0.0, pm, A.mult, A.add, ["PF", "chh"], ["cl"])
+    tt(T.Q3[:], T.QS[:], T.Q3[:], A.subtract, ["QS", "Q3"], ["Q3"])
+    ts(T.Q2[:], T.Q3[:], 1 / 256.0, None, A.mult, None, ["Q3"], ["Q2"])
     for l in range(3):
-        ac(T.SF[:, l, 0:10], T.VW[:, 0, 0:10], I, ["VW0"], ["SFa%d" % l], bias=ub * SC, scale=SC)
-        ac(T.SF[:, l, 10:56], T.VW[:, 0, 10:56], I, ["VW0"], ["SFb%d" % l], scale=SC)
-    SF = ["SFa0", "SFa1", "SFa2", "SFb0", "SFb1", "SFb2"]
-    for i in range(16):
-        if i < 11:
-            ts(T.PT[:, i, :], T.QS[:], T.OH[:, i:i + 1], None, A.mult, None, ["QS", "OH"], [PT[i]])
-        else:
-            ac(T.PT[:, i, :], T.QS[:], I, ["QS", "OH"], [PT[i]], scale=T.OH[:, i:i + 1])
+        ts(T.SF[:, l, 0:10], T.VW[:, 0:10], float(ub), SC, A.add, A.mult, ["VW"], ["SFa"])
+        ts(T.SF[:, l, 10:56], T.VW[:, 10:56], SC, None, A.mult, None, ["VW"], ["SFb"])
     ac(T.NI[:], T.ID[:], I, ["ID"], ["NI"], scale=-1.0)
     ac(T.QH[:], T.QS[:], I, ["QS"], ["QH"], scale=0.5)
-    for b in range(2):
-        c0, c1, _ = HV[b]
-        n = 16 * (c1 - c0)
-        lst = [(pH[b][:, 0:n], T.ID[:], BG[0][:, 0:n], True, False)]
-        for i in range(16):
-            lst += [(pH[b][:, i:n:16], sel(T.PT[:, i, :], 0), T.cl[:, c0:c1], False, False),
-                    (pH[b][:, i:n:16], sel(T.PT[:, i, :], 1), T.chh[:, c0:c1], False, i == 15)]
-        mms(lst, ["ID", "z0", "cl", "chh"] + PT, ["pH%d" % b], ["pH%d" % b])
+    for i in range(16):
+        ac(T.PT[:, i, :], T.QS[:], I, ["QS", "OH"], [PT[i]], scale=T.OH[:, i:i + 1])
+        ac(T.PB[:, i, :], T.Q2[:], I, ["Q2", "OH"], [PB[i]], scale=T.OH[:, i:i + 1])
     ts(T.ia[:], T.nbi[:], 10, None, A.arith_shift_right, None, ["nbi"], ["ia"])
     ts(T.ib[:], T.nbi[:], 1023, None, A.bitwise_and, None, ["nbi"], ["ib"])
     ts(T.fa[:], T.ia[:], float(B), float(UB), A.mult, A.add, ["ia"], ["fa"])
@@ -267,82 +325,78 @@ def rank_program(g, core, T, topo):
     tt(T.fa[:], T.fa[:], T.fb[:], A.mult, ["fa", "fb"], ["fa"])
     ts(T.tri0[:], T.J[:, 0:128], p, -1.0, A.is_lt, A.mult, ["J", "PF"], ["tri0"])
     tt(T.fa[:], T.fa[:], T.ib[:], A.add, ["fa", "ib"], ["fa"])
-    for r in range(RO):
-        ms(hwin(r, V, X), 0.0, ["hc%d" % r])
-    ts(T.NF3[:], T.fa[:], SC, None, A.mult, None, ["fa"], ["NF0", "NF1"])
+    ts(T.O3[:, 0:1], pm, 3.0, None, A.is_lt, None, ["PF"], ["O30"])
+    ts(T.NF[:], T.fa[:], SC, None, A.mult, None, ["fa"], ["NF0", "NF1"])
     cp(T.NU[:], T.fa[:], ["fa"], ["NU0", "NU1"])
-    split_names(0)
-    split_names(1)
-    tt(T.RF[:], T.NF3[:], T.SF[:], A.subtract, ["NF0", "NF1"] + SF, ["RF0", "RF1"])
-    low_names(0)
-    table(0, 0, 16)
-    ac(T.CT[:, 0:512], pH[0][:], Cp, ["pH0"], ["CT0"], ["pH0"])
-    ac(T.CT[:, 512:V], pH[1][:, 0:384], Cp, ["pH1"], ["CT1"], ["pH1"])
+    tt(T.RF[:], T.NF[:], T.SF[:], A.subtract, ["NF0", "NF1"] + SF, ["RF0", "RF1"])
+    ts(T.O3[:, 4:5], pm, 6.0, 0.5, A.is_lt, A.mult, ["PF"], ["O34"])
+    high_names(0)
+    high_names(1)
+    tt(T.O3[:, 5:6], T.O3[:, 4:5], T.O3[:, 0:1], A.subtract, ["O30", "O34"], ["O35"])
+    ts(T.O3[:, 3:4], T.O3[:, 0:1], 1.0 + (UB - 16) * SC, -1.0, A.mult, A.add, ["O30"], ["O33"])
+    ts(T.CZ[:], BG[:, 0:512], T.O3[:, 5:6], None, A.add, None, ["z", "O35"], ["CZ"])
     ts(T.EM[:], T.RF[:], 0.0, 16.0, A.is_equal, A.mult, ["RF0", "RF1"], ["EM0", "EM1"])
     tt(T.TRI[:], T.tri0[:], T.ONE[:], A.mult, ["tri0", "ONE"], ["TRI"])
-    low_names(1)
-    ts(c_b, T.OH[:, 1:2], float(V + CAP * rk), None, A.mult, None, ["OH"], ["c_b"])
-    ts(c_y, pm, 3.0, (UB // 32) / 256.0, A.is_ge, A.mult, ["PF"], ["c_y"])
-    ts(T.c48[:, 0:10], T.VW[:, 0, 0:10], float(CAP), None, A.add, None, ["VW0"], ["c48"])
-    ms(T.LW[:], 0.0, ["LW"])
+    ts(T.S6[:], T.J[:, 0:128], p, 6.0, A.subtract, A.is_equal, ["J", "PF"], ["S6"])
+    ts(T.S6[:], T.S6[:], T.O3[:, 0:1], None, A.mult, None, ["S6", "O30"], ["S6"])
+    ac(T.QK[:], T.QS[:], I, ["QS"], ["QK"], scale=-2048.0)
+    ac(T.IB[:], T.ID[:], I, ["ID"], ["IB"], scale=BIG)
+    ac(T.IU[:], T.ID[:], I, ["ID"], ["IU"], scale=-float(U16))
+    table(0, 0, 16)
+    table(1, 0, 16)
+    ms(T.POS[:], 0.0, ["POS"])
+    ms(T.k6[:, 0], 6.0, ["k6"])
+    ms(T.k6[:, 1], 12.0, ["k6"])
+    for c in range(6):
+        op("v", lambda: v.memset(T.POS[:, c:392:7], float(unit(0, c) if c < 3 else 6 - c)), ["POS"], [POS[c]])
+    keep_table()
+    for l in range(3):
+        ms(cw(l, V, U), 0.0, ["zc%d" % l])
     for r in range(RO):
         ms(DW[r][:, 0:B], 0.0, ["dwz%d" % r])
-        ms(DW[r][:, V:X], 0.0, ["dwy%d" % r])
-    for l in range(3):
-        ms(T.PR[:, l * 56:(l + 1) * 56], 8192.0 * (2 - l), ["PR%d" % l])
-    ts(T.sl[:], T.slf[:], pm, SC, A.add, A.mult, ["slf", "PF"], ["sl"])
-    ts(T.bli[:], T.VW[:, 0, 0:14], -3.0, 1 / 7.0, A.add, A.mult, ["VW0"], ["bli"])
-    ms(T.TIE[:], -1.0, ["TIE"])
+        ms(TT[r][:, 0:B], 0.0, ["ttz%d" % r])
+    ts(T.bli[:], T.VW[:, 0:14], -3.0, 1 / 7.0, A.add, A.mult, ["VW"], ["bli"])
     ms(T.RST[:], 0.0, ["RST"])
     ms(T.n7[:, 0:8], 4.0, ["n7"])
-    ms(T.RB[:, :, 400:408], 0.0, ["RB01", "RB11", "RB21"])
     ms(T.QB[:, :, 400:408], 0.0, ["QB01", "QB11", "QB21"])
     ts(T.BL[:], T.bli[:], 7.0, 6.0, A.mult, A.add, ["bli"], ["BL"])
-    ms(T.RST[:, 0:400:7], 4.0, ["RST"])
-
-    def late_consts():
-        for c in range(6):
-            op("v", lambda: v.memset(T.TIE[:, c:392:7], -(6 - c) / FL), ["TIE"] if c else [], [TIE[c]])
-        for l in range(3):
-            tt(T.QF[:, l, :], T.PT[:, l, :], T.PT[:, 3 + l, :], A.add, PT[:6], ["QF%d" % l])
-    ac(T.QK[:], T.QS[:], I, ["QS"], ["QK"], scale=-8.0 / FL)
-    ac(T.FM[:], T.PT[:, 2, :], I, ["PT2"], ["FM"], scale=0.5 / FL)
+    ms(T.RST[:, 0:400:7], 4 * BIG, ["RST"])
+    for l in range(3):
+        tt(T.O3[:, 1:2], T.OH[:, l:l + 1], T.OH[:, l + 3:l + 4], A.add, ["OH"], ["O31"])
+        tt(T.O3[:, 2:3], T.O3[:, 1:2], T.OH[:, l + 6:l + 7], A.add, ["OH", "O31"], ["O32"])
+        ts(T.QF[:, l, :], T.QS[:], T.O3[:, 2:3], None, A.mult, None, ["QS", "O32"], ["QF%d" % l])
+    ts(T.FM[:], T.QS[:], T.OH[:, 0:1], 1.0 / GF, A.mult, A.mult, ["QS", "OH"], ["FM"])
     ac(T.HI[:], T.ID[:], I, ["ID"], ["HI"], scale=0.5)
-    ac(T.VW[:, 1, :], T.VW[:, 0, :], I, ["VW0"], ["VW1"])
-    ac(T.VW[:, 2, :], T.VW[:, 0, :], I, ["VW0"], ["VW2"])
-    ac(T.sh[:, 0:10], T.shf[:, 0:10], I, ["shf"], ["sha"], bias=(ub // 32) / 256.0, scale=1 / 256.0)
-    ac(T.sh[:, 10:56], T.shf[:, 10:56], I, ["shf"], ["shb"], scale=1 / 256.0)
-
-    def hall(r):
-        return ["hw%d" % r, "hb%d" % r, "hf%d" % r, "hc%d" % r]
+    mark_inner()
+    own_sums(0)
 
     def count_votes(k, tab):
         c0, c1 = CH[k]
         n, o = c1 - c0, 3 * c0
-        lst = [(T.pA[:, o:o + 3 * n], sel(tab, i), T.cmp[:, 48 * c0 + i:48 * c1:16], i == 0, False) for i in range(16)]
-        for l in range(3):
-            lst.append((T.pA[:, o + l * n:o + (l + 1) * n], T.ID[:], T.EM[:, l, c0:c1], False, False))
-            lst.append((T.pA[:, o + l * n:o + (l + 1) * n], T.NI[:], T.DA[:, c0:c1], False, l == 2))
-        mms(lst, ["QS", "QH", "ID", "NI", "DA%d" % k, "EM%d" % (k // 2)] + ["cmp%d%d" % (k, l) for l in range(3)],
-            ["vt%d" % k], ["pA"])
+        lst = [(T.pA[:, o:o + 3 * n], T.ID[:], BG[:, 0:3 * n], True, False)]
+        lst += [(T.pA[:, o + l * n:o + (l + 1) * n], a[:], b, False, False) for l in range(3)
+                for a, b in ((T.ID, T.EM[:, l, c0:c1]), (T.NI, T.DA[:, c0:c1]))]
+        mms(lst, ["ID", "NI", "z", "DA%d" % k, "EM%d" % (k // 2)], ["vt%d" % k], ["pA"])
+        mms([(T.pA[:, o:o + 3 * n], sel(tab, i), T.cmp[:, 48 * c0 + i:48 * c1:16], False, i == 15) for i in range(16)],
+            ["QS", "QH"] + ["cmp%d%d" % (k, l) for l in range(3)], ["vt%d" % k], ["pA"])
 
     def votes(r, k, mid=()):
         c0, c1 = CH[k]
         n = c1 - c0
         for l in range(3):
             tt(T.cmp[:, 48 * c0 + 16 * n * l:48 * c0 + 16 * n * (l + 1)],
-               hwin(r, 0, HW).indirect(T.NU[:, l, c0:c1]), hown(r, 16 * c0, 16 * c1), A.is_lt,
+               HW[r][:].indirect(T.NU[:, l, c0:c1]), hown(r, 16 * c0, 16 * c1), A.is_lt,
                hall(r) + ["h%d" % r, "NU%d" % (k // 2)], ["cmp%d%d" % (k, l)])
             for f in mid[l] if mid else ():
                 f()
         count_votes(k, T.QS)
 
-    def votes_scalar(r, mid=lambda: None):
+    def votes_scalar(r):
         c0, c1 = CH[1]
         n = 16 * (c1 - c0)
 
         def ga(l):
-            ac(T.gI[:, l * n:(l + 1) * n], hwin(r, 0, HW).indirect(T.NU[:, l, c0:c1]), Cp, hall(r) + ["NU0"], ["gI%d" % l])
+            ac(T.gI[:, l * n:(l + 1) * n], HW[r][:].indirect(T.NU[:, l, c0:c1]), Cp, hall(r) + ["NU0"], ["gI%d" % l])
 
         def df(l):
             b = "pH%d" % (l % 2)
@@ -353,7 +407,7 @@ def rank_program(g, core, T, topo):
             b = "pH%d" % (l % 2)
             ac(T.cmp[:, 48 * c0 + n * l:48 * c0 + n * (l + 1)], pH[l % 2][:, 0:n], F.Sign, [b], ["cmp1%d" % l], [b], bias=-0.5)
         return [lambda: (ga(0), ga(1)), lambda: (df(0), df(1), ga(2), sg(0)),
-                lambda: (df(2), sg(1), sg(2), mid(), count_votes(1, T.QH))]
+                lambda: (df(2), sg(1), sg(2), count_votes(1, T.QH))]
 
     def deaths_steps(r, k):
         c0, c1 = CH[k]
@@ -366,13 +420,12 @@ def rank_program(g, core, T, topo):
             ps, pn = (T.pN, "pN") if k == 1 else (pH[1], "pH1")
 
             def rows():
-                lst = [(ps[:, 0:16 * n], T.ID[:], T.CT[:, 16 * c0:16 * c1], True, False)]
-                lst += [(ps[:, i:16 * n:16], sel(T.PT[:, i, :], 2), T.die[:, c0:c1], False, i == 15) for i in range(16)]
-                mms(lst, ["ID", "CT0", "CT1", "die%d" % k] + PT, [pn], [pn])
+                mms([(ps[:, i:16 * n:16], sel(T.PT[:, i, :], 0), T.die[:, c0:c1], True, True) for i in range(16)],
+                    ["die%d" % k] + PT, [pn], [pn])
                 tt(T.DA[:, c0:c1], T.DA[:, c0:c1], T.die[:, c0:c1], A.add, ["DA%d" % k, "die%d" % k], ["DA%d" % k])
             if k == 2:
-                return st + [rows, lambda: cp(DW[r][:, 16 * c0:16 * c1], ps[:, 0:16 * n], [pn], ["dw%d%d" % (r, k)], [pn])]
-            return st + [rows, lambda: ac(DW[r][:, 16 * c0:16 * c1], ps[:, 0:16 * n], Cp, [pn], ["dw%d%d" % (r, k)], [pn])]
+                return st + [rows, lambda: ts(DW[r][:, 16 * c0:16 * c1], ps[:, 0:16 * n], DS, None, A.mult, None, [pn], ["dw%d%d" % (r, k)], [pn])]
+            return st + [rows, lambda: ac(DW[r][:, 16 * c0:16 * c1], ps[:, 0:16 * n], I, [pn], ["dw%d%d" % (r, k)], [pn], scale=DS)]
         cn = T.pA[:, 200:210]
 
         def count():
@@ -380,192 +433,172 @@ def rank_program(g, core, T, topo):
             mms([(cn, T.TRI[:], T.die[:, 0:10], True, False), (cn, T.ONE[:], T.cs[:, 0:10], False, True)],
                 ["TRI", "ONE", "die0", "cs"], ["cn"], ["pA"])
 
-        def cap():
-            ts(T.keep[:, 0:10], cn, float(CAP), None, A.is_le, None, ["cn"], ["keep"], ["pA"])
-            ts(T.pos[:, 0:10], cn, -1.0, CAP - 1.0, A.add, A.min, ["cn"], ["pos"], ["pA"])
-
         def rows0():
             tt(T.dieB[:, 0:10], T.die[:, 0:10], T.keep[:, 0:10], A.mult, ["die0", "keep"], ["dieB"])
-            lst = [(T.pV[:, 352:512], T.ID[:], BG[r][:, 0:B], True, False)]
-            for i in range(16):
-                lst.append((T.pV[:, 352 + i:512:16], sel(T.PT[:, i, :], 3), T.pos[:, 0:10], False, False))
-                lst.append((T.pV[:, 352 + i:512:16], sel(T.PT[:, i, :], 2), T.dieB[:, 0:10], False, i == 15))
-            mms(lst, ["ID", "z%d" % r, "pos", "dieB"] + PT, ["pVb"], ["pV"])
-            ac(DW[r][:, ub:ub + B], T.pV[:, 352:512], Re, ["pVb", "c_b"], ["dw%d0" % r], ["pV"], bias=c_b)
+            mms([(T.pV[:, 352 + i:512:16], sel(T.PT[:, i, :], 0), T.dieB[:, 0:10], True, True) for i in range(16)],
+                ["dieB"] + PT, ["pVb"], ["pV"])
+
+        def out():
+            ts(DW[r][:, ub:ub + B], T.pV[:, 352:512], DS, None, A.mult, None, ["pVb"], ["dw%d0" % r], ["pV"])
             send(DW[r][:, ub:ub + B], "md%d" % r, ["dw%d0" % r], "dwf%d" % r)
+        return st + [count, lambda: None,
+                     lambda: ts(T.keep[:, 0:10], cn, float(CAP), None, A.is_le, None, ["cn"], ["keep"], ["pA"]), rows0,
+                     lambda: tt(T.DA[:, 0:10], T.DA[:, 0:10], T.dieB[:, 0:10], A.add, ["DA0", "dieB"], ["DA0"]), out]
 
-        def scat():
-            op("v", lambda: v.tensor_copy(T.LW[:].indirect(T.SU[:, 0:10]), T.CT[:, 0:B]), ["SU", "CT0"], ["LW"])
-            mms([(T.pV[:, 200:203], sel(T.QS, i), T.LW[:, i:CAP:16], i == 0, i == 15) for i in range(16)],
-                ["QS", "LW"], ["lc"], ["pV"])
+    def before_gone(r):
+        for l in range(3):
+            ts(T.PN[:, l], T.NF[:, l], 0.25 * (2 - l), None, A.add, None, ["NF0", "NF1"], ["PN%d" % l])
+        tt(T.VA[:], T.VW[:], T.DA[:], A.subtract, ["VW", "DA0", "DA1", "DA2"], ["VA"])
+        for l in range(3):
+            ac(T.PA[:, l], T.VA[:], I, ["VA"], ["PA%d" % l], bias=(unit(r, l) * U - W0) / GF, scale=1 / GF)
 
-        def lists():
-            cp(T.LU[:, 0:3], T.pV[:, 200:203], ["lc"], ["LU"], ["pV"])
-            for b in range(4):
-                src = wblk(r, b, 0, B) if b < 3 else hown(r, 0, B)
-                ac(LA[r][:, rk, b * CAP:(b + 1) * CAP], src.indirect(T.LU[:, 0:3]), Cp,
-                   ["LU", "w%d_0" % r, "h%d" % r], ["la%d%d" % (r, b)])
-            send(LA[r][:, rk, :], "ma%d" % r, ["la%d%d" % (r, b) for b in range(4)], "laf%d" % r)
-        return st + [count, lambda: None, cap, rows0,
-                     lambda: ts(T.so1[:, 0:10], T.dieB[:, 0:10], -1000.0 / FL, 1000.0, A.mult, A.add, ["dieB"], ["so1"]),
-                     lambda: tt(T.so2[:, 0:10], T.so1[:, 0:10], T.pos[:, 0:10], A.add, ["so1", "pos"], ["so2"]),
-                     lambda: tt(T.so3[:, 0:10], T.so2[:, 0:10], T.c48[:, 0:10], A.min, ["so2", "c48"], ["so3"]),
-                     lambda: cp(T.SU[:, 0:10], T.so3[:, 0:10], ["so3"], ["SU"]), scat,
-                     lambda: tt(T.DA[:, 0:10], T.DA[:, 0:10], T.dieB[:, 0:10], A.add, ["DA0", "dieB"], ["DA0"]), lists]
+    def gs(h, l, a, b):
+        c0, c1, _ = HV[h]
+        o = 48 * c0 + 16 * (c1 - c0) * l - 16 * c0
+        return T.G[:, o + a:o + b]
 
-    def border_names():
-        ac(T.TB[:], pT[0][:], Cp, ["pT0"], ["TB"], ["pT0"])
-        ac(T.TC[:], T.TB[:, 0:B].indirect(T.LU[:, 0:3]), Cp, ["TB", "LU"], ["TC"])
-
-    def mark_names():
-        ts(T.tmp48[:], T.TC[:], c_y, 0.5, A.is_lt, A.mult, ["TC", "c_y"], ["tmp48"])
-        tt(T.TM[:], T.TC[:], T.tmp48[:], A.add, ["TC", "tmp48"], ["TM"])
-
-    def relay(r):
-        la = ["la%d%d" % (r, b) for b in range(4)] + ["laf%d" % r]
-        for b in range(4):
-            dst = wblk(r, b, V, X) if b < 3 else hwin(r, V, X)
-            cp(dst, LA[r][:, :, b * CAP:(b + 1) * CAP], la, ["wc%d%d" % (r, b) if b < 3 else "hc%d" % r])
+    def first_dead(h):
+        c0, c1, _ = HV[h]
+        o, k = pv[h][:, 0:3 * (c1 - c0)], str(h)
+        return [lambda: tt(T.AB[:, 1, :, c0:c1], o, T.PA[:, :, c0:c1], A.mult, ["val" + k, "PA0", "PA1", "PA2"], ["AB1" + k], [bv[h]]),
+                lambda: tt(T.AB[:, 0, :, c0:c1], o, T.PN[:, :, c0:c1], A.mult, ["val" + k, "PN0", "PN1", "PN2"], ["AB0" + k], [bv[h]]),
+                lambda: tt(T.m1[:, :, c0:c1], T.AB[:, :, 0, c0:c1], T.AB[:, :, 2, c0:c1], A.max, ["AB0" + k, "AB1" + k], ["m1" + k]),
+                lambda: tt(T.m[:, :, c0:c1], T.m1[:, :, c0:c1], T.AB[:, :, 1, c0:c1], A.max, ["m1" + k, "AB0" + k, "AB1" + k], ["m" + k]),
+                lambda: cp(T.WU[:, c0:c1], T.m[:, 1, c0:c1], ["m" + k], ["WU" + k]),
+                lambda: ts(T.oi[:, c0:c1], T.m[:, 0, c0:c1], 2047, None, A.bitwise_and, None, ["m" + k], ["oi" + k]),
+                lambda: cp(T.OU[:, c0:c1], T.oi[:, c0:c1], ["oi" + k], ["OU" + k])]
 
     def gone(r):
-        dwt = ["dw%d%d" % (r, k) for k in range(3)] + ["dwf%d" % r, "dwz%d" % r, "dwy%d" % r, "NU0", "NU1"]
-        for l in range(3):
-            ac(T.G[:, l * V:l * V + B], DW[r][:].indirect(T.NU[:, l, 0:10]), Cp, dwt, ["Gb%d" % l])
-        for l in range(3):
-            ac(T.Gc[:, l], T.G[:, l * V:l * V + B].indirect(T.LU[:, 0:3]), Cp, ["Gb%d" % l, "LU"], ["Gc%d" % l])
-        for l in range(2):
-            cp(T.G[:, l * V + B:(l + 1) * V], DW[r][:].indirect(T.NU[:, l, 10:56]), dwt, ["G%d" % l])
-            if l == 0:
-                mark_names()
-        table1(r, 0)
-        pc, pd = T.pA[:, 256:256 + CAP], T.pA[:, 304:304 + CAP]
-        mms([(o, a, b, j == 0, j == 3) for o, src in ((pd, T.TM), (pc, T.TC))
-             for j, (a, b) in enumerate([(T.ID[:], src[:])] + [(sel(T.FM, 3 + l), T.Gc[:, l]) for l in range(3)])],
-            ["ID", "FM", "TC", "TM", "Gc0", "Gc1", "Gc2"], ["pc"], ["pA"])
-        mine = twin(r, V + CAP * rk, V + CAP * (rk + 1))
-        ac(T.G[:, 2 * V + B:2 * V + 384], DW[r][:].indirect(T.NU[:, 2, 10:24]), Cp, dwt, ["G2a"])
-        ac(T.LS[:, r], pd, Cp, ["pc"], ["ls%d" % r], ["pA"])
-        send(mine, "mb%d" % r, ["ls%d" % r], "tf%d" % r, T.LS[:, r])
-        ac(T.G[:, 2 * V + 384:3 * V], DW[r][:].indirect(T.NU[:, 2, 24:56]), Cp, dwt + ["G2a"], ["G2"])
-        ac(mine, pc, Cp, ["pc"], ["tb%d" % r], ["pA"])
-        pv, bv = [T.pV, T.pN, T.pV], ["pV", "pN", "pV"]
-        for l in range(3):
-            o = pv[l][:, 56 * l:56 * (l + 1)]
-            lst = [(o, T.ID[:], T.PR[:, 56 * l:56 * (l + 1)], True, False)]
-            lst += [(o, sel(T.QS, i), T.G[:, l * V + i:(l + 1) * V:16], False, i == 15) for i in range(16)]
-            mms(lst, ["QS", "ID", "PR%d" % l, "G%d" % l, "Gb%d" % l], ["val%d" % l, bv[l]], [bv[l]])
-            if l == 0:
-                own_sums(r, (0,))
-                cp(T.VI[:, 0], o, ["val0"], ["VI0"], ["pV"])
-                relay(r)
-                ts(T.gm[:, 0], T.VI[:, 0], FL, 0.5, A.is_ge, A.mult, ["VI0"], ["gm0"])
-            if l == 1:
-                tt(T.m01[:], T.VI[:, 0], o, A.max, ["VI0", "val1"], ["m01"], ["pN"])
-                ts(T.gm[:, 1], o, FL, 0.5, A.is_ge, A.mult, ["val1", "pN"], ["gm1"], ["pN"])
-        tt(T.m[:], T.m01[:], o, A.max, ["val2", "m01"], ["m"], ["pV"])
-        ts(T.gm[:, 2], o, FL, 0.5, A.is_ge, A.mult, ["val2"], ["gm2"], ["pV"])
-        tt(T.a4[:], T.m[:], T.DA[:], A.subtract, ["m", "DA0", "DA1", "DA2"], ["a4"])
-        ts(T.a1[:], T.m[:], 13, None, A.arith_shift_right, None, ["m"], ["a1"])
-        ts(T.hx[:], T.a4[:], FL, float(X), A.is_ge, A.mult, ["a4"], ["hx"])
-        ts(T.oi[:], T.m[:], 8191, None, A.bitwise_and, None, ["m"], ["oi"])
-        tt(T.a3[:], T.a1[:], T.hx[:], A.mult, ["a1", "hx"], ["a3"])
-        cp(T.OU[:], T.oi[:], ["oi"], ["OU"])
-        tt(T.a4[:], T.a3[:], T.VW[:, 0], A.add, ["a3", "VW0"], ["a4"])
-        tt(T.HIs[:, :, 32:56], T.HP[:, :, 32:56], T.gm[:, :, 32:56], A.add, ["HP1", "gm0", "gm1", "gm2"], ["HIs1"])
-        cp(T.WU[:], T.a4[:], ["a4"], ["WU"])
-        mms([(pT[0][:], T.ID[:], T.TB[:], True, False)] +
-            [(pT[0][:], sel(T.FM, 3 + l), T.G[:, l * V:l * V + 512], False, l == 2) for l in range(3)],
-            ["FM", "ID", "TB", "G0", "G1", "G2", "Gb0", "Gb1", "Gb2"], ["pT0"], ["pT0"])
-        table1(r, 1)
+        dwt = ["dw%d%d" % (r, k) for k in range(3)] + ["dwf%d" % r, "dwz%d" % r, "NU0", "NU1"]
 
-    def pool_tokens(r):
-        return ["z%d" % r] + ["w%d_%d" % (r, k) for k in range(3)] + ["cw%d_%d" % (r, l) for l in range(3)] + \
-            ["wc%d%d" % (r, b) for b in range(3)]
+        def val(h):
+            c0, c1, _ = HV[h]
+            mms([(pv[h][:, 0:3 * (c1 - c0)], sel(T.QS, i), T.G[:, 48 * c0 + i:48 * c1:16], i == 0, i == 15) for i in range(16)],
+                ["QS"] + ["G%d%d" % (h, l) for l in range(3)] + ["Gb%d" % l for l in range(3 - 3 * h)], ["val%d" % h, bv[h]], [bv[h]])
+
+        def marks(h):
+            a, b = HS[h]
+            lst = [(pT[0][:], T.ID[:], T.TB[:], True, False)] if h == 0 else []
+            lst += [(pT[h][:, 0:b - a], sel(T.FM, 6 + l), gs(h, l, a, b), False, l == 2) for l in range(3)]
+            mms(lst, ["FM", "ID", "TB"] + ["G%d%d" % (h, l) for l in range(3)], ["pT%d" % h], ["pT%d" % h])
+        pb = T.pV[:, 176:176 + B]
+        mms([(pb, T.ID[:], T.TB[:, 0:B], True, False), (pb, T.S6[:], T.mk[:], False, False)], ["ID", "S6", "TB", "mk"], ["pc"], ["pV"])
+        for l in range(3):
+            ac(gs(0, l, 0, B), DW[r][:].indirect(T.NU[:, l, 0:10]), Cp, dwt, ["Gb%d" % l])
+            cp(gs(1, l, 512, V), DW[r][:].indirect(T.NU[:, l, 32:56]), dwt, ["G1%d" % l])
+        mms([(pb, sel(T.FM, 6 + l), gs(0, l, 0, B), False, l == 2) for l in range(3)], ["FM", "Gb0", "Gb1", "Gb2"], ["pc"], ["pV"])
+        ac(gs(0, 0, B, 512), DW[r][:].indirect(T.NU[:, 0, 10:32]), Cp, dwt, ["G00"])
+        ac(T.LS[:, r], pb, Cp, ["pc"], ["ls%d" % r], ["pV"])
+        send(TT[r][:, ub:ub + B], "mb%d" % r, ["ls%d" % r], "tf%d" % r, T.LS[:, r])
+        val(1)
+        cp(gs(0, 2, B, 512), DW[r][:].indirect(T.NU[:, 2, 10:32]), dwt, ["G02"])
+        ac(gs(0, 1, B, 512), DW[r][:].indirect(T.NU[:, 1, 10:32]), Cp, dwt, ["G01"])
+        val(0)
+        marks(1)
+        run(first_dead(1))
+        marks(0)
+        ac(T.gm[:, :, 32:56], pv[1][:, 0:72], Cp, ["val1"], ["gm1"], ["pN"])
+        ac(TT[r][:, 512:V], pT[1][:, 0:384], Cp, ["pT1"], ["TT1"], ["pT1"])
 
     def splice(r):
-        w = ["w%d_%d" % (r, k) for k in range(3)]
         od = T.OU[:]
         kp = ["kp0", "kp1"]
-        ac(T.ws[:, 0:448], BG[r][:, 0:HB].indirect(T.WU[:, 0:28]), Cp, pool_tokens(r) + ["WU"], ["ws0"])
-        cp(T.ws[:, 448:V], BG[r][:, 0:HB].indirect(T.WU[:, 28:56]), pool_tokens(r) + ["WU"], ["ws1"])
-        for l in range(3):
-            ac(T.nh[:, l], T.hx[:], Re, ["hx"], ["nh%d" % l], bias=1.0, scale=-1.0)
+        ou = ["OU0", "OU1"]
+        win = BG[:, W0:unit(r, 0) * U + V]
+        wt = ["zc0"] + [t for q in range(r + 1) for t in wall(q)]
         pb = T.pA[:, 352:512]
+
+        def wd2(h):
+            a, b = HS[h]
+            ac(T.wd2[:, a:b], wblk(r, 2, 0, X).indirect(T.OU[:, a // 16:b // 16]), Cp, wall(r) + ["OU%d" % h], ["wd2%d" % h])
+
+        def hd(h):
+            a, b = HS[h]
+            tt(T.tt[:, a:b], HW[r][:].indirect(T.OU[:, a // 16:b // 16]), T.ws[:, a:b], A.subtract,
+               hall(r) + ["OU%d" % h, "ws%d" % h], ["tt%d" % h])
+
+        def cand2(h):
+            a, b = HS[h]
+            mms([(pH[h][:, 0:b - a], T.ID[:], T.wd2[:, a:b], True, False), (pH[h][:, 0:b - a], T.NI[:], T.tt[:, a:b], False, True)],
+                ["ID", "NI", "wd2%d" % h, "tt%d" % h], ["pH%d" % h], ["pH%d" % h])
+            ac(T.wd2[:, a:b], pH[h][:, 0:b - a], Re, ["pH%d" % h], ["wd2%d" % h], ["pH%d" % h])
+
+        def sums(l):
+            mms([(T.pK[:, 3 + l:392:7], sel(T.QK, i), BG[:, (3 - l) * U + i:(3 - l) * U + V:16], False, False)
+                 for i in range(16)], ["QK", "cw%d" % l], kp, ["pK"])
+
+        def cand(l):
+            tt(cw(l), wblk(r, l, 0, X).indirect(od), T.tt[:], A.subtract, wall(r) + ou + ["tt0", "tt1"], ["cw%d" % l])
+        cp(T.ws[:, 512:V], win.indirect(T.WU[:, 32:56]), wt + ["WU1"], ["ws1"])
+        wd2(1)
+        f = first_dead(0)
+        run(f[:5])
+        ac(T.gm[:, :, 0:32], pv[0][:, 0:96], Cp, ["val0"], ["gm0"], ["pV"])
+        ac(T.ws[:, 0:512], win.indirect(T.WU[:, 0:32]), Cp, wt + ["WU0"], ["ws0"])
+        run(f[5:])
+        if r:
+            own_sums(r)
+        ts(T.nh[:], T.m[:, 1], 0.0, None, A.is_le, None, ["m0", "m1"], ["nh"])
+        hd(1)
         if r + 1 < RO:
             mms([(pb, T.ID[:], T.ws[:, 0:B], True, False), (pb, T.NI[:], hown(r, 0, B), False, True)],
                 ["ID", "NI", "ws0", "h%d" % r], ["pb"], ["pA"])
-        ac(twin(r, 0, 512), pT[0][:], Cp, ["pT0"], ["TT0"], ["pT0"])
-        ac(twin(r, 512, V), pT[1][:, 0:384], Cp, ["pT1"], ["TT1"], ["pT1"])
-        for h in range(2):
-            tt(T.tt[:, 448 * h:448 * (h + 1)], hwin(r, 0, X).indirect(T.OU[:, 28 * h:28 * (h + 1)]),
-               T.ws[:, 448 * h:448 * (h + 1)], A.subtract, ["hw%d" % r, "hc%d" % r, "OU", "ws%d" % h], ["tt%d" % h])
-        ac(T.Fg[:], twin(r).indirect(od), Cp, ["TT0", "TT1", "tb%d" % r, "tf%d" % r, "OU"], ["Fg"])
+        wd2(0)
+        hd(0)
         if r + 1 < RO:
             ts(T.hyb[:], pb, 0.0, 255.6, A.max, A.add, ["pb"], ["hyb"], ["pA"])
             mms([(pb, T.ID[:], hown(r, 0, B), True, False), (pb, T.HI[:], T.hyb[:], False, True)],
                 ["ID", "HI", "hyb", "h%d" % r], ["pb"], ["pA"])
-            ac(hwin(r + 1, ub, ub + B), pb, I, ["pb"], ["hb%d" % (r + 1)], ["pA"], bias=-128.0)
-            send(hwin(r + 1, ub, ub + B), "mh%d" % (r + 1), ["hb%d" % (r + 1)], "hf%d" % (r + 1))
-        tt(T.HIs[:, :, 0:32], T.HP[:, :, 0:32], T.gm[:, :, 0:32], A.add, ["HP0", "gm0", "gm1", "gm2"], ["HIs0"])
-        ac(T.wd2[:], wblk(r, 2, 0, X).indirect(od), Cp, w + ["wc%d2" % r, "OU"], ["wd2"])
-        own_sums(r, (1, 2))
-        mms([(T.pK[:, c:392:7], T.ID[:], T.nh[:, 0], False, False) for c in range(6)], ["ID", "nh0"], kp, ["pK"])
-        lst = [(T.pN[:, 0:400], T.ID[:], BG[r][:, 0:400], True, False)]
-        for c in range(6):
-            o = T.pN[:, c:392:7]
-            lst += [(o, T.NI[:], T.sl[:], False, False), (o, T.NI[:], T.sh[:], False, False)]
-            if c < 3:
-                lst += [(o, T.ID[:], T.LOs[:, c], False, False), (o, T.ID[:], T.HIs[:, c], False, False)]
-        mms(lst, ["ID", "NI", "sl", "sha", "shb", "LOs0", "LOs1", "HIs0", "HIs1", "z%d" % r], ["pN"], ["pN"])
-
-        def cw(l, a=0, b=V):
-            return BG[r][:, (3 - l) * X + a:(3 - l) * X + b]
-
-        def sums(l, last=False):
-            mms([(T.pK[:, 3 + l:392:7], sel(T.QK, i), BG[r][:, (3 - l) * X + i:(3 - l) * X + V:16], False, last and i == 15)
-                 for i in range(16)], ["QK", "cw%d_%d" % (r, l)], kp, ["pK"])
-        for l in range(2):
-            tt(cw(l), wblk(r, l, 0, X).indirect(od), T.tt[:], A.subtract, w + ["wc%d%d" % (r, l), "OU", "tt0", "tt1"], ["cw%d_%d" % (r, l)])
-            ts(cw(l), cw(l), 0.0, 255.0, A.max, A.min, ["cw%d_%d" % (r, l)], ["cw%d_%d" % (r, l)])
+            ac(HW[r + 1][:, ub:ub + B], pb, I, ["pb"], ["hb%d" % (r + 1)], ["pA"], bias=-128.0)
+            send(HW[r + 1][:, ub:ub + B], "mh%d" % (r + 1), ["hb%d" % (r + 1)], "hf%d" % (r + 1))
+        ac(TT[r][:, ub:ub + B], pT[0][:, 0:B], Cp, ["pT0"], ["tb%d" % r], ["pT0"])
+        ac(TT[r][:, B:512], pT[0][:, B:512], Cp, ["pT0"], ["TT0"], ["pT0"])
+        cand(0)
+        ac(T.Fg[:], TT[r][:].indirect(od), Cp, ["TT0", "TT1", "tb%d" % r, "tf%d" % r, "ttz%d" % r] + ou, ["Fg"])
+        mms([(T.pK[:, c:392:7], T.IB[:], a[:, c], False, False) for c in range(3) for a in (T.gm, T.EM)] +
+            [(T.pK[:, c:392:7], T.IB[:], T.nh[:], False, False) for c in range(6)], ["IB", "nh", "gm0", "gm1", "EM0", "EM1"], kp, ["pK"])
+        mms([(T.pN[:, 0:400], T.ID[:], BG[:, 0:400], True, False)] +
+            [(T.pN[:, c:392:7], T.ID[:], T.RF[:, c], False, False) for c in range(3)] +
+            [(T.pN[:, c:392:7], T.NI[:], T.SF[:, 0], False, False) for c in range(3, 6)],
+            ["ID", "NI", "RF0", "RF1", "z"] + SF, ["pN"], ["pN"])
+        cand2(1)
+        cand2(0)
+        ts(cw(0), cw(0), 0.0, 255.0, A.max, A.min, ["cw0"], ["cw0"])
+        cand(1)
+        sums(0)
         mms([(T.pN[:, 3 + l:392:7], sel(T.QF[:, l, :], i), T.Fg[:, i:V:16], False, l == 2 and i == 15)
              for l in range(3) for i in range(16)], ["QF0", "QF1", "QF2", "Fg"], ["pN"], ["pN"])
-        sums(0)
-        for h in range(2):
-            mms([(pH[h][:, 0:448], T.ID[:], T.wd2[:, 448 * h:448 * (h + 1)], True, False),
-                 (pH[h][:, 0:448], T.NI[:], T.tt[:, 448 * h:448 * (h + 1)], False, True)],
-                ["ID", "NI", "wd2", "tt%d" % h], ["pH%d" % h], ["pH%d" % h])
+        for t in range(3):
+            ac(T.NH[:, t], T.nh[:], I, ["nh"], ["NH%d" % t], scale=float(unit(r, t) * U16))
+        ts(cw(1), cw(1), 0.0, 255.0, A.max, A.min, ["cw1"], ["cw1"])
+        ts(cw(2), T.wd2[:], 255.0, None, A.min, None, ["wd20", "wd21"], ["cw2"])
         sums(1)
-        ac(T.P2[:], T.pN[:, 0:400], Re, ["pN"], ["P2"], ["pN"], bias=-64.0, scale=256.0)
-        ac(T.n7[:, 1:401], T.pN[:, 0:400], Cp, ["pN"], ["n7"], ["pN"])
-        ac(T.n7[:, 7:401:7], T.RST[:, 0:399:7], Cp, ["RST", "n7"], ["n7"])
         for l in range(3):
-            ac(T.vbp[:, 56 * l:56 * (l + 1)], T.hx[:], I, ["hx"], ["vbp%d" % l], bias=float((6 - l) * X), scale=-float(6 - l))
-        ts(cw(2, 0, 448), pH[0][:, 0:448], 0.0, 255.0, A.max, A.min, ["pH0"], ["cw%d_2" % r], ["pH0"])
-        ts(T.P1[:], T.pN[:, 0:400], 0.0, None, A.is_equal, None, ["pN"], ["P1"], ["pN"])
-        ts(cw(2, 448, V), pH[1][:, 0:448], 0.0, 255.0, A.max, A.min, ["pH1"], ["cw%d_2" % r], ["pH1"])
-        mms([(T.pK[:, 0:400], T.ID[:], a[:], False, False) for a in (T.P2, T.P1)], ["ID", "P1", "P2"], kp, ["pK"])
-        sums(2, True)
+            ts(T.P1[:, l], T.pN[:, 3 + l:392:7], 0.0, None, A.is_equal, None, ["pN"], ["P1%d" % l], ["pN"])
+        for l in range(3):
+            ac(T.P2[:, l], T.pN[:, 3 + l:392:7], Re, ["pN"], ["P2%d" % l], ["pN"], bias=-64.0, scale=256.0)
+        ac(T.n7[:, 1:401], T.pN[:, 0:400], Cp, ["pN"], ["n7"], ["pN"])
+        ac(T.n7[:, 7:401:7], T.RST[:, 1:400:7], I, ["RST", "n7"], ["n7"], bias=4.0)
+        for t in range(3):
+            tt(T.ON[:, t], T.RF[:, t], T.nh[:], A.mult, ["RF0", "RF1", "nh"], ["ON%d" % t])
+        sums(2)
+        mms([(T.pK[:, 3 + l:392:7], T.IB[:], a[:, l], False, k == 1 and l == 2) for k, a in enumerate((T.P1, T.P2)) for l in range(3)],
+            ["IB", "P10", "P11", "P12", "P20", "P21", "P22"], kp, ["pK"])
         tt(T.dn[:], T.n7[:, 0:400], T.pN[:, 0:400], A.subtract, ["n7", "pN"], ["dn"], ["pN"])
-        tt(T.ON[:], T.RF[:], T.nh[:], A.mult, ["RF0", "RF1", "nh0", "nh1", "nh2"], ["ON"])
-        tt(T.vb[:], T.vbp[:], T.VW[:], A.add, ["vbp0", "vbp1", "vbp2", "VW0", "VW1", "VW2"], ["vb"])
-        ac(T.k0[:, 0:224], T.pK[:, 0:224], Cp, kp, ["k00"], ["pK"])
-        ac(T.k0[:, 224:400], T.pK[:, 224:400], Cp, kp, ["k01"], ["pK"])
 
     def heights(r):
-        for h in range(2):
-            mms([(pH[h][:, 0:448], T.ID[:], T.ws[:, 448 * h:448 * (h + 1)], True, False),
-                 (pH[h][:, 0:448], T.NI[:], hown(r, 448 * h, 448 * (h + 1)), False, True)],
+        for h, (a, b) in enumerate(HS):
+            mms([(pH[h][:, 0:b - a], T.ID[:], T.ws[:, a:b], True, False), (pH[h][:, 0:b - a], T.NI[:], hown(r, a, b), False, True)],
                 ["ID", "NI", "ws%d" % h, "h%d" % r], ["pH%d" % h], ["pH%d" % h])
-            ac(T.hr[:, 448 * h:448 * (h + 1)], pH[h][:, 0:448], Re, ["pH%d" % h], ["hr%d" % h], ["pH%d" % h])
-        for h in range(2):
-            ac(T.hy[:, 448 * h:448 * (h + 1)], T.hr[:, 448 * h:448 * (h + 1)], I, ["hr%d" % h], ["hy%d" % h], bias=255.6)
-            mms([(pH[h][:, 0:448], T.ID[:], hown(r, 448 * h, 448 * (h + 1)), True, False),
-                 (pH[h][:, 0:448], T.HI[:], T.hy[:, 448 * h:448 * (h + 1)], False, True)],
+            ac(T.hr[:, a:b], pH[h][:, 0:b - a], Re, ["pH%d" % h], ["hr%d" % h], ["pH%d" % h])
+        for h, (a, b) in enumerate(HS):
+            ac(T.hy[:, a:b], T.hr[:, a:b], I, ["hr%d" % h], ["hy%d" % h], bias=255.6)
+            mms([(pH[h][:, 0:b - a], T.ID[:], hown(r, a, b), True, False), (pH[h][:, 0:b - a], T.HI[:], T.hy[:, a:b], False, True)],
                 ["ID", "HI", "hy%d" % h, "h%d" % r], ["pH%d" % h], ["pH%d" % h])
-        for h in range(2):
-            ac(hown(r + 1, 448 * h, 448 * (h + 1)), pH[h][:, 0:448], I, ["pH%d" % h], ["h%d" % (r + 1)], ["pH%d" % h], bias=-128.0)
+        for h, (a, b) in enumerate(HS):
+            ac(hown(r + 1, a, b), pH[h][:, 0:b - a], I, ["pH%d" % h], ["h%d" % (r + 1)], ["pH%d" % h], bias=-128.0)
         if r + 1 < RO:
-            ac(hwin(r + 1), hown(r + 1), Cp, ["h%d" % (r + 1)], ["hw%d" % (r + 1)])
+            ac(HW[r + 1][:, 0:V], hown(r + 1), Cp, ["h%d" % (r + 1)], ["hw%d" % (r + 1)])
         else:
             dma("y", "dout", [(T.yh[:], hown(RO))], ["h%d" % RO], [])
 
@@ -573,19 +606,19 @@ def rank_program(g, core, T, topo):
         b = a + n
         bl = T.BL[:, 0:n // 16]
         h = k[0]
-        kp = "kq" + k
+        kq = "kq" + k
         st = []
         for t in range(3):
             st.append(lambda t=t: scan(T.RB[:, t, a:b], T.RST[:, a:b], T.pK[:, a:b], 0.0, A.add, A.min,
-                                       ["RST", kp, "kp" + h], ["RB%d%s" % (t, k)], ["pK"]))
-            st.append(lambda t=t: tt(T.nq[:, a:b], T.RB[:, t, a:b + pad].indirect(bl), T.k0[:, a:b], A.not_equal,
-                                     ["RB%d%s" % (t, k), "k0" + h, "BL"], ["nq" + k]))
-            st.append(lambda t=t: scan(T.QB[:, t, a:b], T.dn[:, a:b], T.nq[:, a:b], 4.0, A.add, A.min,
+                                       ["RST", kq, "kp" + h], ["RB%d%s" % (t, k)], ["pK"]))
+            st.append(lambda t=t: tt(T.nq[:, a:b], T.RB[:, t, a:b], T.pK[:, a:b], A.not_equal,
+                                     ["RB%d%s" % (t, k), kq, "kp" + h], ["nq" + k], ["pK"]))
+            st.append(lambda t=t: scan(T.QB[:, t, a:b], T.dn[:, a:b], T.nq[:, a:b], 0.0, A.add, A.mult,
                                        ["dn", "nq" + k], ["QB%d%s" % (t, k)]))
             if t < 2:
-                st.append(lambda t=t: tt(T.pen[:, a:b], T.QB[:, t, a:b + pad].indirect(bl), T.n7[:, 1 + a:1 + b], A.is_equal,
+                st.append(lambda t=t: tt(T.kp[:, a:b], T.QB[:, t, a:b + pad].indirect(bl), T.n7[:, 1 + a:1 + b], A.not_equal,
                                          ["QB%d%s" % (t, k), "n7", "BL"], ["pen" + k]))
-                st.append(lambda: tt(T.pK[:, a:b], T.pK[:, a:b], T.pen[:, a:b], A.add, [kp, "kp" + h, "pen" + k], [kp], ["pK"]))
+                st.append(lambda: tt(T.pK[:, a:b], T.pK[:, a:b], T.kp[:, a:b], A.mult, [kq, "kp" + h, "pen" + k], [kq], ["pK"]))
         return st
 
     def both(x, y):
@@ -603,47 +636,52 @@ def rank_program(g, core, T, topo):
             st, ks = extract(a, n, "1", 8), ["1"]
         rb = ["RB%d%s" % (t, x) for t in range(3) for x in ks]
         qb = ["QB%d%s" % (t, x) for t in range(3) for x in ks]
-        ki = lambda: ts(T.Ki[:, :, c0:c1], T.RB[:, :, a + 6:7 * c1:7], -FL, None, A.mult, None, rb, ["Ki" + k])
-        xi = lambda: ts(T.xi[:, :, c0:c1], T.Ki[:, :, c0:c1], 7, None, A.bitwise_and, None, ["Ki" + k], ["xi" + k])
+        ki = lambda: tt(T.Ki[:, :, c0:c1], T.NH[:, :, c0:c1], T.RB[:, :, a + 6:7 * c1:7], A.subtract, rb + ["NH0", "NH1", "NH2"], ["Ki" + k])
+        xi = lambda: ts(T.xi[:, :, c0:c1], T.Ki[:, :, c0:c1], 2047, None, A.bitwise_and, None, ["Ki" + k], ["xi" + k])
         st = st[:-1] + [lambda f=st[-1]: (ki(), f(), xi())]
-        st += [
-            lambda: tt(T.RF[:, :, c0:c1], T.QB[:, :, a + 6:7 * c1:7], T.ON[:, :, c0:c1], A.add, qb + ["ON"], ["RF" + k]),
-            lambda: ts(T.xf[:, :, c0:c1], T.xi[:, :, c0:c1], float(X), None, A.mult, None, ["xi" + k], ["xf" + k]),
-            lambda: tt(T.NF3[:, :, c0:c1], T.RF[:, :, c0:c1], T.SF[:, :, c0:c1], A.add, ["RF" + k] + SF, ["NF" + k]),
-            lambda: tt(T.ef[:, :, c0:c1], T.xf[:, :, c0:c1], T.vb[:, :, c0:c1], A.add, ["xf" + k, "vb"], ["ef" + k]),
-            lambda: cp(T.EU[:, :, c0:c1], T.ef[:, :, c0:c1], ["ef" + k], ["EU" + k]),
-        ]
-        if r + 1 < RO:
-            st.insert(-1, lambda: ts(T.NU[:, :, c0:c1], T.NF3[:, :, c0:c1], 1 / SC, None, A.mult, None, ["NF" + k], ["NU" + k]))
-            st.append(lambda: ts(T.EM[:, :, c0:c1], T.RF[:, :, c0:c1], 0.0, 16.0, A.is_equal, A.mult, ["RF" + k], ["EM" + k]))
-        return st
+        rf = lambda: tt(T.RF[:, :, c0:c1], T.QB[:, :, a + 6:7 * c1:7], T.ON[:, :, c0:c1], A.add, qb + ["ON0", "ON1", "ON2"], ["RF" + k])
+        nf = lambda: tt(T.NF[:, :, c0:c1], T.RF[:, :, c0:c1], T.SF[:, :, c0:c1], A.add, ["RF" + k] + SF, ["NF" + k])
+        eu = lambda: ts(T.EU[:, :, c0:c1], T.xi[:, :, c0:c1], 16.0, pm, A.mult, A.add, ["xi" + k, "PF"], ["EU" + k])
+        if r + 1 == RO:
+            return st + [eu, rf, nf]
+        nu = lambda: ts(T.NU[:, :, c0:c1], T.NF[:, :, c0:c1], 1 / SC, None, A.mult, None, ["NF" + k], ["NU" + k])
+        em = lambda: ts(T.EM[:, :, c0:c1], T.RF[:, :, c0:c1], 0.0, 16.0, A.is_equal, A.mult, ["RF" + k], ["EM" + k])
+        if h:
+            return st + [rf, eu, nf, em, nu]
+        eb = lambda: ts(T.EB[:], T.xi[:, :, 0:10], 16.0, pm, A.mult, A.add, ["xi0", "PF"], ["EB"])
+        return st + [rf, eb, nf, em, nu, eu]
+
+    def pool(r):
+        return BG[:, 0:unit(r, 0) * U + V], ["z", "zc0", "zc1", "zc2", "cw0", "cw1", "cw2"] + [t for q in range(r + 1) for t in wall(q)]
+
+    def border_weights(r):
+        win, R = pool(r)
+        ac(SB[r + 1][:], win.indirect(T.EB[:]), Cp, R + ["EB"], ["sb%d" % (r + 1)])
+        hand_over(r + 1)
+
+    def place_border(r):
+        dma("y", "dc%d" % r, [(wblk(r, l, o, o + B), SB[r][:, l * B:(l + 1) * B]) for l in range(3) for o in (0, ub)],
+            ["sb%d" % r, "die1"], ["wb%d" % r, "w%d_3" % r])
 
     def new_weights(r, h, eng="sss", which=(0, 1, 2)):
         c0, c1, _ = HV[h]
+        if h == 0 and r + 1 < RO:
+            c0 = 10
+        win, R = pool(r)
         for t in which:
-            src = BG[r][:, 0:HB].indirect(T.EU[:, t, c0:c1])
-            R = pool_tokens(r) + ["EU%d" % h]
+            src = win.indirect(T.EU[:, t, c0:c1])
             if r + 1 < RO:
                 o, tok = wblk(r + 1, t, 16 * c0, 16 * c1), "w%d_%d" % (r + 1, h if eng[t] == "s" else 2)
             else:
-                o, tok = T.WF[:, t * V + 16 * c0:t * V + 16 * c1], "wf%d%d" % (t, h)
+                o, tok = T.WF[:, t * V + 16 * c0:t * V + 16 * c1], "yw%d%d" % (t, h)
             if eng[t] == "s":
-                ac(o, src, Cp, R, [tok])
+                ac(o, src, Cp, R + ["EU%d" % h], [tok])
             else:
-                cp(o, src, R, [tok])
+                cp(o, src, R + ["EU%d" % h], [tok])
             if r + 1 == RO:
                 dma("y", "dout", [(T.yw[:, t * V + 16 * c0:t * V + 16 * c1], o)], [tok], [])
 
-    def run(*lists):
-        for k in range(max(len(x) for x in lists)):
-            for x in lists:
-                if k < len(x):
-                    x[k]()
-
     nop = [lambda: None]
-
-    def tb(r, a, b):
-        return lambda: table(r, a, b)
 
     votes(0, 0)
     vs = votes_scalar(0)
@@ -655,42 +693,46 @@ def rank_program(g, core, T, topo):
     for r in range(RO):
         d1, d2 = deaths_steps(r, 1), deaths_steps(r, 2)
         if r == 0:
-            votes(r, 2, [db[7:12], db[12:14], d1])
-            late_consts()
-            border_names()
+            votes(r, 2, [db[7:], d1[:4], d1[4:]])
         else:
-            votes(r, 2, [db[13:] + [lambda: split_names(1), lambda: new_weights(r - 1, 1, which=(0, 1))], [], []])
-            run(d1[:3], [lambda: low_names(1)])
-            table(r, 13, 16)
-            run(d1[3:])
-            border_names()
+            votes(r, 2, [[lambda: new_weights(r - 1, 0), lambda: table(0, 8, 13)], d1[:4], d1[4:]])
+            place_border(r)
+            table(0, 13, 16)
+            new_weights(r - 1, 1, which=(0,))
+            high_names(1)
         run(d2[:4])
         if r:
+            keep_table()
+            table(1, 0, 16)
             new_weights(r - 1, 1, "vvv", which=(2,))
         d2[4]()
+        before_gone(r)
+        if r:
+            mark_inner()
+            new_weights(r - 1, 1, which=(1,))
         gone(r)
         splice(r)
         heights(r)
         run(choose_steps(r, 0))
         if r + 1 < RO:
-            split_names(0)
-            new_weights(r, 0)
+            border_weights(r)
             votes(r + 1, 0)
             db = deaths_steps(r + 1, 0)
-            vs = votes_scalar(r + 1, tb(r + 1, 9, 13))
+            vs = votes_scalar(r + 1)
             run(choose_steps(r, 1),
-                [lambda: (low_names(0), table(r + 1, 0, 4), vs[0]()), nop[0]] + db[:4] + [tb(r + 1, 4, 6), db[5]] + db[6:13],
-                nop * 8 + [vs[1], tb(r + 1, 6, 9)] + nop * 3 + [vs[2]])
+                [vs[0], lambda: (high_names(0), table(0, 0, 3))] + db[:4] + [lambda: table(0, 3, 5), db[5], db[6], db[7], db[8]],
+                nop * 6 + [vs[1]] + nop * 3 + [vs[2], lambda: table(0, 5, 8)])
         else:
             new_weights(r, 0)
             run(choose_steps(r, 1))
             new_weights(r, 1, "svv")
-            ac(T.q128[:], T.NF3[:], I, ["NF0", "NF1"], ["q128"], bias=192.0 - (UB + 79.5) / B, scale=1 / (SC * B))
+            ts(T.NA[:], T.NF[:], 1 / SC, None, A.mult, None, ["NF0", "NF1"], ["NA"])
+            ac(T.q128[:], T.NA[:], I, ["NA"], ["q128"], bias=192.0 - (UB + 79.5) / B, scale=1.0 / B)
             ac(T.fa[:], T.q128[:], I, ["q128"], ["fa"], bias=-192.0 * 864 - UB - 1024.0 * rk, scale=864.0)
-            ts(T.fb[:], T.NF3[:], UB * SC, None, A.is_ge, None, ["NF0", "NF1"], ["fb"])
-            ts(T.h32[:], T.NF3[:], 1 / SC, 1024.0 * rk, A.mult, A.add, ["NF0", "NF1"], ["h320", "h321"])
+            ts(T.fb[:], T.NA[:], float(UB), None, A.is_ge, None, ["NA"], ["fb"])
+            ts(T.NA[:], T.NA[:], 1024.0 * rk, None, A.add, None, ["NA", "q128"], ["NA"])
             tt(T.fa[:], T.fa[:], T.fb[:], A.mult, ["fa", "fb"], ["fa"])
-            tt(T.YN[:], T.fa[:], T.h32[:], A.add, ["fa", "h320"], ["YN"])
+            tt(T.YN[:], T.fa[:], T.NA[:], A.add, ["fa", "NA"], ["YN"])
             dma("y", "dout", [(T.yn[:], T.YN[:])], ["YN"], [])
     for k, n in cnt.items():
         g.wait_ge(T.sem[k], n)

@@ -9,12 +9,17 @@ U16 = U // 16
 W0 = 4 * U - 16
 FL = 32768.0
 GF = 8192.0
-DS = GF / FL
 SC = 2.0 ** -13
 BIG = 2.0 ** 23
 CH = [(0, 10), (10, 32), (32, 56)]
-HV = [(0, 32, 224), (32, 56, 176)]
+PS = [(0, 256), (256, V)]
+CUT = [[(0, 256)], [(256, 512), (512, V)]]
+WIDE = [112, 400]
+EX = [(0, 16, 112), (16, 32, 112), (32, 56, 176)]
 HS = [(0, 512), (512, V)]
+GE, WE, LE = ("svv", "vsv"), "vv", ("sss", "svs", "vsv")
+CY, WAKE, FLIGHT = 0.83e-3, 0.2, 6.5
+PLAN = []
 
 bf, f2, f4, i4, u2 = "bfloat16", "float16", "float32", "int32", "uint16"
 
@@ -26,24 +31,25 @@ def _s(n, d):
 SCRATCH = {
     "BG": _s([(4 + 6 * RO) * U], bf),
     "nbi": _s([168], i4), "ia": _s([168], i4), "ib": _s([168], i4), "fa": _s([168], f4), "fb": _s([168], f4),
-    "NU": _s([3, 56], u2), "RF": _s([3, 56], f2), "NF": _s([3, 56], f2), "ON": _s([3, 56], f2), "EM": _s([3, 56], bf),
-    "PN": _s([3, 56], f4), "VA": _s([56], f4), "PA": _s([3, 56], f4), "AB": _s([2, 3, 56], f4), "m1": _s([2, 56], f4),
-    "m": _s([2, 56], i4), "oi": _s([56], i4), "OU": _s([56], u2), "WU": _s([56], u2), "nh": _s([56], bf),
-    "NH": _s([3, 56], f4), "gm": _s([3, 56], bf), "DA": _s([56], bf), "cmp": _s([2688], bf), "gI": _s([1056], bf),
-    "ok": _s([176], bf), "d01": _s([56], bf), "die": _s([56], bf), "dieB": _s([16], bf), "cs": _s([16], bf),
-    "keep": _s([16], bf), "G": _s([2688], bf), "TB": _s([512], bf), "H8": _s([3, 56], bf), "mk": _s([B], bf), "LS": _s([RO, B], bf),
-    "ws": _s([V], bf), "tt": _s([V], bf), "wd2": _s([V], bf), "Fg": _s([V], bf), "hr": _s([V], bf), "hy": _s([V], bf),
-    "hyb": _s([B], bf), "P1": _s([3, 56], bf), "P2": _s([3, 56], bf), "n7": _s([408], f4), "dn": _s([400], f4),
-    "RB": _s([3, 400], f4), "QB": _s([3, 408], f4), "nq": _s([400], bf), "kp": _s([400], bf),
-    "Ki": _s([3, 56], i4), "xi": _s([3, 56], i4), "EU": _s([3, 56], u2), "EB": _s([30], u2),
-    "WF": _s([2688], bf), "HO": _s([4 * V], bf), "NA": _s([168], f4), "YN": _s([168], f4), "q128": _s([168], bf),
+    "NU": _s([3, 56], u2), "RF": _s([3, 56], f2), "NF": _s([3, 56], f2), "ON": _s([3, 56], f2), "OS": _s([3, 56], f2),
+    "EM": _s([3, 56], bf), "PN": _s([3, 56], f4), "VA": _s([56], f4), "PA": _s([3, 56], f4), "AB": _s([2, 3, 56], f4),
+    "m1": _s([2, 56], f4), "m": _s([2, 56], i4), "oi": _s([56], i4), "OU": _s([56], u2), "WU": _s([56], u2),
+    "nh": _s([3, 56], bf), "NH": _s([3, 56], f4), "gm": _s([3, 56], bf), "DA": _s([56], bf), "cmp": _s([2688], bf),
+    "gI": _s([1056], bf), "ok": _s([176], bf), "d01": _s([56], bf), "die": _s([56], bf), "dieB": _s([16], bf),
+    "cs": _s([16], bf), "G": _s([2688], bf), "TB": _s([512], bf), "H8": _s([3, 56], bf), "mk": _s([B], bf),
+    "LS": _s([RO, B], bf), "ws": _s([V], bf), "tt": _s([V], bf), "wd2": _s([V], bf), "wr2": _s([V], bf),
+    "Fg": _s([V], bf), "hr": _s([V], bf), "hy": _s([V], bf), "hyb": _s([B], bf), "P1": _s([400], bf), "P2": _s([400], bf),
+    "n7": _s([408], f4), "dn": _s([400], f4), "RB": _s([3, 400], f4), "QB": _s([3, 408], f4), "nq": _s([400], bf),
+    "kp": _s([400], bf), "Ki": _s([3, 56], i4), "xi": _s([3, 56], i4), "EU": _s([3, 56], u2), "KS": _s([3, 56], f4),
+    "KP": _s([3, 56], f4), "E": _s([128, 16], bf), "E2": _s([2, 384], f4), "WF": _s([2688], bf), "HO": _s([V], bf),
+    "NA": _s([168], f4), "NB": _s([168], f4), "YN": _s([168], f4), "q128": _s([168], bf),
     "PI": _s([2], i4), "PF": _s([16], f4), "J": _s([144], f4), "JG": _s([128], f4), "QS": _s([144], bf),
-    "Q3": _s([144], bf), "Q2": _s([144], bf), "QK": _s([144], bf), "QH": _s([144], bf), "FM": _s([144], bf),
-    "QF": _s([3, 144], bf), "PT": _s([16, 144], bf), "PB": _s([16, 144], bf), "OH": _s([16], f4), "O3": _s([6], f4),
-    "ID": _s([128], bf), "NI": _s([128], bf), "HI": _s([128], bf), "IB": _s([128], bf), "IU": _s([128], bf),
-    "S6": _s([128], bf), "CZ": _s([512], bf), "ONE": _s([128], bf), "TRI": _s([128], bf), "tri0": _s([128], bf),
-    "c16": _s([56], f4), "VW": _s([56], f4), "SF": _s([3, 56], f2), "T7": _s([406], bf), "POS": _s([400], bf),
-    "RST": _s([400], f4), "BL": _s([14], u2), "bli": _s([14], i4), "o16": _s([16], bf), "k6": _s([2, 56], bf),
+    "QK": _s([144], bf), "QH": _s([144], bf), "FM": _s([144], bf), "QF": _s([24], bf), "PT": _s([16, 144], bf),
+    "OH": _s([16], f4), "O3": _s([6], f4), "ID": _s([128], bf), "NI": _s([128], bf), "HI": _s([128], bf),
+    "IB": _s([128], bf), "N4": _s([128], f4), "I4": _s([40], f4), "S6": _s([128], bf), "I8": _s([128], bf),
+    "N8": _s([128], bf), "ONE": _s([128], bf), "TRI": _s([128], bf), "tri0": _s([128], bf), "tri1": _s([128], bf),
+    "c16": _s([56], f4), "VW": _s([56], f4), "SF": _s([3, 56], f2), "T7": _s([406], bf), "S7": _s([400], f2),
+    "RST": _s([400], f4), "BL": _s([14], u2), "bli": _s([14], i4), "o16": _s([16], bf), "m56": _s([56], bf),
     "pA": ("psum", [128, 512], f4), "pV": ("psum", [128, 512], f4), "pN": ("psum", [128, 512], f4),
     "pK": ("psum", [128, 512], f4), "pT0": ("psum", [128, 512], f4), "pT1": ("psum", [128, 512], f4),
     "pH0": ("psum", [128, 512], f4), "pH1": ("psum", [128, 512], f4),
@@ -52,10 +58,10 @@ for _r in range(RO):
     SCRATCH["HW%d" % _r] = _s([X], bf)
     SCRATCH["DW%d" % _r] = _s([X], bf)
     SCRATCH["TT%d" % _r] = _s([X], bf)
-    SCRATCH["SB%d" % _r] = _s([3 * B], bf)
+    SCRATCH["SB%d" % _r] = _s([B], bf)
 
 SEMAPHORES = ["cv", "cs", "ct", "cg", "snt", "dnb", "dhb", "dh", "dw", "dsb", "dout"] + \
-    ["%s%d" % (k, r) for k in ("mh", "md", "mb", "mw", "ho", "dc") for r in range(RO)]
+    ["%s%d" % (k, r) for k in ("mh", "md", "mb", "mw", "ho") for r in range(RO)]
 
 
 def unit(r, l):
@@ -69,7 +75,8 @@ def peers_of(core, T, turn=0):
 
 
 def carriers(core, peers, topo):
-    return [c for c in topo.cores_of(core) if topo.die(c) != topo.die(core) and all(topo.may_write(c, p) for p in peers)][:2]
+    ok = [c for c in topo.cores_of(core) if c != core and all(topo.may_write(c, p) for p in peers)]
+    return sorted(ok, key=lambda c: topo.die(c) == topo.die(core))[:3]
 
 
 def common_mask(core, dsts, topo):
@@ -92,10 +99,10 @@ def carrier_program(g, core, owner, k, T, topo):
     mask, ne = common_mask(core, peers, topo)
     ub = UB + B * T.rank_of(owner)
     for r in range(RO):
-        g.wait_ge(T.sem["ho%d" % r], len(spare(owner, core, peers, topo)) // 2)
+        g.wait_ge(T.sem["ho%d" % r], len(spare(owner, core, peers, topo)) // 2 if k < 2 else ne)
         o = unit(r, k) * U + ub
         g.remote_dma_fused([RemoteDMATransfer(dst_ids=ids_of(core, peers, topo), dma_engine_mask=mask, remote_sem=T.sem["mw%d" % r],
-                                              src=T["SB%d" % r][:, k * B:(k + 1) * B], dsts=[T.BG[:, o:o + B]] * len(peers))],
+                                              src=T["SB%d" % r][:], dsts=[T.BG[:, o:o + B]] * len(peers))],
                            local_sem=T.sem.snt)
     g.wait_ge(T.sem.snt, RO * ne)
 
@@ -109,55 +116,118 @@ def rank_program(g, core, T, topo):
                 carrier_program(g, core, owner, cs.index(core), T, topo)
         return
     Q = {"v": g.vector, "s": g.scalar, "t": g.tensor, "g": g, "y": g.sync}
-    cnt = {"cv": 0, "cs": 0, "ct": 0, "cg": 0}
-    waited = {e: {} for e in Q}
-    wr, rd, bank = {}, {}, {}
+    calls, wr, rd, bank, gathers = [], {}, {}, {}, []
 
-    def need(e, R, W, Bk):
-        deps = {}
-        ps = [wr[t] for t in R if t in wr] + [wr[t] for t in W if t in wr]
+    def call(e, fn, hold, R, W, Bk=(), late=WAKE, sem=None):
+        k = len(calls)
+        dep = {wr[t] for t in list(R) + list(W) if t in wr}
         for t in W:
-            ps += list(rd.get(t, {}).items())
+            dep.update(rd.get(t, ()))
         for b in Bk:
-            ps += [p for p in bank.get(b, {}).items() if p[0] != "c" + e]
-        for s, n in ps:
-            if not (e == "t" and s == "ct"):
-                deps[s] = max(deps.get(s, 0), n)
-        for s, n in deps.items():
-            if waited[e].get(s, 0) < n:
-                Q[e].wait_ge(T.sem[s], n)
-                waited[e][s] = n
-
-    def note(p, R, W, Bk):
+            who, now, before = bank.get(b, (e, [], []))
+            if who != e:
+                now, before = [], now
+            dep.update(before + (now[-1:] if e == "t" else []))
+            bank[b] = (e, now + [k], before)
         for t in R:
-            rd.setdefault(t, {})[p[0]] = p[1]
+            rd.setdefault(t, []).append(k)
         for t in W:
-            wr[t] = p
-            rd[t] = {}
-        for b in Bk:
-            bank.setdefault(b, {})[p[0]] = p[1]
+            wr[t], rd[t] = k, []
+        calls.append({"e": e, "fn": fn, "hold": hold, "late": late, "dep": dep, "sem": sem})
+        return k
 
-    def op(e, fn, R, W, Bk=()):
-        need(e, R, W, Bk)
-        s = "c" + e
-        fn().then_inc(T.sem[s], 1)
-        cnt[s] += 1
-        note((s, cnt[s]), R, W, Bk)
+    def issue():
+        n = len(calls)
+        before = [sorted(c["dep"]) for c in calls]
+        after = [[] for _ in calls]
+        for k in range(n):
+            for d in before[k]:
+                after[d].append(k)
+
+        def gap(d, k):
+            return 0.0 if calls[d]["e"] == calls[k]["e"] == "t" else calls[d]["late"]
+
+        def place(order, links, back):
+            end, busy = [0.0] * n, {e: [] for e in "vstgyx"}
+            for k in order:
+                t = max([calls[k]["late"] if back else 0.0] + [end[d] + (gap(k, d) if back else gap(d, k)) for d in links[k]])
+                h, line = calls[k]["hold"], busy[calls[k]["e"]]
+                i = len(line)
+                while i and line[i - 1][1] > t:
+                    i -= 1
+                while i < len(line) and line[i][0] < t + h:
+                    t = max(t, line[i][1])
+                    i += 1
+                line.insert(i, (t, t + h))
+                end[k] = t + h
+            return end
+        if not PLAN:
+            way = [0.0] * n
+            for k in range(n - 1, -1, -1):
+                way[k] = calls[k]["hold"] + max([calls[k]["late"]] + [way[j] + gap(k, j) for j in after[k]])
+            best = None
+            for _ in range(3):
+                end = place(sorted(range(n), key=lambda k: (-way[k], k)), before, False)
+                span = max(end[k] + calls[k]["late"] for k in range(n))
+                if best is None or span < best[0]:
+                    best = (span, end)
+                way = place(sorted(range(n), key=lambda k: (-end[k], -k)), after, True)
+            PLAN.extend(sorted(range(n), key=lambda k: (best[1][k] - calls[k]["hold"], k)))
+        cnt, waited = {}, {e: {} for e in Q}
+        for k in PLAN:
+            c = calls[k]
+            e = c["e"]
+            if e == "x":
+                c["done"] = c["sem"]
+                cnt[c["sem"][0]] = c["sem"][1]
+                continue
+            need = {}
+            for d in before[k]:
+                s, m = calls[d]["done"]
+                if not (e == "t" and s == "ct"):
+                    need[s] = max(need.get(s, 0), m)
+            for s, m in need.items():
+                if waited[e].get(s, 0) < m:
+                    Q[e].wait_ge(T.sem[s], m)
+                    waited[e][s] = m
+            s, m = c["sem"] or ("c" + e, 1)
+            c["fn"](s)
+            cnt[s] = cnt.get(s, 0) + m
+            c["done"] = (s, cnt[s])
+        for s, m in cnt.items():
+            g.wait_ge(T.sem[s], m)
+
+    def size(o):
+        n = 1
+        for d in o.shape[1:]:
+            n *= d
+        return n
+
+    def ind(win, off):
+        gathers.append(win.indirect(off))
+        return gathers[-1]
+
+    def op(e, fn, o, i, per, R, W, Bk=()):
+        if any(i is x for x in gathers):
+            hold = 70 + 1.56 * size(o)
+        else:
+            if per == 1 and e == "v" and "16" in str(o.dtype) and "16" in str(i.dtype):
+                per = 0.5
+            hold = max(64, per * size(o))
+        call(e, lambda s: fn().then_inc(T.sem[s], 1), CY * hold, R, W, Bk)
 
     def mms(lst, R, W, Bk):
-        need("t", R, W, Bk)
-        for a in lst[:-1]:
-            g.tensor.matmul(*a)
-        g.tensor.matmul(*lst[-1]).then_inc(T.sem.ct, 1)
-        cnt["ct"] += 1
-        note(("ct", cnt["ct"]), R, W, Bk)
+        def fn(s):
+            for a in lst[:-1]:
+                g.tensor.matmul(*a)
+            g.tensor.matmul(*lst[-1]).then_inc(T.sem[s], 1)
+        call("t", fn, sum(CY / 2 * max(64, size(a[0])) * (4 if "32" in str(a[1].dtype) else 1) for a in lst), R, W, Bk)
 
     def dma(e, sem, pairs, R, W):
-        need(e, R, W, ())
-        for o, i in pairs:
-            Q[e].dma_start(o, i).then_inc(T.sem[sem], 16)
-            cnt[sem] = cnt.get(sem, 0) + 16
-        note((sem, cnt[sem]), R, W, ())
+        def fn(s):
+            for o, i in pairs:
+                Q[e].dma_start(o, i).then_inc(T.sem[s], 16)
+        call(e, fn, 0.05 * len(pairs), R, W, late=2.0 + len(pairs), sem=(sem, 16 * len(pairs)))
 
     peers = peers_of(core, T)
     mask, ne = common_mask(core, peers, topo)
@@ -165,60 +235,60 @@ def rank_program(g, core, T, topo):
     cars = carriers(core, peers, topo)
     on = spare(core, cars[0], peers, topo)
 
+    def remote(trs, n, R, sem, m, tok, flight):
+        k = call("g", lambda s: g.remote_dma_fused(trs, local_sem=T.sem[s]), 0.3, R, [], late=0.01, sem=("snt", n))
+        calls[call("x", None, 0.0, [], [tok], late=flight, sem=(sem, m))]["dep"].add(k)
+
     def send(ap, sem, R, tok, src=None):
-        need("g", R, [], ())
-        g.remote_dma_fused([RemoteDMATransfer(dst_ids=ids, dma_engine_mask=mask, remote_sem=T.sem[sem],
-                                              src=ap if src is None else src, dsts=[ap] * len(ids))], local_sem=T.sem.snt)
-        cnt["snt"] = cnt.get("snt", 0) + ne
-        cnt[sem] = ne * len(ids)
-        wr[tok] = (sem, cnt[sem])
+        remote([RemoteDMATransfer(dst_ids=ids, dma_engine_mask=mask, remote_sem=T.sem[sem], src=ap if src is None else src,
+                                  dsts=[ap] * len(ids))], ne, R, sem, ne * len(ids), tok, FLIGHT)
 
     def hand_over(r):
-        sb = T["SB%d" % r]
-        need("g", ["sb%d" % r], [], ())
-        g.remote_dma_fused([RemoteDMATransfer(dst_ids=ids_of(core, [c], topo), dma_engine_mask=sum(1 << e for e in on[k::2]),
-                                              remote_sem=T.sem["ho%d" % r], src=sb[:, k * B:(k + 1) * B], dsts=[sb[:, k * B:(k + 1) * B]])
-                            for k, c in enumerate(cars)], local_sem=T.sem.snt)
-        cnt["snt"] += len(on)
-        o = unit(r, 2) * U + UB + B * rk
-        send(T.BG[:, o:o + B], "mw%d" % r, [], "wf%d" % r, sb[:, 2 * B:3 * B])
-        cnt["mw%d" % r] = 3 * ne * len(ids)
-        wr["wf%d" % r] = ("mw%d" % r, cnt["mw%d" % r])
+        o = [unit(r, l) * U + UB + B * rk for l in range(3)]
+        remote([RemoteDMATransfer(dst_ids=ids_of(core, [c], topo), dma_engine_mask=sum(1 << e for e in on[k::2]) if k < 2 else mask,
+                                  remote_sem=T.sem["ho%d" % r], src=T.BG[:, o[k]:o[k] + B], dsts=[T["SB%d" % r][:]])
+                for k, c in enumerate(cars)], len(on) + ne, ["wb%d%d" % (r, l) for l in range(3)],
+               "mw%d" % r, 3 * ne * len(ids), "wf%d" % r, 2.2 * FLIGHT)
 
     v, s = g.vector, g.scalar
 
     def ts(o, i, a, b, o0, o1, R, W, Bk=()):
         op("v", (lambda: v.tensor_scalar(o, i, a, b, o0, o1)) if o1 is not None else
-           (lambda: v.tensor_scalar(o, i, a, None, o0)), R, W, Bk)
+           (lambda: v.tensor_scalar(o, i, a, None, o0)), o, i, 1, R, W, Bk)
 
     def tt(o, i, j, o0, R, W, Bk=()):
-        op("v", lambda: v.tensor_tensor(o, i, j, o0), R, W, Bk)
+        op("v", lambda: v.tensor_tensor(o, i, j, o0), o, i, 1.0001 if Bk else 2, R, W, Bk)
 
     def cp(o, i, R, W, Bk=()):
-        op("v", lambda: v.tensor_copy(o, i), R, W, Bk)
+        op("v", lambda: v.tensor_copy(o, i), o, i, 1, R, W, Bk)
 
     def ms(o, c, W, Bk=()):
-        op("v", lambda: v.memset(o, c), [], W, Bk)
+        op("v", lambda: v.memset(o, c), o, o, 1, [], W, Bk)
 
     def scan(o, a, b, c, o0, o1, R, W, Bk=()):
-        op("v", lambda: v.tensor_tensor_scan(o, a, b, c, o0, o1), R, W, Bk)
+        op("v", lambda: v.tensor_tensor_scan(o, a, b, c, o0, o1), o, a, 1, R, W, Bk)
 
     def ac(o, i, f, R, W, Bk=(), bias=0.0, scale=1.0):
-        op("s", lambda: s.activation(o, i, f, bias=bias, scale=scale), R, W, Bk)
+        op("s", lambda: s.activation(o, i, f, bias=bias, scale=scale), o, i, 1, R, W, Bk)
 
     def io(o, pat, base, cm, W, fl=True):
         op("g", (lambda: g.iota(o, pat, base, cm, allow_small_or_imprecise_dtypes=True)) if fl else
-           (lambda: g.iota(o, pat, base, cm)), [], W)
+           (lambda: g.iota(o, pat, base, cm)), o, o, 3, [], W)
 
     BG = T.BG
     HW = [T["HW%d" % r] for r in range(RO)]
     DW = [T["DW%d" % r] for r in range(RO)]
     TT = [T["TT%d" % r] for r in range(RO)]
-    SB = [T["SB%d" % r] for r in range(RO)]
     ub = UB + B * rk
     pT, pH = [T.pT0, T.pT1], [T.pH0, T.pH1]
-    pv, bv = [T.pV, T.pN], ["pV", "pN"]
+    VAL, KEY, NAME = [(T.pV, "pV"), (T.pN, "pN")], [(T.pV, "pV"), (T.pK, "pK")], [(T.pA, "pA"), (T.pN, "pN")]
     I, Re, Cp = F.Identity, F.Relu, F.Copy
+
+    def gather(e, o, win, off, R, W):
+        if e == "s":
+            ac(o, ind(win, off), Cp, R, W)
+        else:
+            cp(o, ind(win, off), R, W)
 
     def wblk(r, l, a=0, b=V):
         return BG[:, unit(r, l) * U + a:unit(r, l) * U + b]
@@ -227,66 +297,48 @@ def rank_program(g, core, T, topo):
         return BG[:, (3 - l) * U + a:(3 - l) * U + b]
 
     def hown(r, a=0, b=V):
-        return T.HO[:, r * V + a:r * V + b]
+        return HW[r][:, a:b] if r < RO else T.hr[:, a:b]
 
     def sel(tab, i):
         return tab[:, 15 - i:143 - i]
 
     PT = ["PT%d" % i for i in range(16)]
-    PB = ["PB%d" % i for i in range(16)]
-    POS = ["POS%d" % c for c in range(6)]
+    T7 = ["T7%d" % c for c in range(3)]
+    ET = ["E%d" % l for l in range(6)]
     SF = ["SFa", "SFb"]
 
+    def tok(name, c0=0, c1=56):
+        return [name + k for k, (a, b, _) in zip("abc", EX) if a < c1 and c0 < b]
+
     def wown(r):
-        return ["w%d_%d" % (r, k) for k in range(4)]
+        return ["w%d_%d%d" % (r, h, c) for h in range(3) for c in range(3)]
 
     def wall(r):
-        return wown(r) + ["wb%d" % r, "wf%d" % r]
+        return wown(r) + ["wb%d%d" % (r, l) for l in range(3)] + ["wf%d" % r]
 
     def hall(r):
-        return ["hw%d" % r, "hb%d" % r, "hf%d" % r]
+        return ["h%d0" % r, "h%d1" % r, "hb%d" % r, "hf%d" % r]
 
-    def run(*lists):
-        for k in range(max(len(x) for x in lists)):
-            for x in lists:
-                if k < len(x):
-                    x[k]()
-
-    def table(h, i0, i1):
-        c0, c1, _ = HV[h]
-        n = 16 * (c1 - c0)
-        b = "pT%d" % h
-        lst = [(pT[h][:, 0:n], T.ID[:], T.CZ[:, 0:n], True, False)] if i0 == 0 else []
-        for i in range(i0, i1):
-            for l in range(3):
-                lst += [(pT[h][:, i:n:16], sel(T.PT[:, i, :], 3 + l), T.NF[:, l, c0:c1], False, False),
-                        (pT[h][:, i:n:16], sel(T.PB[:, i, :], l), T.H8[:, l, c0:c1], False, h == 0 and i == 15 and l == 2)]
-        mms(lst, ["ID", "CZ", "NF%d" % h, "H8%d" % h] + PT + PB, [b], [b])
-
-    def high_names(h):
-        c0, c1, _ = HV[h]
-        ts(T.H8[:, :, c0:c1], T.NF[:, :, c0:c1], 256.0, 127.516, A.mult, A.add, ["NF%d" % h], ["H8%d" % h])
-
-    def keep_table():
+    def name_table():
+        ts(T.H8[:], T.NF[:], 256.0, 127.516, A.mult, A.add, tok("NF"), ["H8"])
+        mms([(T.pK[0:56, 128 * l:128 * (l + 1)], T.H8[:, l], T.I8[:], True, True) for l in range(3)], ["H8", "I8"], ["key1"], ["pK"])
+        mms([(pT[0][0:56, 128 * l:128 * (l + 1)], a[:, l], b[:], k == 0, k == 1) for l in range(3)
+             for k, (a, b) in enumerate(((T.NF, T.ID), (T.H8, T.N8)))], ["H8", "ID", "N8"] + tok("NF"), ["pT0"], ["pT0"])
+        for l in range(6):
+            src, t, b = (T.pK, "key1", "pK") if l < 3 else (pT[0], "pT0", "pT0")
+            ac(T.E[0:56, l:128:16, :], src[0:56, 128 * (l % 3):128 * (l % 3 + 1)], I, [t, "Ez"], [ET[l]], [b], bias=-0.5 if l < 3 else 0.5)
+        for h, (a, b) in enumerate(HS):
+            lst = [(pT[h][:, 0:b - a], T.ID[:], BG[:, 0:b - a], True, False)] if h else []
+            lst += [(pT[h][:, i:b - a:16], T.E[0:56, :, i], T.ID[0:56, a // 16:b // 16], h == 0, h == 0) for i in range(16)]
+            mms(lst, ["ID", "z"] + ET, ["pT%d" % h], ["pT%d" % h])
         ac(T.TB[:], pT[0][:], Cp, ["pT0"], ["TB"], ["pT0"])
-
-    def mark_inner():
         ts(T.mk[:], T.TB[:, 0:B], T.O3[:, 3:4], 0.5, A.is_lt, A.mult, ["TB", "O33"], ["mk"])
-
-    def own_sums(r):
-        lst = [(T.pK[:, 0:400], T.NI[:], T.T7[:, 0:400], True, False), (T.pK[:, 0:400], T.IU[:], T.POS[:], False, False)]
-        if r:
-            lst += [(T.pK[:, c:392:7], T.IU[:], T.k6[:, r - 1], False, False) for c in range(3)]
-        for c in range(3):
-            lst += [(T.pK[:, c:392:7], sel(T.QK, i), BG[:, unit(r, c) * U + i:unit(r, c) * U + V:16], False, False) for i in range(16)]
-        mms(lst, ["NI", "IU", "QK", "T7", "k6"] + POS + wown(r), ["kp0", "kp1"], ["pK"])
 
     dma("y", "dhb", [(HW[0][:, ub:ub + B], T.h0[:, 0:B])], [], ["hb0"])
     dma("s", "dnb", [(T.nbi[:], T.nb[:])], [], ["nbi"])
-    dma("y", "dsb", [(SB[0][:, l * B:(l + 1) * B], T.w0[:, l * V:l * V + B]) for l in range(3)], [], ["sb0"])
-    dma("s", "dh", [(hown(0), T.h0[:]), (HW[0][:, 0:V], T.h0[:])], [], ["h0", "hw0"])
+    dma("y", "dsb", [(wblk(0, l, ub, ub + B), T.w0[:, l * V:l * V + B]) for l in range(3)], [], ["wb00", "wb01", "wb02"])
+    dma("s", "dh", [(hown(0), T.h0[:]), (T.HO[:], T.h0[:])], [], ["h00", "h01", "hc0", "hc2"])
     dma("y", "dw", [(wblk(0, l), T.w0[:, l * V:(l + 1) * V]) for l in range(3)], [], wown(0))
-    dma("y", "dc0", [(wblk(0, l, ub, ub + B), T.w0[:, l * V:l * V + B]) for l in range(3)], [], ["wb0"])
     io(T.PI[:, 0:1], [[0, 1]], 0, 1, ["PI0"], False)
     io(T.J[:], [[1, 144]], 0, 0, ["J"])
     io(T.c16[:], [[16, 56]], 0, 0, ["c16"])
@@ -305,434 +357,298 @@ def rank_program(g, core, T, topo):
     ts(T.OH[:], T.J[:, 0:16], pm, None, A.is_equal, None, ["J", "PF"], ["OH"])
     ts(T.QS[:], T.J[:], pg, 15.0, A.subtract, A.is_equal, ["J", "pg"], ["QS"])
     ts(T.VW[:], T.c16[:], pm, None, A.add, None, ["PF", "c16"], ["VW"])
-    ts(T.Q3[:], T.J[:], pg, 18.0, A.subtract, A.is_equal, ["J", "pg"], ["Q3"])
     ts(T.ID[:], T.J[:, 0:128], p, None, A.is_equal, None, ["J", "PF"], ["ID"])
-    tt(T.Q3[:], T.QS[:], T.Q3[:], A.subtract, ["QS", "Q3"], ["Q3"])
-    ts(T.Q2[:], T.Q3[:], 1 / 256.0, None, A.mult, None, ["Q3"], ["Q2"])
+    ms(T.E[:], 0.0, ["Ez"])
     for l in range(3):
         ts(T.SF[:, l, 0:10], T.VW[:, 0:10], float(ub), SC, A.add, A.mult, ["VW"], ["SFa"])
         ts(T.SF[:, l, 10:56], T.VW[:, 10:56], SC, None, A.mult, None, ["VW"], ["SFb"])
-    ac(T.NI[:], T.ID[:], I, ["ID"], ["NI"], scale=-1.0)
+    for t, k in (("NI", -1.0), ("I8", 1 / 256.0), ("N8", -1 / 256.0), ("IB", BIG), ("N4", -1.0), ("HI", 0.5)):
+        ac(T[t][:], T.ID[:], I, ["ID"], [t], scale=k)
+    ac(T.I4[:], T.ID[:, 0:40], Cp, ["ID"], ["I4"])
     ac(T.QH[:], T.QS[:], I, ["QS"], ["QH"], scale=0.5)
+    ac(T.QK[:], T.QS[:], I, ["QS"], ["QK"], scale=-2048.0)
     for i in range(16):
         ac(T.PT[:, i, :], T.QS[:], I, ["QS", "OH"], [PT[i]], scale=T.OH[:, i:i + 1])
-        ac(T.PB[:, i, :], T.Q2[:], I, ["Q2", "OH"], [PB[i]], scale=T.OH[:, i:i + 1])
     ts(T.ia[:], T.nbi[:], 10, None, A.arith_shift_right, None, ["nbi"], ["ia"])
     ts(T.ib[:], T.nbi[:], 1023, None, A.bitwise_and, None, ["nbi"], ["ib"])
     ts(T.fa[:], T.ia[:], float(B), float(UB), A.mult, A.add, ["ia"], ["fa"])
     ts(T.fb[:], T.ib[:], float(B), None, A.is_lt, None, ["ib"], ["fb"])
-    ts(T.ONE[:], T.JG[:], pg, 1.0 / FL, A.is_equal, A.mult, ["JG", "pg"], ["ONE"])
     tt(T.fa[:], T.fa[:], T.fb[:], A.mult, ["fa", "fb"], ["fa"])
-    ts(T.tri0[:], T.J[:, 0:128], p, -1.0, A.is_lt, A.mult, ["J", "PF"], ["tri0"])
     tt(T.fa[:], T.fa[:], T.ib[:], A.add, ["fa", "ib"], ["fa"])
+    ts(T.NF[:], T.fa[:], SC, None, A.mult, None, ["fa"], tok("NF"))
+    cp(T.NU[:], T.fa[:], ["fa"], tok("NU"))
+    tt(T.RF[:], T.NF[:], T.SF[:], A.subtract, tok("NF") + SF, tok("RF"))
+    ts(T.EM[:], T.RF[:], 0.0, 16.0, A.is_equal, A.mult, tok("RF"), tok("EM"))
     ts(T.O3[:, 0:1], pm, 3.0, None, A.is_lt, None, ["PF"], ["O30"])
-    ts(T.NF[:], T.fa[:], SC, None, A.mult, None, ["fa"], ["NF0", "NF1"])
-    cp(T.NU[:], T.fa[:], ["fa"], ["NU0", "NU1"])
-    tt(T.RF[:], T.NF[:], T.SF[:], A.subtract, ["NF0", "NF1"] + SF, ["RF0", "RF1"])
-    ts(T.O3[:, 4:5], pm, 6.0, 0.5, A.is_lt, A.mult, ["PF"], ["O34"])
-    high_names(0)
-    high_names(1)
-    tt(T.O3[:, 5:6], T.O3[:, 4:5], T.O3[:, 0:1], A.subtract, ["O30", "O34"], ["O35"])
     ts(T.O3[:, 3:4], T.O3[:, 0:1], 1.0 + (UB - 16) * SC, -1.0, A.mult, A.add, ["O30"], ["O33"])
-    ts(T.CZ[:], BG[:, 0:512], T.O3[:, 5:6], None, A.add, None, ["z", "O35"], ["CZ"])
-    ts(T.EM[:], T.RF[:], 0.0, 16.0, A.is_equal, A.mult, ["RF0", "RF1"], ["EM0", "EM1"])
+    ts(T.ONE[:], T.JG[:], pg, 1.0 / FL, A.is_equal, A.mult, ["JG", "pg"], ["ONE"])
+    ts(T.tri0[:], T.J[:, 0:128], p, -1.0, A.is_lt, A.mult, ["J", "PF"], ["tri0"])
+    ac(T.tri1[:], T.ID[:], I, ["ID"], ["tri1"], scale=-64.0)
+    tt(T.tri0[:], T.tri0[:], T.tri1[:], A.add, ["tri0", "tri1"], ["tri0"])
     tt(T.TRI[:], T.tri0[:], T.ONE[:], A.mult, ["tri0", "ONE"], ["TRI"])
     ts(T.S6[:], T.J[:, 0:128], p, 6.0, A.subtract, A.is_equal, ["J", "PF"], ["S6"])
     ts(T.S6[:], T.S6[:], T.O3[:, 0:1], None, A.mult, None, ["S6", "O30"], ["S6"])
-    ac(T.QK[:], T.QS[:], I, ["QS"], ["QK"], scale=-2048.0)
-    ac(T.IB[:], T.ID[:], I, ["ID"], ["IB"], scale=BIG)
-    ac(T.IU[:], T.ID[:], I, ["ID"], ["IU"], scale=-float(U16))
-    table(0, 0, 16)
-    table(1, 0, 16)
-    ms(T.POS[:], 0.0, ["POS"])
-    ms(T.k6[:, 0], 6.0, ["k6"])
-    ms(T.k6[:, 1], 12.0, ["k6"])
-    for c in range(6):
-        op("v", lambda: v.memset(T.POS[:, c:392:7], float(unit(0, c) if c < 3 else 6 - c)), ["POS"], [POS[c]])
-    keep_table()
+    ms(T.S7[:], 0.0, ["S7"])
     for l in range(3):
+        ts(T.T7[:, 3 + l:392:7], T.T7[:, 3 + l:392:7], float((3 - l) * U16), None, A.add, None, ["T7"], [T7[l]])
+        cp(T.S7[:, 3 + l:392:7], T.SF[:, 0], SF + ["S7"], ["S7%d" % l])
         ms(cw(l, V, U), 0.0, ["zc%d" % l])
     for r in range(RO):
         ms(DW[r][:, 0:B], 0.0, ["dwz%d" % r])
         ms(TT[r][:, 0:B], 0.0, ["ttz%d" % r])
     ts(T.bli[:], T.VW[:, 0:14], -3.0, 1 / 7.0, A.add, A.mult, ["VW"], ["bli"])
-    ms(T.RST[:], 0.0, ["RST"])
-    ms(T.n7[:, 0:8], 4.0, ["n7"])
-    ms(T.QB[:, :, 400:408], 0.0, ["QB01", "QB11", "QB21"])
     ts(T.BL[:], T.bli[:], 7.0, 6.0, A.mult, A.add, ["bli"], ["BL"])
+    ms(T.RST[:], 0.0, ["RST"])
     ms(T.RST[:, 0:400:7], 4 * BIG, ["RST"])
+    ms(T.n7[:, 0:8], 4.0, ["n70"])
+    ms(T.m56[:], -1.0, ["m56"])
+    ms(T.QB[:, :, 400:408], 0.0, ["QB0c", "QB1c", "QB2c"])
     for l in range(3):
         tt(T.O3[:, 1:2], T.OH[:, l:l + 1], T.OH[:, l + 3:l + 4], A.add, ["OH"], ["O31"])
         tt(T.O3[:, 2:3], T.O3[:, 1:2], T.OH[:, l + 6:l + 7], A.add, ["OH", "O31"], ["O32"])
-        ts(T.QF[:, l, :], T.QS[:], T.O3[:, 2:3], None, A.mult, None, ["QS", "O32"], ["QF%d" % l])
-    ts(T.FM[:], T.QS[:], T.OH[:, 0:1], 1.0 / GF, A.mult, A.mult, ["QS", "OH"], ["FM"])
-    ac(T.HI[:], T.ID[:], I, ["ID"], ["HI"], scale=0.5)
-    mark_inner()
-    own_sums(0)
+        ts(T.QF[:, 8 * l:8 * (l + 1)], T.JG[:, 0:128:16], pg, T.O3[:, 2:3], A.is_equal, A.mult, ["JG", "pg", "O32"], ["QF%d" % l])
+    ts(T.FM[:], T.QS[:], T.OH[:, 0:1], 0.5 / GF, A.mult, A.mult, ["QS", "OH"], ["FM"])
+    mms([(T.pN[:, 56 * c:56 * (c + 1)], sel(T.QK, i), BG[:, unit(0, c) * U + i:unit(0, c) * U + V:16], i == 0, i == 15)
+         for c in range(3) for i in range(16)], ["QK"] + wown(0), ["pN"], ["pN"])
+    ac(T.KS[:], T.pN[:, 0:168], I, ["pN"], ["KS"], ["pN"], scale=-1.0)
 
-    def count_votes(k, tab):
+    def votes(r, k):
         c0, c1 = CH[k]
-        n, o = c1 - c0, 3 * c0
-        lst = [(T.pA[:, o:o + 3 * n], T.ID[:], BG[:, 0:3 * n], True, False)]
-        lst += [(T.pA[:, o + l * n:o + (l + 1) * n], a[:], b, False, False) for l in range(3)
-                for a, b in ((T.ID, T.EM[:, l, c0:c1]), (T.NI, T.DA[:, c0:c1]))]
-        mms(lst, ["ID", "NI", "z", "DA%d" % k, "EM%d" % (k // 2)], ["vt%d" % k], ["pA"])
-        mms([(T.pA[:, o:o + 3 * n], sel(tab, i), T.cmp[:, 48 * c0 + i:48 * c1:16], False, i == 15) for i in range(16)],
+        n, o = 16 * (c1 - c0), 3 * c0
+        for l in range(3):
+            out, w, t = T.cmp[:, 48 * c0 + n * l:48 * c0 + n * (l + 1)], ind(HW[r][:], T.NU[:, l, c0:c1]), hall(r) + tok("NU", c0, c1)
+            if k != 1:
+                tt(out, w, T.HO[:, 16 * c0:16 * c1], A.is_lt, t + ["hc%d" % k], ["cmp%d%d" % (k, l)])
+                continue
+            b, ps = "pH%d" % (l % 2), pH[l % 2][:, 0:n]
+            ac(T.gI[:, l * n:(l + 1) * n], w, Cp, t, ["gI%d" % l])
+            mms([(ps, T.ID[:], hown(r, 16 * c0, 16 * c1), True, False), (ps, T.NI[:], T.gI[:, l * n:(l + 1) * n], False, True)],
+                ["ID", "NI", "gI%d" % l] + hall(r)[:2], [b], [b])
+            ac(out, ps, F.Sign, [b], ["cmp1%d" % l], [b], bias=-0.5)
+        lst = [(T.pA[:, o:3 * c1], T.ID[:], T.EM[:, :, c0:c1], True, False)]
+        if k == 0:
+            lst.append((T.pA[:, c0:c1], T.NI[:], T.DA[:, c0:c1], False, False))
+        mms(lst, ["ID", "NI", "DA%d" % k] + tok("EM", c0, c1), ["vt%d" % k], ["pA"])
+        mms([(T.pA[:, o:3 * c1], sel(T.QH if k == 1 else T.QS, i), T.cmp[:, 48 * c0 + i:48 * c1:16], False, i == 15) for i in range(16)],
             ["QS", "QH"] + ["cmp%d%d" % (k, l) for l in range(3)], ["vt%d" % k], ["pA"])
 
-    def votes(r, k, mid=()):
-        c0, c1 = CH[k]
-        n = c1 - c0
-        for l in range(3):
-            tt(T.cmp[:, 48 * c0 + 16 * n * l:48 * c0 + 16 * n * (l + 1)],
-               HW[r][:].indirect(T.NU[:, l, c0:c1]), hown(r, 16 * c0, 16 * c1), A.is_lt,
-               hall(r) + ["h%d" % r, "NU%d" % (k // 2)], ["cmp%d%d" % (k, l)])
-            for f in mid[l] if mid else ():
-                f()
-        count_votes(k, T.QS)
-
-    def votes_scalar(r):
-        c0, c1 = CH[1]
-        n = 16 * (c1 - c0)
-
-        def ga(l):
-            ac(T.gI[:, l * n:(l + 1) * n], HW[r][:].indirect(T.NU[:, l, c0:c1]), Cp, hall(r) + ["NU0"], ["gI%d" % l])
-
-        def df(l):
-            b = "pH%d" % (l % 2)
-            mms([(pH[l % 2][:, 0:n], T.ID[:], hown(r, 16 * c0, 16 * c1), True, False),
-                 (pH[l % 2][:, 0:n], T.NI[:], T.gI[:, l * n:(l + 1) * n], False, True)], ["ID", "NI", "h%d" % r, "gI%d" % l], [b], [b])
-
-        def sg(l):
-            b = "pH%d" % (l % 2)
-            ac(T.cmp[:, 48 * c0 + n * l:48 * c0 + n * (l + 1)], pH[l % 2][:, 0:n], F.Sign, [b], ["cmp1%d" % l], [b], bias=-0.5)
-        return [lambda: (ga(0), ga(1)), lambda: (df(0), df(1), ga(2), sg(0)),
-                lambda: (df(2), sg(1), sg(2), count_votes(1, T.QH))]
-
-    def deaths_steps(r, k):
+    def deaths(r, k):
         c0, c1 = CH[k]
         n, o = c1 - c0, 3 * c0
-        st = [lambda: ts(T.ok[:, o:o + 3 * n], T.pA[:, o:o + 3 * n], 1.0 if k == 1 else 9.0, 32.0, A.is_ge, A.mult,
-                         ["vt%d" % k], ["ok%d" % k], ["pA"]),
-              lambda: tt(T.d01[:, c0:c1], T.ok[:, o:o + n], T.ok[:, o + n:o + 2 * n], A.mult, ["ok%d" % k], ["d01%d" % k]),
-              lambda: tt(T.die[:, c0:c1], T.d01[:, c0:c1], T.ok[:, o + 2 * n:o + 3 * n], A.mult, ["ok%d" % k, "d01%d" % k], ["die%d" % k])]
-        if k:
-            ps, pn = (T.pN, "pN") if k == 1 else (pH[1], "pH1")
-
-            def rows():
-                mms([(ps[:, i:16 * n:16], sel(T.PT[:, i, :], 0), T.die[:, c0:c1], True, True) for i in range(16)],
-                    ["die%d" % k] + PT, [pn], [pn])
-                tt(T.DA[:, c0:c1], T.DA[:, c0:c1], T.die[:, c0:c1], A.add, ["DA%d" % k, "die%d" % k], ["DA%d" % k])
-            if k == 2:
-                return st + [rows, lambda: ts(DW[r][:, 16 * c0:16 * c1], ps[:, 0:16 * n], DS, None, A.mult, None, [pn], ["dw%d%d" % (r, k)], [pn])]
-            return st + [rows, lambda: ac(DW[r][:, 16 * c0:16 * c1], ps[:, 0:16 * n], I, [pn], ["dw%d%d" % (r, k)], [pn], scale=DS)]
-        cn = T.pA[:, 200:210]
-
-        def count():
+        ts(T.ok[:, o:o + 3 * n], T.pA[:, o:o + 3 * n], 1.0 if k == 1 else 9.0, 32.0, A.is_ge, A.mult, ["vt%d" % k], ["ok%d" % k], ["pA"])
+        tt(T.d01[:, c0:c1], T.ok[:, o:o + n], T.ok[:, o + n:o + 2 * n], A.mult, ["ok%d" % k], ["d01%d" % k])
+        tt(T.die[:, c0:c1], T.d01[:, c0:c1], T.ok[:, o + 2 * n:o + 3 * n], A.mult, ["ok%d" % k, "d01%d" % k], ["die%d" % k])
+        die, ps, pn, at = T.die[:, c0:c1], (T.pV, T.pN, pH[1])[k][:, 0:16 * n], ("pV", "pN", "pH1")[k], 16 * c0
+        if k == 0:
+            cn, die, at = T.pA[:, 200:210], T.dieB[:, 0:10], ub
             scan(T.cs[:, 0:10], T.o16[:, 0:10], T.die[:, 0:10], 0.0, A.mult, A.add, ["o16", "die0"], ["cs"])
             mms([(cn, T.TRI[:], T.die[:, 0:10], True, False), (cn, T.ONE[:], T.cs[:, 0:10], False, True)],
                 ["TRI", "ONE", "die0", "cs"], ["cn"], ["pA"])
-
-        def rows0():
-            tt(T.dieB[:, 0:10], T.die[:, 0:10], T.keep[:, 0:10], A.mult, ["die0", "keep"], ["dieB"])
-            mms([(T.pV[:, 352 + i:512:16], sel(T.PT[:, i, :], 0), T.dieB[:, 0:10], True, True) for i in range(16)],
-                ["dieB"] + PT, ["pVb"], ["pV"])
-
-        def out():
-            ts(DW[r][:, ub:ub + B], T.pV[:, 352:512], DS, None, A.mult, None, ["pVb"], ["dw%d0" % r], ["pV"])
+            ts(die, cn, CAP - 64.0, FL, A.is_le, A.mult, ["cn"], ["dieB"], ["pA"])
+        t = "dieB" if k == 0 else "die%d" % k
+        mms([(ps[:, i:16 * n:16], sel(T.PT[:, i, :], 0), die, True, True) for i in range(16)], [t] + PT, [pn], [pn])
+        ac(DW[r][:, at:at + 16 * n], ps, I, [pn], ["dw%d%d" % (r, k)], [pn], scale=GF / FL)
+        if k == 0:
             send(DW[r][:, ub:ub + B], "md%d" % r, ["dw%d0" % r], "dwf%d" % r)
-        return st + [count, lambda: None,
-                     lambda: ts(T.keep[:, 0:10], cn, float(CAP), None, A.is_le, None, ["cn"], ["keep"], ["pA"]), rows0,
-                     lambda: tt(T.DA[:, 0:10], T.DA[:, 0:10], T.dieB[:, 0:10], A.add, ["DA0", "dieB"], ["DA0"]), out]
+        tt(T.DA[:, c0:c1], T.DA[:, c0:c1], die, A.max, ["DA%d" % k, t], ["DA%d" % k])
 
     def before_gone(r):
         for l in range(3):
-            ts(T.PN[:, l], T.NF[:, l], 0.25 * (2 - l), None, A.add, None, ["NF0", "NF1"], ["PN%d" % l])
+            ts(T.PN[:, l], T.NF[:, l], 0.25 * (2 - l), None, A.add, None, tok("NF"), ["PN%d" % l])
         tt(T.VA[:], T.VW[:], T.DA[:], A.subtract, ["VW", "DA0", "DA1", "DA2"], ["VA"])
+        if r:
+            tt(T.KS[:], T.Ki[:], T.xi[:], A.subtract, tok("Ki") + tok("xi"), ["KS"])
         for l in range(3):
             ac(T.PA[:, l], T.VA[:], I, ["VA"], ["PA%d" % l], bias=(unit(r, l) * U - W0) / GF, scale=1 / GF)
+            ac(T.KP[:, l], T.KS[:, l], I, ["KS"], ["KP%d" % l], bias=float(unit(r, l) * U16))
 
-    def gs(h, l, a, b):
-        c0, c1, _ = HV[h]
-        o = 48 * c0 + 16 * (c1 - c0) * l - 16 * c0
+    def gs(l, a, b):
+        e, f = PS[int(a >= PS[1][0])]
+        o = 2 * e + (f - e) * l
         return T.G[:, o + a:o + b]
 
-    def first_dead(h):
-        c0, c1, _ = HV[h]
-        o, k = pv[h][:, 0:3 * (c1 - c0)], str(h)
-        return [lambda: tt(T.AB[:, 1, :, c0:c1], o, T.PA[:, :, c0:c1], A.mult, ["val" + k, "PA0", "PA1", "PA2"], ["AB1" + k], [bv[h]]),
-                lambda: tt(T.AB[:, 0, :, c0:c1], o, T.PN[:, :, c0:c1], A.mult, ["val" + k, "PN0", "PN1", "PN2"], ["AB0" + k], [bv[h]]),
-                lambda: tt(T.m1[:, :, c0:c1], T.AB[:, :, 0, c0:c1], T.AB[:, :, 2, c0:c1], A.max, ["AB0" + k, "AB1" + k], ["m1" + k]),
-                lambda: tt(T.m[:, :, c0:c1], T.m1[:, :, c0:c1], T.AB[:, :, 1, c0:c1], A.max, ["m1" + k, "AB0" + k, "AB1" + k], ["m" + k]),
-                lambda: cp(T.WU[:, c0:c1], T.m[:, 1, c0:c1], ["m" + k], ["WU" + k]),
-                lambda: ts(T.oi[:, c0:c1], T.m[:, 0, c0:c1], 2047, None, A.bitwise_and, None, ["m" + k], ["oi" + k]),
-                lambda: cp(T.OU[:, c0:c1], T.oi[:, c0:c1], ["oi" + k], ["OU" + k])]
-
-    def gone(r):
-        dwt = ["dw%d%d" % (r, k) for k in range(3)] + ["dwf%d" % r, "dwz%d" % r, "NU0", "NU1"]
-
-        def val(h):
-            c0, c1, _ = HV[h]
-            mms([(pv[h][:, 0:3 * (c1 - c0)], sel(T.QS, i), T.G[:, 48 * c0 + i:48 * c1:16], i == 0, i == 15) for i in range(16)],
-                ["QS"] + ["G%d%d" % (h, l) for l in range(3)] + ["Gb%d" % l for l in range(3 - 3 * h)], ["val%d" % h, bv[h]], [bv[h]])
-
-        def marks(h):
-            a, b = HS[h]
-            lst = [(pT[0][:], T.ID[:], T.TB[:], True, False)] if h == 0 else []
-            lst += [(pT[h][:, 0:b - a], sel(T.FM, 6 + l), gs(h, l, a, b), False, l == 2) for l in range(3)]
-            mms(lst, ["FM", "ID", "TB"] + ["G%d%d" % (h, l) for l in range(3)], ["pT%d" % h], ["pT%d" % h])
-        pb = T.pV[:, 176:176 + B]
-        mms([(pb, T.ID[:], T.TB[:, 0:B], True, False), (pb, T.S6[:], T.mk[:], False, False)], ["ID", "S6", "TB", "mk"], ["pc"], ["pV"])
+    def gone(r, h):
+        a, b = PS[h]
+        c0, c1, k = a // 16, b // 16, str(h)
+        dwt = ["dw%d%d" % (r, j) for j in range(3)] + ["dwf%d" % r, "dwz%d" % r] + tok("NU", c0, c1)
+        gt = ["G%d%d" % (h, l) for l in range(3)]
         for l in range(3):
-            ac(gs(0, l, 0, B), DW[r][:].indirect(T.NU[:, l, 0:10]), Cp, dwt, ["Gb%d" % l])
-            cp(gs(1, l, 512, V), DW[r][:].indirect(T.NU[:, l, 32:56]), dwt, ["G1%d" % l])
-        mms([(pb, sel(T.FM, 6 + l), gs(0, l, 0, B), False, l == 2) for l in range(3)], ["FM", "Gb0", "Gb1", "Gb2"], ["pc"], ["pV"])
-        ac(gs(0, 0, B, 512), DW[r][:].indirect(T.NU[:, 0, 10:32]), Cp, dwt, ["G00"])
-        ac(T.LS[:, r], pb, Cp, ["pc"], ["ls%d" % r], ["pV"])
-        send(TT[r][:, ub:ub + B], "mb%d" % r, ["ls%d" % r], "tf%d" % r, T.LS[:, r])
-        val(1)
-        cp(gs(0, 2, B, 512), DW[r][:].indirect(T.NU[:, 2, 10:32]), dwt, ["G02"])
-        ac(gs(0, 1, B, 512), DW[r][:].indirect(T.NU[:, 1, 10:32]), Cp, dwt, ["G01"])
-        val(0)
-        marks(1)
-        run(first_dead(1))
-        marks(0)
-        ac(T.gm[:, :, 32:56], pv[1][:, 0:72], Cp, ["val1"], ["gm1"], ["pN"])
-        ac(TT[r][:, 512:V], pT[1][:, 0:384], Cp, ["pT1"], ["TT1"], ["pT1"])
+            gather(GE[h][l], gs(l, a, b), DW[r][:], T.NU[:, l, c0:c1], dwt, [gt[l]])
+        if h == 0:
+            pc = T.pV[:, 176:176 + B]
+            mms([(pc, T.ID[:], T.TB[:, 0:B], True, False), (pc, T.S6[:], T.mk[:], False, False)], ["ID", "S6", "TB", "mk"], ["pV"], ["pV"])
+            mms([(pc, sel(T.FM, 6 + l), gs(l, 0, B), False, l == 2) for l in range(3)], ["FM"] + gt, ["pV"], ["pV"])
+            ac(T.LS[:, r], pc, Cp, ["pV"], ["ls%d" % r], ["pV"])
+            send(TT[r][:, ub:ub + B], "mb%d" % r, ["ls%d" % r], "tf%d" % r, T.LS[:, r])
+        o, bk = VAL[h][0][:, 0:3 * (c1 - c0)], VAL[h][1]
+        mms([(o, sel(T.QS, i), T.G[:, 3 * a + i:3 * b:16], i == 0, i == 15) for i in range(16)], ["QS"] + gt, [bk], [bk])
+        tt(T.AB[:, 1, :, c0:c1], o, T.PA[:, :, c0:c1], A.mult, [bk, "PA0", "PA1", "PA2"], ["AB1" + k], [bk])
+        tt(T.AB[:, 0, :, c0:c1], o, T.PN[:, :, c0:c1], A.mult, [bk, "PN0", "PN1", "PN2"], ["AB0" + k], [bk])
+        ac(T.gm[:, :, c0:c1], o, Cp, [bk], ["gm" + k], [bk])
+        tt(T.m1[:, :, c0:c1], T.AB[:, :, 0, c0:c1], T.AB[:, :, 2, c0:c1], A.max, ["AB0" + k, "AB1" + k], ["m1" + k])
+        tt(T.m[:, :, c0:c1], T.m1[:, :, c0:c1], T.AB[:, :, 1, c0:c1], A.max, ["m1" + k, "AB0" + k, "AB1" + k], ["m" + k])
+        cp(T.WU[:, c0:c1], T.m[:, 1, c0:c1], ["m" + k], ["WU" + k])
+        ts(T.oi[:, c0:c1], T.m[:, 0, c0:c1], 2047, None, A.bitwise_and, None, ["m" + k], ["oi" + k])
+        cp(T.OU[:, c0:c1], T.oi[:, c0:c1], ["oi" + k], ["OU" + k])
+        ts(T.nh[:, 0, c0:c1], T.m[:, 1, c0:c1], 0.0, None, A.is_le, None, ["m" + k], ["nh" + k])
+        for t in (1, 2):
+            ac(T.nh[:, t, c0:c1], T.nh[:, 0, c0:c1], Cp, ["nh" + k], ["nh%d%s" % (t, k)])
+        gather(WE[h], T.ws[:, a:b], BG[:, W0:unit(r, 0) * U + V], T.WU[:, c0:c1],
+               ["zc0", "WU" + k] + [t for q in range(r + 1) for t in wall(q)], ["ws" + k])
 
-    def splice(r):
-        od = T.OU[:]
-        kp = ["kp0", "kp1"]
-        ou = ["OU0", "OU1"]
-        win = BG[:, W0:unit(r, 0) * U + V]
-        wt = ["zc0"] + [t for q in range(r + 1) for t in wall(q)]
-        pb = T.pA[:, 352:512]
-
-        def wd2(h):
-            a, b = HS[h]
-            ac(T.wd2[:, a:b], wblk(r, 2, 0, X).indirect(T.OU[:, a // 16:b // 16]), Cp, wall(r) + ["OU%d" % h], ["wd2%d" % h])
-
-        def hd(h):
-            a, b = HS[h]
-            tt(T.tt[:, a:b], HW[r][:].indirect(T.OU[:, a // 16:b // 16]), T.ws[:, a:b], A.subtract,
-               hall(r) + ["OU%d" % h, "ws%d" % h], ["tt%d" % h])
-
-        def cand2(h):
-            a, b = HS[h]
-            mms([(pH[h][:, 0:b - a], T.ID[:], T.wd2[:, a:b], True, False), (pH[h][:, 0:b - a], T.NI[:], T.tt[:, a:b], False, True)],
-                ["ID", "NI", "wd2%d" % h, "tt%d" % h], ["pH%d" % h], ["pH%d" % h])
-            ac(T.wd2[:, a:b], pH[h][:, 0:b - a], Re, ["pH%d" % h], ["wd2%d" % h], ["pH%d" % h])
-
-        def sums(l):
-            mms([(T.pK[:, 3 + l:392:7], sel(T.QK, i), BG[:, (3 - l) * U + i:(3 - l) * U + V:16], False, False)
-                 for i in range(16)], ["QK", "cw%d" % l], kp, ["pK"])
-
-        def cand(l):
-            tt(cw(l), wblk(r, l, 0, X).indirect(od), T.tt[:], A.subtract, wall(r) + ou + ["tt0", "tt1"], ["cw%d" % l])
-        cp(T.ws[:, 512:V], win.indirect(T.WU[:, 32:56]), wt + ["WU1"], ["ws1"])
-        wd2(1)
-        f = first_dead(0)
-        run(f[:5])
-        ac(T.gm[:, :, 0:32], pv[0][:, 0:96], Cp, ["val0"], ["gm0"], ["pV"])
-        ac(T.ws[:, 0:512], win.indirect(T.WU[:, 0:32]), Cp, wt + ["WU0"], ["ws0"])
-        run(f[5:])
-        if r:
-            own_sums(r)
-        ts(T.nh[:], T.m[:, 1], 0.0, None, A.is_le, None, ["m0", "m1"], ["nh"])
-        hd(1)
-        if r + 1 < RO:
-            mms([(pb, T.ID[:], T.ws[:, 0:B], True, False), (pb, T.NI[:], hown(r, 0, B), False, True)],
-                ["ID", "NI", "ws0", "h%d" % r], ["pb"], ["pA"])
-        wd2(0)
-        hd(0)
-        if r + 1 < RO:
-            ts(T.hyb[:], pb, 0.0, 255.6, A.max, A.add, ["pb"], ["hyb"], ["pA"])
-            mms([(pb, T.ID[:], hown(r, 0, B), True, False), (pb, T.HI[:], T.hyb[:], False, True)],
-                ["ID", "HI", "hyb", "h%d" % r], ["pb"], ["pA"])
-            ac(HW[r + 1][:, ub:ub + B], pb, I, ["pb"], ["hb%d" % (r + 1)], ["pA"], bias=-128.0)
-            send(HW[r + 1][:, ub:ub + B], "mh%d" % (r + 1), ["hb%d" % (r + 1)], "hf%d" % (r + 1))
+    def marks(r):
+        mms([(pT[0][:], T.ID[:], T.TB[:], True, False)] +
+            [(pT[0][:, a:b], sel(T.FM, 6 + l), gs(l, a, b), False, a > 0 and l == 2) for a, b in (CUT[0][0], CUT[1][0]) for l in range(3)],
+            ["FM", "ID", "TB"] + ["G%d%d" % (h, l) for h in range(2) for l in range(3)], ["pT0"], ["pT0"])
+        mms([(pT[1][:, 0:384], sel(T.FM, 6 + l), gs(l, 512, V), False, l == 2) for l in range(3)],
+            ["FM", "G10", "G11", "G12"], ["pT1"], ["pT1"])
         ac(TT[r][:, ub:ub + B], pT[0][:, 0:B], Cp, ["pT0"], ["tb%d" % r], ["pT0"])
         ac(TT[r][:, B:512], pT[0][:, B:512], Cp, ["pT0"], ["TT0"], ["pT0"])
-        cand(0)
-        ac(T.Fg[:], TT[r][:].indirect(od), Cp, ["TT0", "TT1", "tb%d" % r, "tf%d" % r, "ttz%d" % r] + ou, ["Fg"])
-        mms([(T.pK[:, c:392:7], T.IB[:], a[:, c], False, False) for c in range(3) for a in (T.gm, T.EM)] +
-            [(T.pK[:, c:392:7], T.IB[:], T.nh[:], False, False) for c in range(6)], ["IB", "nh", "gm0", "gm1", "EM0", "EM1"], kp, ["pK"])
-        mms([(T.pN[:, 0:400], T.ID[:], BG[:, 0:400], True, False)] +
-            [(T.pN[:, c:392:7], T.ID[:], T.RF[:, c], False, False) for c in range(3)] +
-            [(T.pN[:, c:392:7], T.NI[:], T.SF[:, 0], False, False) for c in range(3, 6)],
-            ["ID", "NI", "RF0", "RF1", "z"] + SF, ["pN"], ["pN"])
-        cand2(1)
-        cand2(0)
-        ts(cw(0), cw(0), 0.0, 255.0, A.max, A.min, ["cw0"], ["cw0"])
-        cand(1)
-        sums(0)
-        mms([(T.pN[:, 3 + l:392:7], sel(T.QF[:, l, :], i), T.Fg[:, i:V:16], False, l == 2 and i == 15)
-             for l in range(3) for i in range(16)], ["QF0", "QF1", "QF2", "Fg"], ["pN"], ["pN"])
-        for t in range(3):
-            ac(T.NH[:, t], T.nh[:], I, ["nh"], ["NH%d" % t], scale=float(unit(r, t) * U16))
-        ts(cw(1), cw(1), 0.0, 255.0, A.max, A.min, ["cw1"], ["cw1"])
-        ts(cw(2), T.wd2[:], 255.0, None, A.min, None, ["wd20", "wd21"], ["cw2"])
-        sums(1)
+        ac(TT[r][:, 512:V], pT[1][:, 0:384], Cp, ["pT1"], ["TT1"], ["pT1"])
+
+    def border_heights(r):
+        pb = T.pA[:, 352:512]
+        mms([(pb, T.ID[:], T.ws[:, 0:B], True, False), (pb, T.NI[:], hown(r, 0, B), False, True)], ["ID", "NI", "ws0", "h%d0" % r], ["pb"], ["pA"])
+        ts(T.hyb[:], pb, 0.0, 255.6, A.max, A.add, ["pb"], ["hyb"], ["pA"])
+        mms([(pb, T.ID[:], hown(r, 0, B), True, False), (pb, T.HI[:], T.hyb[:], False, True)], ["ID", "HI", "hyb", "h%d0" % r], ["pb"], ["pA"])
+        ac(HW[r + 1][:, ub:ub + B], pb, I, ["pb"], ["hb%d" % (r + 1)], ["pA"], bias=-128.0)
+        send(HW[r + 1][:, ub:ub + B], "mh%d" % (r + 1), ["hb%d" % (r + 1)], "hf%d" % (r + 1))
+
+    def splice(r, h):
+        a, b = PS[h]
+        c0, c1, k = a // 16, b // 16, str(h)
+        n, x, y = c1 - c0, 7 * c0, WIDE[h]
+        od, ou = T.OU[:, c0:c1], ["OU" + k]
+        (pk, bk), (pn, bn) = KEY[h], NAME[h]
+        nh = ["nh" + k, "nh1" + k, "nh2" + k]
+
+        def col(p, c):
+            return p[:, x + c:7 * c1:7]
+        mms([(pk[:, x:y], T.NI[:], T.T7[:, x:y], True, False), (col(pk, 6), T.IB[:], T.m56[:, 0:n], False, False)] +
+            [(col(pk, c), T.N4[:], T.KP[:, c, c0:c1], False, False) for c in range(3)],
+            ["NI", "N4", "IB", "m56", "KP0", "KP1", "KP2"] + T7, ["key" + k], [bk])
+        mms([(col(pk, c), T.IB[:], T.gm[:, c, c0:c1], False, False) for c in range(3)] +
+            [(col(pk, c), T.IB[:], T.nh[:, 0, c0:c1], False, False) for c in range(6)], ["IB", "nh" + k, "gm" + k], ["key" + k], [bk])
+        tt(T.ON[:, :, c0:c1], T.RF[:, :, c0:c1], T.nh[:, :, c0:c1], A.mult, tok("RF", c0, c1) + nh, ["ON" + k])
+        tt(T.NH[:, :, c0:c1], T.KP[:, :, c0:c1], T.nh[:, :, c0:c1], A.mult, ["KP0", "KP1", "KP2"] + nh, ["NH" + k])
+        tt(T.OS[:, :, c0:c1], T.ON[:, :, c0:c1], T.SF[:, :, c0:c1], A.add, ["ON" + k] + SF, ["OS" + k])
+        tt(T.tt[:, a:b], ind(HW[r][:], od), T.ws[:, a:b], A.subtract, hall(r) + ou + ["ws" + k], ["tt" + k])
+        ac(T.wd2[:, a:b], ind(wblk(r, 2, 0, X), od), Cp, wall(r) + ou, ["wd2" + k])
+        for e, f in CUT[h]:
+            j = e // 512
+            ps = pH[j][:, e - 512 * j:f - 512 * j]
+            mms([(ps, T.ID[:], T.wd2[:, e:f], True, False), (ps, T.NI[:], T.tt[:, e:f], False, True)],
+                ["ID", "NI", "wd2" + k, "tt" + k], ["pH%d" % j], ["pH%d" % j])
+            ac(T.wr2[:, e:f], ps, Re, ["pH%d" % j], ["wr%d" % e], ["pH%d" % j])
         for l in range(3):
-            ts(T.P1[:, l], T.pN[:, 3 + l:392:7], 0.0, None, A.is_equal, None, ["pN"], ["P1%d" % l], ["pN"])
-        for l in range(3):
-            ac(T.P2[:, l], T.pN[:, 3 + l:392:7], Re, ["pN"], ["P2%d" % l], ["pN"], bias=-64.0, scale=256.0)
-        ac(T.n7[:, 1:401], T.pN[:, 0:400], Cp, ["pN"], ["n7"], ["pN"])
-        ac(T.n7[:, 7:401:7], T.RST[:, 1:400:7], I, ["RST", "n7"], ["n7"], bias=4.0)
-        for t in range(3):
-            tt(T.ON[:, t], T.RF[:, t], T.nh[:], A.mult, ["RF0", "RF1", "nh"], ["ON%d" % t])
-        sums(2)
-        mms([(T.pK[:, 3 + l:392:7], T.IB[:], a[:, l], False, k == 1 and l == 2) for k, a in enumerate((T.P1, T.P2)) for l in range(3)],
-            ["IB", "P10", "P11", "P12", "P20", "P21", "P22"], kp, ["pK"])
-        tt(T.dn[:], T.n7[:, 0:400], T.pN[:, 0:400], A.subtract, ["n7", "pN"], ["dn"], ["pN"])
+            t = "cw%d%s" % (l, k)
+            if l < 2:
+                tt(cw(l, a, b), ind(wblk(r, l, 0, X), od), T.tt[:, a:b], A.subtract, wall(r) + ou + ["tt" + k], [t])
+                ts(cw(l, a, b), cw(l, a, b), 0.0, 255.0, A.max, A.min, [t], [t])
+            else:
+                ts(cw(l, a, b), T.wr2[:, a:b], 255.0, None, A.min, None, ["wr%d" % e for e, f in CUT[h]], [t])
+            mms([(col(pk, 3 + l), sel(T.QK, i), BG[:, (3 - l) * U + a + i:(3 - l) * U + b:16], False, False) for i in range(16)],
+                ["QK", t], ["key" + k], [bk])
+        ac(T.Fg[:, a:b], ind(TT[r][:], od), Cp, ["TT0", "TT1", "tb%d" % r, "tf%d" % r, "ttz%d" % r] + ou, ["Fg" + k])
+        mms([(pT[0][0:n, i:384:16], T.Fg[:, a + i:b:16], T.QF[:], True, True) for i in range(16)], ["QF0", "QF1", "QF2", "Fg" + k], ["pT0"], ["pT0"])
+        ac(T.E2[0:n, h], pT[0][0:n, 0:384], Cp, ["pT0"], ["E2" + k], ["pT0"])
+        mms([(pn[:, x:y], T.NI[:], T.S7[:, x:y], True, False)] + [(col(pn, c), T.ID[:], T.RF[:, c, c0:c1], False, False) for c in range(3)],
+            ["ID", "NI", "S70", "S71", "S72"] + tok("RF", c0, c1), ["nam" + k], [bn])
+        mms([(col(pn, 3 + l), T.E2[0:n, h, 128 * l:128 * (l + 1)], T.I4[0:n, 0:n], False, l == 2) for l in range(3)],
+            ["I4", "E2" + k], ["nam" + k], [bn])
+        ac(T.P2[:, x:y], pn[:, x:y], Re, ["nam" + k], ["P2" + k], [bn], bias=-64.0, scale=256.0)
+        ac(T.n7[:, 1 + x:1 + y], pn[:, x:y], Cp, ["nam" + k], ["n7" + k], [bn])
+        ac(T.n7[:, x + 7:y + 1:7], T.RST[:, x + 1:y - 5:7], I, ["RST"], ["n7" + k], bias=4.0)
+        ts(T.P1[:, x:y], pn[:, x:y], 0.0, None, A.is_equal, None, ["nam" + k], ["P1" + k], [bn])
+        mms([(pk[:, x:y], T.IB[:], q[:, x:y], False, j == 1) for j, q in enumerate((T.P2, T.P1))], ["IB", "P1" + k, "P2" + k], ["key" + k], [bk])
+        tt(T.dn[:, x:y], T.n7[:, x:y], pn[:, x:y], A.subtract, ["n70", "n7" + k, "nam" + k], ["dn" + k], [bn])
 
     def heights(r):
         for h, (a, b) in enumerate(HS):
-            mms([(pH[h][:, 0:b - a], T.ID[:], T.ws[:, a:b], True, False), (pH[h][:, 0:b - a], T.NI[:], hown(r, a, b), False, True)],
-                ["ID", "NI", "ws%d" % h, "h%d" % r], ["pH%d" % h], ["pH%d" % h])
-            ac(T.hr[:, a:b], pH[h][:, 0:b - a], Re, ["pH%d" % h], ["hr%d" % h], ["pH%d" % h])
-        for h, (a, b) in enumerate(HS):
-            ac(T.hy[:, a:b], T.hr[:, a:b], I, ["hr%d" % h], ["hy%d" % h], bias=255.6)
-            mms([(pH[h][:, 0:b - a], T.ID[:], hown(r, a, b), True, False), (pH[h][:, 0:b - a], T.HI[:], T.hy[:, a:b], False, True)],
-                ["ID", "HI", "hy%d" % h, "h%d" % r], ["pH%d" % h], ["pH%d" % h])
-        for h, (a, b) in enumerate(HS):
-            ac(hown(r + 1, a, b), pH[h][:, 0:b - a], I, ["pH%d" % h], ["h%d" % (r + 1)], ["pH%d" % h], bias=-128.0)
-        if r + 1 < RO:
-            ac(HW[r + 1][:, 0:V], hown(r + 1), Cp, ["h%d" % (r + 1)], ["hw%d" % (r + 1)])
-        else:
-            dma("y", "dout", [(T.yh[:], hown(RO))], ["h%d" % RO], [])
-
-    def extract(a, n, k, pad=0):
-        b = a + n
-        bl = T.BL[:, 0:n // 16]
-        h = k[0]
-        kq = "kq" + k
-        st = []
-        for t in range(3):
-            st.append(lambda t=t: scan(T.RB[:, t, a:b], T.RST[:, a:b], T.pK[:, a:b], 0.0, A.add, A.min,
-                                       ["RST", kq, "kp" + h], ["RB%d%s" % (t, k)], ["pK"]))
-            st.append(lambda t=t: tt(T.nq[:, a:b], T.RB[:, t, a:b], T.pK[:, a:b], A.not_equal,
-                                     ["RB%d%s" % (t, k), kq, "kp" + h], ["nq" + k], ["pK"]))
-            st.append(lambda t=t: scan(T.QB[:, t, a:b], T.dn[:, a:b], T.nq[:, a:b], 0.0, A.add, A.mult,
-                                       ["dn", "nq" + k], ["QB%d%s" % (t, k)]))
-            if t < 2:
-                st.append(lambda t=t: tt(T.kp[:, a:b], T.QB[:, t, a:b + pad].indirect(bl), T.n7[:, 1 + a:1 + b], A.not_equal,
-                                         ["QB%d%s" % (t, k), "n7", "BL"], ["pen" + k]))
-                st.append(lambda: tt(T.pK[:, a:b], T.pK[:, a:b], T.kp[:, a:b], A.mult, [kq, "kp" + h, "pen" + k], [kq], ["pK"]))
-        return st
-
-    def both(x, y):
-        return [(lambda f=f, e=e: (f(), e())) for f, e in zip(x, y)]
-
-    def choose_steps(r, h):
-        c0, c1, n = HV[h]
-        a = 7 * c0
-        k = str(h)
-        if h == 0:
-            st, ks = both(extract(0, 112, "0a"), extract(112, 112, "0b")), ["0a", "0b"]
-        elif r + 1 == RO:
-            st, ks = both(extract(a, 112, "1a"), extract(a + 112, 64, "1", 8)), ["1a", "1"]
-        else:
-            st, ks = extract(a, n, "1", 8), ["1"]
-        rb = ["RB%d%s" % (t, x) for t in range(3) for x in ks]
-        qb = ["QB%d%s" % (t, x) for t in range(3) for x in ks]
-        ki = lambda: tt(T.Ki[:, :, c0:c1], T.NH[:, :, c0:c1], T.RB[:, :, a + 6:7 * c1:7], A.subtract, rb + ["NH0", "NH1", "NH2"], ["Ki" + k])
-        xi = lambda: ts(T.xi[:, :, c0:c1], T.Ki[:, :, c0:c1], 2047, None, A.bitwise_and, None, ["Ki" + k], ["xi" + k])
-        st = st[:-1] + [lambda f=st[-1]: (ki(), f(), xi())]
-        rf = lambda: tt(T.RF[:, :, c0:c1], T.QB[:, :, a + 6:7 * c1:7], T.ON[:, :, c0:c1], A.add, qb + ["ON0", "ON1", "ON2"], ["RF" + k])
-        nf = lambda: tt(T.NF[:, :, c0:c1], T.RF[:, :, c0:c1], T.SF[:, :, c0:c1], A.add, ["RF" + k] + SF, ["NF" + k])
-        eu = lambda: ts(T.EU[:, :, c0:c1], T.xi[:, :, c0:c1], 16.0, pm, A.mult, A.add, ["xi" + k, "PF"], ["EU" + k])
-        if r + 1 == RO:
-            return st + [eu, rf, nf]
-        nu = lambda: ts(T.NU[:, :, c0:c1], T.NF[:, :, c0:c1], 1 / SC, None, A.mult, None, ["NF" + k], ["NU" + k])
-        em = lambda: ts(T.EM[:, :, c0:c1], T.RF[:, :, c0:c1], 0.0, 16.0, A.is_equal, A.mult, ["RF" + k], ["EM" + k])
-        if h:
-            return st + [rf, eu, nf, em, nu]
-        eb = lambda: ts(T.EB[:], T.xi[:, :, 0:10], 16.0, pm, A.mult, A.add, ["xi0", "PF"], ["EB"])
-        return st + [rf, eb, nf, em, nu, eu]
-
-    def pool(r):
-        return BG[:, 0:unit(r, 0) * U + V], ["z", "zc0", "zc1", "zc2", "cw0", "cw1", "cw2"] + [t for q in range(r + 1) for t in wall(q)]
-
-    def border_weights(r):
-        win, R = pool(r)
-        ac(SB[r + 1][:], win.indirect(T.EB[:]), Cp, R + ["EB"], ["sb%d" % (r + 1)])
-        hand_over(r + 1)
-
-    def place_border(r):
-        dma("y", "dc%d" % r, [(wblk(r, l, o, o + B), SB[r][:, l * B:(l + 1) * B]) for l in range(3) for o in (0, ub)],
-            ["sb%d" % r, "die1"], ["wb%d" % r, "w%d_3" % r])
-
-    def new_weights(r, h, eng="sss", which=(0, 1, 2)):
-        c0, c1, _ = HV[h]
-        if h == 0 and r + 1 < RO:
-            c0 = 10
-        win, R = pool(r)
-        for t in which:
-            src = win.indirect(T.EU[:, t, c0:c1])
+            ps, bk, k = pH[h][:, 0:b - a], "pH%d" % h, str(h)
+            mms([(ps, T.ID[:], T.ws[:, a:b], True, False), (ps, T.NI[:], hown(r, a, b), False, True)],
+                ["ID", "NI", "ws0", "ws1", "h%d%d" % (r, h)], [bk], [bk])
+            ac(T.hr[:, a:b], ps, Re, [bk], ["hr" + k], [bk])
+            ac(T.hy[:, a:b], T.hr[:, a:b], I, ["hr" + k], ["hy" + k], bias=255.6)
+            mms([(ps, T.ID[:], hown(r, a, b), True, False), (ps, T.HI[:], T.hy[:, a:b], False, True)],
+                ["ID", "HI", "hy" + k, "h%d%d" % (r, h)], [bk], [bk])
+            ac(hown(r + 1, a, b), ps, I, [bk], ["h%d%d" % (r + 1, h), "hr" + k], [bk], bias=-128.0)
             if r + 1 < RO:
-                o, tok = wblk(r + 1, t, 16 * c0, 16 * c1), "w%d_%d" % (r + 1, h if eng[t] == "s" else 2)
-            else:
-                o, tok = T.WF[:, t * V + 16 * c0:t * V + 16 * c1], "yw%d%d" % (t, h)
-            if eng[t] == "s":
-                ac(o, src, Cp, R + ["EU%d" % h], [tok])
-            else:
-                cp(o, src, R + ["EU%d" % h], [tok])
-            if r + 1 == RO:
-                dma("y", "dout", [(T.yw[:, t * V + 16 * c0:t * V + 16 * c1], o)], [tok], [])
+                e = B if h == 0 else b - a
+                ac(T.HO[:, a:a + e], ps[:, 0:e], I, [bk], ["hc%d" % (2 * h)], [bk], bias=-128.0)
+        if r + 1 == RO:
+            dma("y", "dout", [(T.yh[:], hown(RO))], ["h%d0" % RO, "h%d1" % RO], [])
 
-    nop = [lambda: None]
-
-    votes(0, 0)
-    vs = votes_scalar(0)
-    vs[0]()
-    vs[1]()
-    db = deaths_steps(0, 0)
-    run(db[:7])
-    vs[2]()
-    for r in range(RO):
-        d1, d2 = deaths_steps(r, 1), deaths_steps(r, 2)
-        if r == 0:
-            votes(r, 2, [db[7:], d1[:4], d1[4:]])
-        else:
-            votes(r, 2, [[lambda: new_weights(r - 1, 0), lambda: table(0, 8, 13)], d1[:4], d1[4:]])
-            place_border(r)
-            table(0, 13, 16)
-            new_weights(r - 1, 1, which=(0,))
-            high_names(1)
-        run(d2[:4])
-        if r:
-            keep_table()
-            table(1, 0, 16)
-            new_weights(r - 1, 1, "vvv", which=(2,))
-        d2[4]()
-        before_gone(r)
-        if r:
-            mark_inner()
-            new_weights(r - 1, 1, which=(1,))
-        gone(r)
-        splice(r)
-        heights(r)
-        run(choose_steps(r, 0))
+    def choose(r, j):
+        c0, c1, n = EX[j]
+        a, b, k, h = 7 * c0, 7 * c0 + n, "abc"[j], str(min(j, 1))
+        pk, bk = KEY[min(j, 1)]
+        for t in range(3):
+            rb, qb = "RB%d%s" % (t, k), "QB%d%s" % (t, k)
+            scan(T.RB[:, t, a:b], T.RST[:, a:b], pk[:, a:b], 0.0, A.add, A.min, ["RST", "kq" + k, "key" + h], [rb], [bk])
+            tt(T.nq[:, a:b], T.RB[:, t, a:b], pk[:, a:b], A.not_equal, [rb, "kq" + k, "key" + h], ["nq" + k], [bk])
+            scan(T.QB[:, t, a:b], T.dn[:, a:b], T.nq[:, a:b], 0.0, A.add, A.mult, ["dn" + h, "nq" + k], [qb])
+            if t < 2:
+                tt(T.kp[:, a:b], ind(T.QB[:, t, a:b + 8 * (j == 2)], T.BL[:, 0:n // 16]), T.n7[:, 1 + a:1 + b], A.not_equal,
+                   [qb, "n7" + h, "BL"], ["pen" + k])
+                tt(pk[:, a:b], pk[:, a:b], T.kp[:, a:b], A.mult, ["kq" + k, "key" + h, "pen" + k], ["kq" + k], [bk])
+        rb, qb = ["RB%d%s" % (t, k) for t in range(3)], ["QB%d%s" % (t, k) for t in range(3)]
+        tt(T.NF[:, :, c0:c1], T.QB[:, :, a + 6:7 * c1:7], T.OS[:, :, c0:c1], A.add, qb + ["OS" + h], ["NF" + k])
+        tt(T.Ki[:, :, c0:c1], T.NH[:, :, c0:c1], T.RB[:, :, a + 6:7 * c1:7], A.subtract, rb + ["NH" + h], ["Ki" + k])
+        ts(T.xi[:, :, c0:c1], T.Ki[:, :, c0:c1], 2047, None, A.bitwise_and, None, ["Ki" + k], ["xi" + k])
+        ts(T.EU[:, :, c0:c1], T.xi[:, :, c0:c1], 16.0, pm, A.mult, A.add, ["xi" + k, "PF"], ["EU" + k])
         if r + 1 < RO:
-            border_weights(r)
-            votes(r + 1, 0)
-            db = deaths_steps(r + 1, 0)
-            vs = votes_scalar(r + 1)
-            run(choose_steps(r, 1),
-                [vs[0], lambda: (high_names(0), table(0, 0, 3))] + db[:4] + [lambda: table(0, 3, 5), db[5], db[6], db[7], db[8]],
-                nop * 6 + [vs[1]] + nop * 3 + [vs[2], lambda: table(0, 5, 8)])
-        else:
-            new_weights(r, 0)
-            run(choose_steps(r, 1))
-            new_weights(r, 1, "svv")
-            ts(T.NA[:], T.NF[:], 1 / SC, None, A.mult, None, ["NF0", "NF1"], ["NA"])
-            ac(T.q128[:], T.NA[:], I, ["NA"], ["q128"], bias=192.0 - (UB + 79.5) / B, scale=1.0 / B)
-            ac(T.fa[:], T.q128[:], I, ["q128"], ["fa"], bias=-192.0 * 864 - UB - 1024.0 * rk, scale=864.0)
-            ts(T.fb[:], T.NA[:], float(UB), None, A.is_ge, None, ["NA"], ["fb"])
-            ts(T.NA[:], T.NA[:], 1024.0 * rk, None, A.add, None, ["NA", "q128"], ["NA"])
-            tt(T.fa[:], T.fa[:], T.fb[:], A.mult, ["fa", "fb"], ["fa"])
-            tt(T.YN[:], T.fa[:], T.NA[:], A.add, ["fa", "NA"], ["YN"])
-            dma("y", "dout", [(T.yn[:], T.YN[:])], ["YN"], [])
-    for k, n in cnt.items():
-        g.wait_ge(T.sem[k], n)
+            ts(T.NU[:, :, c0:c1], T.NF[:, :, c0:c1], 1 / SC, None, A.mult, None, ["NF" + k], ["NU" + k])
+            tt(T.RF[:, :, c0:c1], T.QB[:, :, a + 6:7 * c1:7], T.ON[:, :, c0:c1], A.add, qb + ["ON" + h], ["RF" + k])
+            ts(T.EM[:, :, c0:c1], T.RF[:, :, c0:c1], 0.0, 16.0, A.is_equal, A.mult, ["RF" + k], ["EM" + k])
+
+    def new_weights(r, c0, c1, eng):
+        R = ["z", "zc0", "zc1", "zc2"] + ["cw%d%d" % (l, h) for l in range(3) for h in range(2)] + [t for q in range(r + 1) for t in wall(q)]
+        for t in range(3):
+            if r + 1 == RO:
+                o, w = T.WF[:, t * V + 16 * c0:t * V + 16 * c1], "yw%d%d" % (t, c0)
+            elif c0 == 0:
+                o, w = wblk(r + 1, t, ub, ub + B), "wb%d%d" % (r + 1, t)
+            else:
+                o, w = wblk(r + 1, t, 16 * c0, 16 * c1), "w%d_%d%d" % (r + 1, c0 // 32, t)
+            gather(eng[t], o, BG[:, 0:unit(r, 0) * U + V], T.EU[:, t, c0:c1], R + tok("EU", c0, c1), [w])
+            if r + 1 == RO:
+                dma("y", "dout", [(T.yw[:, t * V + 16 * c0:t * V + 16 * c1], o)], [w], [])
+            elif c0 == 0:
+                ac(wblk(r + 1, t, 0, B), o, Cp, [w], ["w%d_2%d" % (r + 1, t)])
+
+    for r in range(RO):
+        if r == 0:
+            name_table()
+        for k in range(3):
+            votes(r, k)
+            deaths(r, k)
+        if r:
+            name_table()
+        before_gone(r)
+        gone(r, 0)
+        gone(r, 1)
+        marks(r)
+        if r + 1 < RO:
+            border_heights(r)
+        splice(r, 0)
+        splice(r, 1)
+        heights(r)
+        for j in range(3):
+            choose(r, j)
+        if r + 1 < RO:
+            new_weights(r, 0, 10, "sss")
+            hand_over(r + 1)
+            new_weights(r, 10, 32, "sss")
+            new_weights(r, 32, 56, "sss")
+    for (c0, c1, _), eng in zip(EX, LE):
+        new_weights(RO - 1, c0, c1, eng)
+    ts(T.NA[:], T.NF[:], 1 / SC, None, A.mult, None, tok("NF"), ["NA"])
+    ac(T.q128[:], T.NA[:], I, ["NA"], ["q128"], bias=192.0 - (UB + 79.5) / B, scale=1.0 / B)
+    ac(T.fa[:], T.q128[:], I, ["q128"], ["fa"], bias=-192.0 * 864 - UB - 1024.0 * rk, scale=864.0)
+    ts(T.fb[:], T.NA[:], float(UB), None, A.is_ge, None, ["NA"], ["fb"])
+    ts(T.NB[:], T.NA[:], 1024.0 * rk, None, A.add, None, ["NA"], ["NB"])
+    tt(T.fa[:], T.fa[:], T.fb[:], A.mult, ["fa", "fb"], ["fa"])
+    tt(T.YN[:], T.fa[:], T.NB[:], A.add, ["fa", "NB"], ["YN"])
+    dma("y", "dout", [(T.yn[:], T.YN[:])], ["YN"], [])
+    issue()

@@ -17,8 +17,10 @@ CUT = [[(0, 256)], [(256, 512), (512, V)]]
 WIDE = [112, 400]
 EX = [(0, 16, 112), (16, 32, 112), (32, 56, 176)]
 HS = [(0, 512), (512, V)]
-GE, WE, LE = ("svv", "vsv"), "vv", ("sss", "svs", "vsv")
-CY, WAKE, FLIGHT = 0.83e-3, 0.2, 6.5
+GE = [[(0, 0, 16, "s"), (1, 0, 16, "v"), (2, 0, 16, "v")],
+      [(0, 16, 56, "v"), (1, 16, 56, "s"), (2, 16, 36, "s"), (2, 36, 56, "v")]]
+LE = ("sss", "sss", "vsv")
+CY, WAKE, FLIGHT = 0.83e-3, 0.2, 5.5
 PLAN = []
 
 bf, f2, f4, i4, u2 = "bfloat16", "float16", "float32", "int32", "uint16"
@@ -41,8 +43,8 @@ SCRATCH = {
     "Fg": _s([V], bf), "hr": _s([V], bf), "hy": _s([V], bf), "hyb": _s([B], bf), "P1": _s([400], bf), "P2": _s([400], bf),
     "n7": _s([408], f4), "dn": _s([400], f4), "RB": _s([3, 400], f4), "QB": _s([3, 408], f4), "nq": _s([400], bf),
     "kp": _s([400], bf), "Ki": _s([3, 56], i4), "xi": _s([3, 56], i4), "EU": _s([3, 56], u2), "KS": _s([3, 56], f4),
-    "KP": _s([3, 56], f4), "E": _s([128, 16], bf), "E2": _s([2, 384], f4), "WF": _s([2688], bf), "HO": _s([V], bf),
-    "NA": _s([168], f4), "NB": _s([168], f4), "YN": _s([168], f4), "q128": _s([168], bf),
+    "KP": _s([3, 56], f4), "E": _s([128, 16], bf), "E2": _s([384], f4), "E3": _s([384], f2), "P0": _s([400], bf), "WF": _s([2688], bf), "HO": _s([V], bf),
+    "NB": _s([168], f4), "YN": _s([168], f4), "q128": _s([168], bf),
     "PI": _s([2], i4), "PF": _s([16], f4), "J": _s([144], f4), "JG": _s([128], f4), "QS": _s([144], bf),
     "QK": _s([144], bf), "QH": _s([144], bf), "FM": _s([144], bf), "QF": _s([24], bf), "PT": _s([16, 144], bf),
     "OH": _s([16], f4), "O3": _s([6], f4), "ID": _s([128], bf), "NI": _s([128], bf), "HI": _s([128], bf),
@@ -227,7 +229,10 @@ def rank_program(g, core, T, topo):
         def fn(s):
             for o, i in pairs:
                 Q[e].dma_start(o, i).then_inc(T.sem[s], 16)
-        call(e, fn, 0.05 * len(pairs), R, W, late=2.0 + len(pairs), sem=(sem, 16 * len(pairs)))
+        if W:
+            call(e, fn, 0.05 * len(pairs), R, W, late=2.0 + len(pairs), sem=(sem, 16 * len(pairs)))
+        else:
+            call(e, fn, 0.35, R, W, late=2.0, sem=(sem, 16))
 
     peers = peers_of(core, T)
     mask, ne = common_mask(core, peers, topo)
@@ -305,6 +310,7 @@ def rank_program(g, core, T, topo):
     PT = ["PT%d" % i for i in range(16)]
     T7 = ["T7%d" % c for c in range(3)]
     ET = ["E%d" % l for l in range(6)]
+    GT = [["G%d%d" % (h, j) for j in range(len(GE[h]))] for h in range(2)]
     SF = ["SFa", "SFb"]
 
     def tok(name, c0=0, c1=56):
@@ -471,9 +477,9 @@ def rank_program(g, core, T, topo):
         a, b = PS[h]
         c0, c1, k = a // 16, b // 16, str(h)
         dwt = ["dw%d%d" % (r, j) for j in range(3)] + ["dwf%d" % r, "dwz%d" % r] + tok("NU", c0, c1)
-        gt = ["G%d%d" % (h, l) for l in range(3)]
-        for l in range(3):
-            gather(GE[h][l], gs(l, a, b), DW[r][:], T.NU[:, l, c0:c1], dwt, [gt[l]])
+        gt = GT[h]
+        for (l, e, f, eng), t in zip(GE[h], gt):
+            gather(eng, gs(l, 16 * e, 16 * f), DW[r][:], T.NU[:, l, e:f], dwt, [t])
         if h == 0:
             pc = T.pV[:, 176:176 + B]
             mms([(pc, T.ID[:], T.TB[:, 0:B], True, False), (pc, T.S6[:], T.mk[:], False, False)], ["ID", "S6", "TB", "mk"], ["pV"], ["pV"])
@@ -493,15 +499,14 @@ def rank_program(g, core, T, topo):
         ts(T.nh[:, 0, c0:c1], T.m[:, 1, c0:c1], 0.0, None, A.is_le, None, ["m" + k], ["nh" + k])
         for t in (1, 2):
             ac(T.nh[:, t, c0:c1], T.nh[:, 0, c0:c1], Cp, ["nh" + k], ["nh%d%s" % (t, k)])
-        gather(WE[h], T.ws[:, a:b], BG[:, W0:unit(r, 0) * U + V], T.WU[:, c0:c1],
+        gather("s", T.ws[:, a:b], BG[:, W0:unit(r, 0) * U + V], T.WU[:, c0:c1],
                ["zc0", "WU" + k] + [t for q in range(r + 1) for t in wall(q)], ["ws" + k])
 
     def marks(r):
         mms([(pT[0][:], T.ID[:], T.TB[:], True, False)] +
             [(pT[0][:, a:b], sel(T.FM, 6 + l), gs(l, a, b), False, a > 0 and l == 2) for a, b in (CUT[0][0], CUT[1][0]) for l in range(3)],
-            ["FM", "ID", "TB"] + ["G%d%d" % (h, l) for h in range(2) for l in range(3)], ["pT0"], ["pT0"])
-        mms([(pT[1][:, 0:384], sel(T.FM, 6 + l), gs(l, 512, V), False, l == 2) for l in range(3)],
-            ["FM", "G10", "G11", "G12"], ["pT1"], ["pT1"])
+            ["FM", "ID", "TB"] + GT[0] + GT[1], ["pT0"], ["pT0"])
+        mms([(pT[1][:, 0:384], sel(T.FM, 6 + l), gs(l, 512, V), False, l == 2) for l in range(3)], ["FM"] + GT[1], ["pT1"], ["pT1"])
         ac(TT[r][:, ub:ub + B], pT[0][:, 0:B], Cp, ["pT0"], ["tb%d" % r], ["pT0"])
         ac(TT[r][:, B:512], pT[0][:, B:512], Cp, ["pT0"], ["TT0"], ["pT0"])
         ac(TT[r][:, 512:V], pT[1][:, 0:384], Cp, ["pT1"], ["TT1"], ["pT1"])
@@ -509,7 +514,8 @@ def rank_program(g, core, T, topo):
     def border_heights(r):
         pb = T.pA[:, 352:512]
         mms([(pb, T.ID[:], T.ws[:, 0:B], True, False), (pb, T.NI[:], hown(r, 0, B), False, True)], ["ID", "NI", "ws0", "h%d0" % r], ["pb"], ["pA"])
-        ts(T.hyb[:], pb, 0.0, 255.6, A.max, A.add, ["pb"], ["hyb"], ["pA"])
+        ac(T.hyb[:], pb, Re, ["pb"], ["hyb"], ["pA"])
+        ac(T.hyb[:], T.hyb[:], I, ["hyb"], ["hyb"], bias=255.6)
         mms([(pb, T.ID[:], hown(r, 0, B), True, False), (pb, T.HI[:], T.hyb[:], False, True)], ["ID", "HI", "hyb", "h%d0" % r], ["pb"], ["pA"])
         ac(HW[r + 1][:, ub:ub + B], pb, I, ["pb"], ["hb%d" % (r + 1)], ["pA"], bias=-128.0)
         send(HW[r + 1][:, ub:ub + B], "mh%d" % (r + 1), ["hb%d" % (r + 1)], "hf%d" % (r + 1))
@@ -531,7 +537,8 @@ def rank_program(g, core, T, topo):
             [(col(pk, c), T.IB[:], T.nh[:, 0, c0:c1], False, False) for c in range(6)], ["IB", "nh" + k, "gm" + k], ["key" + k], [bk])
         tt(T.ON[:, :, c0:c1], T.RF[:, :, c0:c1], T.nh[:, :, c0:c1], A.mult, tok("RF", c0, c1) + nh, ["ON" + k])
         tt(T.NH[:, :, c0:c1], T.KP[:, :, c0:c1], T.nh[:, :, c0:c1], A.mult, ["KP0", "KP1", "KP2"] + nh, ["NH" + k])
-        tt(T.OS[:, :, c0:c1], T.ON[:, :, c0:c1], T.SF[:, :, c0:c1], A.add, ["ON" + k] + SF, ["OS" + k])
+        if h == 0:
+            tt(T.OS[:, :, c0:c1], T.ON[:, :, c0:c1], T.SF[:, :, c0:c1], A.add, ["ON" + k] + SF, ["OS" + k])
         tt(T.tt[:, a:b], ind(HW[r][:], od), T.ws[:, a:b], A.subtract, hall(r) + ou + ["ws" + k], ["tt" + k])
         ac(T.wd2[:, a:b], ind(wblk(r, 2, 0, X), od), Cp, wall(r) + ou, ["wd2" + k])
         for e, f in CUT[h]:
@@ -551,15 +558,24 @@ def rank_program(g, core, T, topo):
                 ["QK", t], ["key" + k], [bk])
         ac(T.Fg[:, a:b], ind(TT[r][:], od), Cp, ["TT0", "TT1", "tb%d" % r, "tf%d" % r, "ttz%d" % r] + ou, ["Fg" + k])
         mms([(pT[0][0:n, i:384:16], T.Fg[:, a + i:b:16], T.QF[:], True, True) for i in range(16)], ["QF0", "QF1", "QF2", "Fg" + k], ["pT0"], ["pT0"])
-        ac(T.E2[0:n, h], pT[0][0:n, 0:384], Cp, ["pT0"], ["E2" + k], ["pT0"])
+        e2, i2 = (T.E2[0:n, :], T.I4) if h else (T.E3[0:n, :], T.ID)
+        if h:
+            ac(e2, pT[0][0:n, 0:384], Cp, ["pT0"], ["E2" + k], ["pT0"])
+        else:
+            cp(e2, pT[0][0:n, 0:384], ["pT0"], ["E2" + k], ["pT0"])
         mms([(pn[:, x:y], T.NI[:], T.S7[:, x:y], True, False)] + [(col(pn, c), T.ID[:], T.RF[:, c, c0:c1], False, False) for c in range(3)],
             ["ID", "NI", "S70", "S71", "S72"] + tok("RF", c0, c1), ["nam" + k], [bn])
-        mms([(col(pn, 3 + l), T.E2[0:n, h, 128 * l:128 * (l + 1)], T.I4[0:n, 0:n], False, l == 2) for l in range(3)],
+        mms([(col(pn, 3 + l), e2[:, 128 * l:128 * (l + 1)], i2[0:n, 0:n], False, l == 2) for l in range(3)],
             ["I4", "E2" + k], ["nam" + k], [bn])
-        ac(T.P2[:, x:y], pn[:, x:y], Re, ["nam" + k], ["P2" + k], [bn], bias=-64.0, scale=256.0)
+        if h:
+            ac(T.P2[:, x:y], pn[:, x:y], Re, ["nam" + k], ["P2" + k], [bn], bias=-64.0, scale=256.0)
+            ac(T.P0[:, x:y], pn[:, x:y], F.Abs, ["nam" + k], ["P0"], [bn])
+            ac(T.P1[:, x:y], T.P0[:, x:y], Re, ["P0"], ["P1" + k], bias=1.0, scale=-2 / SC)
+        else:
+            ts(T.P1[:, x:y], pn[:, x:y], 0.0, None, A.is_equal, None, ["nam" + k], ["P1" + k], [bn])
+            ts(T.P2[:, x:y], pn[:, x:y], 0.25, None, A.is_gt, None, ["nam" + k], ["P2" + k], [bn])
         ac(T.n7[:, 1 + x:1 + y], pn[:, x:y], Cp, ["nam" + k], ["n7" + k], [bn])
         ac(T.n7[:, x + 7:y + 1:7], T.RST[:, x + 1:y - 5:7], I, ["RST"], ["n7" + k], bias=4.0)
-        ts(T.P1[:, x:y], pn[:, x:y], 0.0, None, A.is_equal, None, ["nam" + k], ["P1" + k], [bn])
         mms([(pk[:, x:y], T.IB[:], q[:, x:y], False, j == 1) for j, q in enumerate((T.P2, T.P1))], ["IB", "P1" + k, "P2" + k], ["key" + k], [bk])
         tt(T.dn[:, x:y], T.n7[:, x:y], pn[:, x:y], A.subtract, ["n70", "n7" + k, "nam" + k], ["dn" + k], [bn])
 
@@ -593,13 +609,17 @@ def rank_program(g, core, T, topo):
                    [qb, "n7" + h, "BL"], ["pen" + k])
                 tt(pk[:, a:b], pk[:, a:b], T.kp[:, a:b], A.mult, ["kq" + k, "key" + h, "pen" + k], ["kq" + k], [bk])
         rb, qb = ["RB%d%s" % (t, k) for t in range(3)], ["QB%d%s" % (t, k) for t in range(3)]
-        tt(T.NF[:, :, c0:c1], T.QB[:, :, a + 6:7 * c1:7], T.OS[:, :, c0:c1], A.add, qb + ["OS" + h], ["NF" + k])
+        if j or r + 1 < RO:
+            tt(T.RF[:, :, c0:c1], T.QB[:, :, a + 6:7 * c1:7], T.ON[:, :, c0:c1], A.add, qb + ["ON" + h], ["RF" + k])
+        if j:
+            tt(T.NF[:, :, c0:c1], T.RF[:, :, c0:c1], T.SF[:, :, c0:c1], A.add, ["RF" + k] + SF, ["NF" + k])
+        else:
+            tt(T.NF[:, :, c0:c1], T.QB[:, :, a + 6:7 * c1:7], T.OS[:, :, c0:c1], A.add, qb + ["OS" + h], ["NF" + k])
         tt(T.Ki[:, :, c0:c1], T.NH[:, :, c0:c1], T.RB[:, :, a + 6:7 * c1:7], A.subtract, rb + ["NH" + h], ["Ki" + k])
         ts(T.xi[:, :, c0:c1], T.Ki[:, :, c0:c1], 2047, None, A.bitwise_and, None, ["Ki" + k], ["xi" + k])
         ts(T.EU[:, :, c0:c1], T.xi[:, :, c0:c1], 16.0, pm, A.mult, A.add, ["xi" + k, "PF"], ["EU" + k])
         if r + 1 < RO:
             ts(T.NU[:, :, c0:c1], T.NF[:, :, c0:c1], 1 / SC, None, A.mult, None, ["NF" + k], ["NU" + k])
-            tt(T.RF[:, :, c0:c1], T.QB[:, :, a + 6:7 * c1:7], T.ON[:, :, c0:c1], A.add, qb + ["ON" + h], ["RF" + k])
             ts(T.EM[:, :, c0:c1], T.RF[:, :, c0:c1], 0.0, 16.0, A.is_equal, A.mult, ["RF" + k], ["EM" + k])
 
     def new_weights(r, c0, c1, eng):
@@ -643,11 +663,10 @@ def rank_program(g, core, T, topo):
             new_weights(r, 32, 56, "sss")
     for (c0, c1, _), eng in zip(EX, LE):
         new_weights(RO - 1, c0, c1, eng)
-    ts(T.NA[:], T.NF[:], 1 / SC, None, A.mult, None, tok("NF"), ["NA"])
-    ac(T.q128[:], T.NA[:], I, ["NA"], ["q128"], bias=192.0 - (UB + 79.5) / B, scale=1.0 / B)
-    ac(T.fa[:], T.q128[:], I, ["q128"], ["fa"], bias=-192.0 * 864 - UB - 1024.0 * rk, scale=864.0)
-    ts(T.fb[:], T.NA[:], float(UB), None, A.is_ge, None, ["NA"], ["fb"])
-    ts(T.NB[:], T.NA[:], 1024.0 * rk, None, A.add, None, ["NA"], ["NB"])
+    ts(T.q128[:], T.NF[:], 1 / (SC * B), 192.0 - (UB + 79.5) / B, A.mult, A.add, tok("NF"), ["q128"])
+    ts(T.fb[:], T.NF[:], UB * SC, None, A.is_ge, None, tok("NF"), ["fb"])
+    ts(T.NB[:], T.NF[:], 1 / SC, 1024.0 * rk, A.mult, A.add, tok("NF"), ["NB"])
+    ts(T.fa[:], T.q128[:], 864.0, -192.0 * 864 - UB - 1024.0 * rk, A.mult, A.add, ["q128"], ["fa"])
     tt(T.fa[:], T.fa[:], T.fb[:], A.mult, ["fa", "fb"], ["fa"])
     tt(T.YN[:], T.fa[:], T.NB[:], A.add, ["fa", "NB"], ["YN"])
     dma("y", "dout", [(T.yn[:], T.YN[:])], ["YN"], [])

@@ -12,15 +12,13 @@ GF = 8192.0
 SC = 2.0 ** -13
 BIG = 2.0 ** 23
 CH = [(0, 10), (10, 32), (32, 56)]
+EX = [(0, 16), (16, 32), (32, 56)]
 PS = [(0, 256), (256, V)]
-CUT = [[(0, 256)], [(256, 512), (512, V)]]
-WIDE = [112, 400]
-EX = [(0, 16, 112), (16, 32, 112), (32, 56, 176)]
 HS = [(0, 512), (512, V)]
 GE = [[(0, 0, 16, "s"), (1, 0, 16, "v"), (2, 0, 16, "v")],
       [(0, 16, 56, "v"), (1, 16, 56, "s"), (2, 16, 36, "s"), (2, 36, 56, "v")]]
-LE = ("sss", "sss", "vsv")
-CY, WAKE, FLIGHT = 0.83e-3, 0.2, 5.5
+LE = (("sss", 3.0), ("sss", 2.0), ("svs", 0.0))
+CY, WAKE, FLIGHT = 0.83e-3, 0.2, 5.0
 PLAN = []
 
 bf, f2, f4, i4, u2 = "bfloat16", "float16", "float32", "int32", "uint16"
@@ -37,18 +35,18 @@ SCRATCH = {
     "EM": _s([3, 56], bf), "PN": _s([3, 56], f4), "VA": _s([56], f4), "PA": _s([3, 56], f4), "AB": _s([2, 3, 56], f4),
     "m1": _s([2, 56], f4), "m": _s([2, 56], i4), "oi": _s([56], i4), "OU": _s([56], u2), "WU": _s([56], u2),
     "nh": _s([3, 56], bf), "NH": _s([3, 56], f4), "gm": _s([3, 56], bf), "DA": _s([56], bf), "cmp": _s([2688], bf),
-    "gI": _s([1056], bf), "ok": _s([176], bf), "d01": _s([56], bf), "die": _s([56], bf), "dieB": _s([16], bf),
+    "gI": _s([1152], bf), "ok": _s([176], bf), "d01": _s([56], bf), "die": _s([56], bf), "dieB": _s([16], bf),
     "cs": _s([16], bf), "G": _s([2688], bf), "TB": _s([512], bf), "H8": _s([3, 56], bf), "mk": _s([B], bf),
     "LS": _s([RO, B], bf), "ws": _s([V], bf), "tt": _s([V], bf), "wd2": _s([V], bf), "wr2": _s([V], bf),
     "Fg": _s([V], bf), "hr": _s([V], bf), "hy": _s([V], bf), "hyb": _s([B], bf), "P1": _s([400], bf), "P2": _s([400], bf),
-    "n7": _s([408], f4), "dn": _s([400], f4), "RB": _s([3, 400], f4), "QB": _s([3, 408], f4), "nq": _s([400], bf),
-    "kp": _s([400], bf), "Ki": _s([3, 56], i4), "xi": _s([3, 56], i4), "EU": _s([3, 56], u2), "KS": _s([3, 56], f4),
+    "n7": _s([2, 408], f4), "dn": _s([400], f4), "RB": _s([3, 400], f4), "QB": _s([4, 3, 184], f4), "nq": _s([400], bf),
+    "kp": _s([4, 176], bf), "Ki": _s([3, 56], i4), "xi": _s([3, 56], i4), "EU": _s([3, 56], u2), "KS": _s([3, 56], f4),
     "KP": _s([3, 56], f4), "E": _s([128, 16], bf), "E2": _s([384], f4), "E3": _s([384], f2), "P0": _s([400], bf), "WF": _s([2688], bf), "HO": _s([V], bf),
     "NB": _s([168], f4), "YN": _s([168], f4), "q128": _s([168], bf),
     "PI": _s([2], i4), "PF": _s([16], f4), "J": _s([144], f4), "JG": _s([128], f4), "QS": _s([144], bf),
     "QK": _s([144], bf), "QH": _s([144], bf), "FM": _s([144], bf), "QF": _s([24], bf), "PT": _s([16, 144], bf),
     "OH": _s([16], f4), "O3": _s([6], f4), "ID": _s([128], bf), "NI": _s([128], bf), "HI": _s([128], bf),
-    "IB": _s([128], bf), "N4": _s([128], f4), "I4": _s([40], f4), "S6": _s([128], bf), "I8": _s([128], bf),
+    "IB": _s([128], bf), "N4": _s([128], f4), "I4": _s([48], f4), "S6": _s([128], bf), "I8": _s([128], bf),
     "N8": _s([128], bf), "ONE": _s([128], bf), "TRI": _s([128], bf), "tri0": _s([128], bf), "tri1": _s([128], bf),
     "c16": _s([56], f4), "VW": _s([56], f4), "SF": _s([3, 56], f2), "T7": _s([406], bf), "S7": _s([400], f2),
     "RST": _s([400], f4), "BL": _s([14], u2), "bli": _s([14], i4), "o16": _s([16], bf), "m56": _s([56], bf),
@@ -120,6 +118,14 @@ def rank_program(g, core, T, topo):
     Q = {"v": g.vector, "s": g.scalar, "t": g.tensor, "g": g, "y": g.sync}
     calls, wr, rd, bank, gathers = [], {}, {}, {}, []
 
+    seen = {}
+
+    def kind(e, t):
+        for p in ("dw", "hb", "wb", "ls", "tb", "hf", "tf", "wf", "dwf", "h", "w"):
+            if t.startswith(p) and t[len(p):len(p) + 1].isdigit():
+                t = p + t[len(p) + 1:]
+        return seen.setdefault(e + t, len(seen))
+
     def call(e, fn, hold, R, W, Bk=(), late=WAKE, sem=None):
         k = len(calls)
         dep = {wr[t] for t in list(R) + list(W) if t in wr}
@@ -129,13 +135,13 @@ def rank_program(g, core, T, topo):
             who, now, before = bank.get(b, (e, [], []))
             if who != e:
                 now, before = [], now
-            dep.update(before + (now[-1:] if e == "t" else []))
+            dep.update(before + (now[-1:] if e == "t" and W else []))
             bank[b] = (e, now + [k], before)
         for t in R:
             rd.setdefault(t, []).append(k)
         for t in W:
             wr[t], rd[t] = k, []
-        calls.append({"e": e, "fn": fn, "hold": hold, "late": late, "dep": dep, "sem": sem})
+        calls.append({"e": e, "fn": fn, "hold": hold, "late": late, "dep": dep, "sem": sem, "kind": kind(e, (list(W) or list(R))[-1])})
         return k
 
     def issue():
@@ -149,10 +155,10 @@ def rank_program(g, core, T, topo):
         def gap(d, k):
             return 0.0 if calls[d]["e"] == calls[k]["e"] == "t" else calls[d]["late"]
 
-        def place(order, links, back):
+        def place(order):
             end, busy = [0.0] * n, {e: [] for e in "vstgyx"}
             for k in order:
-                t = max([calls[k]["late"] if back else 0.0] + [end[d] + (gap(k, d) if back else gap(d, k)) for d in links[k]])
+                t = max([0.0] + [end[d] + gap(d, k) for d in before[k]])
                 h, line = calls[k]["hold"], busy[calls[k]["e"]]
                 i = len(line)
                 while i and line[i - 1][1] > t:
@@ -164,16 +170,24 @@ def rank_program(g, core, T, topo):
                 end[k] = t + h
             return end
         if not PLAN:
+            best, seed, bias = None, 1, [0.0] * len(seen)
             way = [0.0] * n
             for k in range(n - 1, -1, -1):
                 way[k] = calls[k]["hold"] + max([calls[k]["late"]] + [way[j] + gap(k, j) for j in after[k]])
-            best = None
-            for _ in range(3):
-                end = place(sorted(range(n), key=lambda k: (-way[k], k)), before, False)
+            for turn in range(1500):
+                trial = list(bias)
+                for _ in range(2 if turn else 0):
+                    seed = (seed * 1103515245 + 12345) % 2 ** 31
+                    j = (seed >> 8) % len(seen)
+                    seed = (seed * 1103515245 + 12345) % 2 ** 31
+                    trial[j] += 1.0 * (2 * seed / 2 ** 31 - 1)
+                pr = [0.0] * n
+                for k in range(n - 1, -1, -1):
+                    pr[k] = max([way[k] + trial[calls[k]["kind"]]] + [pr[j] + 1e-3 for j in after[k]])
+                end = place(sorted(range(n), key=lambda k: (-pr[k], k)))
                 span = max(end[k] + calls[k]["late"] for k in range(n))
-                if best is None or span < best[0]:
-                    best = (span, end)
-                way = place(sorted(range(n), key=lambda k: (-end[k], -k)), after, True)
+                if best is None or span <= best[0]:
+                    best, bias = (span, end), trial
             PLAN.extend(sorted(range(n), key=lambda k: (best[1][k] - calls[k]["hold"], k)))
         cnt, waited = {}, {e: {} for e in Q}
         for k in PLAN:
@@ -223,16 +237,16 @@ def rank_program(g, core, T, topo):
             for a in lst[:-1]:
                 g.tensor.matmul(*a)
             g.tensor.matmul(*lst[-1]).then_inc(T.sem[s], 1)
-        call("t", fn, sum(CY / 2 * max(64, size(a[0])) * (4 if "32" in str(a[1].dtype) else 1) for a in lst), R, W, Bk)
+        call("t", fn, sum(CY / 1.8 * max(64, size(a[0])) * (4 if "32" in str(a[1].dtype) else 1) for a in lst), R, W, Bk)
 
-    def dma(e, sem, pairs, R, W):
+    def dma(e, sem, pairs, R, W, early=0.0):
         def fn(s):
             for o, i in pairs:
                 Q[e].dma_start(o, i).then_inc(T.sem[s], 16)
         if W:
             call(e, fn, 0.05 * len(pairs), R, W, late=2.0 + len(pairs), sem=(sem, 16 * len(pairs)))
         else:
-            call(e, fn, 0.35, R, W, late=2.0, sem=(sem, 16))
+            call(e, fn, 0.35, R, W, late=2.0 + early, sem=(sem, 16))
 
     peers = peers_of(core, T)
     mask, ne = common_mask(core, peers, topo)
@@ -280,6 +294,9 @@ def rank_program(g, core, T, topo):
         op("g", (lambda: g.iota(o, pat, base, cm, allow_small_or_imprecise_dtypes=True)) if fl else
            (lambda: g.iota(o, pat, base, cm)), o, o, 3, [], W)
 
+    def copy(o, i, n, R, W):
+        call("g", lambda s: g.affine_select(o, i, [[0, n]], A.is_equal, 0.0, 0, 0).then_inc(T.sem[s], 1), 0.17 + 2 * CY * n, R, W)
+
     BG = T.BG
     HW = [T["HW%d" % r] for r in range(RO)]
     DW = [T["DW%d" % r] for r in range(RO)]
@@ -314,7 +331,7 @@ def rank_program(g, core, T, topo):
     SF = ["SFa", "SFb"]
 
     def tok(name, c0=0, c1=56):
-        return [name + k for k, (a, b, _) in zip("abc", EX) if a < c1 and c0 < b]
+        return [name + k for k, (a, b) in zip("abc", EX) if a < c1 and c0 < b]
 
     def wown(r):
         return ["w%d_%d%d" % (r, h, c) for h in range(3) for c in range(3)]
@@ -370,7 +387,7 @@ def rank_program(g, core, T, topo):
         ts(T.SF[:, l, 10:56], T.VW[:, 10:56], SC, None, A.mult, None, ["VW"], ["SFb"])
     for t, k in (("NI", -1.0), ("I8", 1 / 256.0), ("N8", -1 / 256.0), ("IB", BIG), ("N4", -1.0), ("HI", 0.5)):
         ac(T[t][:], T.ID[:], I, ["ID"], [t], scale=k)
-    ac(T.I4[:], T.ID[:, 0:40], Cp, ["ID"], ["I4"])
+    ac(T.I4[:], T.ID[:, 0:48], Cp, ["ID"], ["I4"])
     ac(T.QH[:], T.QS[:], I, ["QS"], ["QH"], scale=0.5)
     ac(T.QK[:], T.QS[:], I, ["QS"], ["QK"], scale=-2048.0)
     for i in range(16):
@@ -406,9 +423,12 @@ def rank_program(g, core, T, topo):
     ts(T.BL[:], T.bli[:], 7.0, 6.0, A.mult, A.add, ["bli"], ["BL"])
     ms(T.RST[:], 0.0, ["RST"])
     ms(T.RST[:, 0:400:7], 4 * BIG, ["RST"])
-    ms(T.n7[:, 0:8], 4.0, ["n70"])
+    ms(T.n7[:, 0, 0:8], 4.0, ["n70"])
+    ms(T.n7[:, 1, 112:120], 4.0, ["n71"])
+    ms(T.n7[:, 1, 392:408], 4.0, ["n71"])
     ms(T.m56[:], -1.0, ["m56"])
-    ms(T.QB[:, :, 400:408], 0.0, ["QB0c", "QB1c", "QB2c"])
+    for j, u in enumerate("abcd"):
+        ms(T.QB[:, j, 0:2, 64:184], 0.0, ["QB0" + u, "QB1" + u])
     for l in range(3):
         tt(T.O3[:, 1:2], T.OH[:, l:l + 1], T.OH[:, l + 3:l + 4], A.add, ["OH"], ["O31"])
         tt(T.O3[:, 2:3], T.O3[:, 1:2], T.OH[:, l + 6:l + 7], A.add, ["OH", "O31"], ["O32"])
@@ -504,7 +524,7 @@ def rank_program(g, core, T, topo):
 
     def marks(r):
         mms([(pT[0][:], T.ID[:], T.TB[:], True, False)] +
-            [(pT[0][:, a:b], sel(T.FM, 6 + l), gs(l, a, b), False, a > 0 and l == 2) for a, b in (CUT[0][0], CUT[1][0]) for l in range(3)],
+            [(pT[0][:, a:b], sel(T.FM, 6 + l), gs(l, a, b), False, a > 0 and l == 2) for a, b in ((0, 256), (256, 512)) for l in range(3)],
             ["FM", "ID", "TB"] + GT[0] + GT[1], ["pT0"], ["pT0"])
         mms([(pT[1][:, 0:384], sel(T.FM, 6 + l), gs(l, 512, V), False, l == 2) for l in range(3)], ["FM"] + GT[1], ["pT1"], ["pT1"])
         ac(TT[r][:, ub:ub + B], pT[0][:, 0:B], Cp, ["pT0"], ["tb%d" % r], ["pT0"])
@@ -519,11 +539,12 @@ def rank_program(g, core, T, topo):
         mms([(pb, T.ID[:], hown(r, 0, B), True, False), (pb, T.HI[:], T.hyb[:], False, True)], ["ID", "HI", "hyb", "h%d0" % r], ["pb"], ["pA"])
         ac(HW[r + 1][:, ub:ub + B], pb, I, ["pb"], ["hb%d" % (r + 1)], ["pA"], bias=-128.0)
         send(HW[r + 1][:, ub:ub + B], "mh%d" % (r + 1), ["hb%d" % (r + 1)], "hf%d" % (r + 1))
+        copy(T.HO[:, 0:B], HW[r + 1][:, ub:ub + B], B, ["hb%d" % (r + 1)], ["hc0"])
 
     def splice(r, h):
         a, b = PS[h]
         c0, c1, k = a // 16, b // 16, str(h)
-        n, x, y = c1 - c0, 7 * c0, WIDE[h]
+        n, x, y = c1 - c0, 7 * c0, 7 * c1
         od, ou = T.OU[:, c0:c1], ["OU" + k]
         (pk, bk), (pn, bn) = KEY[h], NAME[h]
         nh = ["nh" + k, "nh1" + k, "nh2" + k]
@@ -534,14 +555,16 @@ def rank_program(g, core, T, topo):
             [(col(pk, c), T.N4[:], T.KP[:, c, c0:c1], False, False) for c in range(3)],
             ["NI", "N4", "IB", "m56", "KP0", "KP1", "KP2"] + T7, ["key" + k], [bk])
         mms([(col(pk, c), T.IB[:], T.gm[:, c, c0:c1], False, False) for c in range(3)] +
-            [(col(pk, c), T.IB[:], T.nh[:, 0, c0:c1], False, False) for c in range(6)], ["IB", "nh" + k, "gm" + k], ["key" + k], [bk])
+            [(col(pk, c), T.IB[:], T.nh[:, 0, c0:c1], False, False) for c in range(6)], ["IB", "nh" + k, "gm" + k, "key" + k], [], [bk])
         tt(T.ON[:, :, c0:c1], T.RF[:, :, c0:c1], T.nh[:, :, c0:c1], A.mult, tok("RF", c0, c1) + nh, ["ON" + k])
         tt(T.NH[:, :, c0:c1], T.KP[:, :, c0:c1], T.nh[:, :, c0:c1], A.mult, ["KP0", "KP1", "KP2"] + nh, ["NH" + k])
         if h == 0:
             tt(T.OS[:, :, c0:c1], T.ON[:, :, c0:c1], T.SF[:, :, c0:c1], A.add, ["ON" + k] + SF, ["OS" + k])
         tt(T.tt[:, a:b], ind(HW[r][:], od), T.ws[:, a:b], A.subtract, hall(r) + ou + ["ws" + k], ["tt" + k])
-        ac(T.wd2[:, a:b], ind(wblk(r, 2, 0, X), od), Cp, wall(r) + ou, ["wd2" + k])
-        for e, f in CUT[h]:
+        cut = [(256, 512), (512, V)] if h else []
+        if h:
+            ac(T.wd2[:, a:b], ind(wblk(r, 2, 0, X), od), Cp, wall(r) + ou, ["wd2" + k])
+        for e, f in cut:
             j = e // 512
             ps = pH[j][:, e - 512 * j:f - 512 * j]
             mms([(ps, T.ID[:], T.wd2[:, e:f], True, False), (ps, T.NI[:], T.tt[:, e:f], False, True)],
@@ -549,18 +572,19 @@ def rank_program(g, core, T, topo):
             ac(T.wr2[:, e:f], ps, Re, ["pH%d" % j], ["wr%d" % e], ["pH%d" % j])
         for l in range(3):
             t = "cw%d%s" % (l, k)
-            if l < 2:
+            if l < 2 or not h:
                 tt(cw(l, a, b), ind(wblk(r, l, 0, X), od), T.tt[:, a:b], A.subtract, wall(r) + ou + ["tt" + k], [t])
                 ts(cw(l, a, b), cw(l, a, b), 0.0, 255.0, A.max, A.min, [t], [t])
             else:
-                ts(cw(l, a, b), T.wr2[:, a:b], 255.0, None, A.min, None, ["wr%d" % e for e, f in CUT[h]], [t])
+                ts(cw(l, a, b), T.wr2[:, a:b], 255.0, None, A.min, None, ["wr%d" % e for e, f in cut], [t])
             mms([(col(pk, 3 + l), sel(T.QK, i), BG[:, (3 - l) * U + a + i:(3 - l) * U + b:16], False, False) for i in range(16)],
-                ["QK", t], ["key" + k], [bk])
+                ["QK", t, "key" + k], [], [bk])
         ac(T.Fg[:, a:b], ind(TT[r][:], od), Cp, ["TT0", "TT1", "tb%d" % r, "tf%d" % r, "ttz%d" % r] + ou, ["Fg" + k])
-        mms([(pT[0][0:n, i:384:16], T.Fg[:, a + i:b:16], T.QF[:], True, True) for i in range(16)], ["QF0", "QF1", "QF2", "Fg" + k], ["pT0"], ["pT0"])
+        mms([(pT[h][0:n, i:384:16], T.Fg[:, a + i:b:16], T.QF[:], True, True) for i in range(16)], ["QF0", "QF1", "QF2", "Fg" + k],
+            ["pT" + k], ["pT" + k])
         e2, i2 = (T.E2[0:n, :], T.I4) if h else (T.E3[0:n, :], T.ID)
         if h:
-            ac(e2, pT[0][0:n, 0:384], Cp, ["pT0"], ["E2" + k], ["pT0"])
+            ac(e2, pT[1][0:n, 0:384], Cp, ["pT1"], ["E2" + k], ["pT1"])
         else:
             cp(e2, pT[0][0:n, 0:384], ["pT0"], ["E2" + k], ["pT0"])
         mms([(pn[:, x:y], T.NI[:], T.S7[:, x:y], True, False)] + [(col(pn, c), T.ID[:], T.RF[:, c, c0:c1], False, False) for c in range(3)],
@@ -574,10 +598,10 @@ def rank_program(g, core, T, topo):
         else:
             ts(T.P1[:, x:y], pn[:, x:y], 0.0, None, A.is_equal, None, ["nam" + k], ["P1" + k], [bn])
             ts(T.P2[:, x:y], pn[:, x:y], 0.25, None, A.is_gt, None, ["nam" + k], ["P2" + k], [bn])
-        ac(T.n7[:, 1 + x:1 + y], pn[:, x:y], Cp, ["nam" + k], ["n7" + k], [bn])
-        ac(T.n7[:, x + 7:y + 1:7], T.RST[:, x + 1:y - 5:7], I, ["RST"], ["n7" + k], bias=4.0)
+        ac(T.n7[:, h, 1 + x:1 + y], pn[:, x:y], Cp, ["nam" + k], ["n7" + k], [bn])
         mms([(pk[:, x:y], T.IB[:], q[:, x:y], False, j == 1) for j, q in enumerate((T.P2, T.P1))], ["IB", "P1" + k, "P2" + k], ["key" + k], [bk])
-        tt(T.dn[:, x:y], T.n7[:, x:y], pn[:, x:y], A.subtract, ["n70", "n7" + k, "nam" + k], ["dn" + k], [bn])
+        tt(T.dn[:, x:y], T.n7[:, h, x:y], pn[:, x:y], A.subtract, ["n7" + k, "nam" + k], ["dn" + k], [bn])
+        ac(T.n7[:, h, x + 7:y + 1:7], T.RST[:, x + 1:y:7], I, ["RST"], ["n7" + k], bias=4.0)
 
     def heights(r):
         for h, (a, b) in enumerate(HS):
@@ -589,32 +613,32 @@ def rank_program(g, core, T, topo):
             mms([(ps, T.ID[:], hown(r, a, b), True, False), (ps, T.HI[:], T.hy[:, a:b], False, True)],
                 ["ID", "HI", "hy" + k, "h%d%d" % (r, h)], [bk], [bk])
             ac(hown(r + 1, a, b), ps, I, [bk], ["h%d%d" % (r + 1, h), "hr" + k], [bk], bias=-128.0)
-            if r + 1 < RO:
-                e = B if h == 0 else b - a
-                ac(T.HO[:, a:a + e], ps[:, 0:e], I, [bk], ["hc%d" % (2 * h)], [bk], bias=-128.0)
-        if r + 1 == RO:
+        if r + 1 < RO:
+            copy(T.HO[:, 16 * CH[2][0]:V], hown(r + 1, 16 * CH[2][0], V), V - 16 * CH[2][0], ["h%d1" % (r + 1)], ["hc2"])
+        else:
             dma("y", "dout", [(T.yh[:], hown(RO))], ["h%d0" % RO, "h%d1" % RO], [])
 
     def choose(r, j):
-        c0, c1, n = EX[j]
-        a, b, k, h = 7 * c0, 7 * c0 + n, "abc"[j], str(min(j, 1))
+        c0, c1 = EX[j]
+        a, b, k, h = 7 * c0, 7 * c1, "abc"[j], str(min(j, 1))
+        n, m = b - a, -(-(b - a) // 16)
         pk, bk = KEY[min(j, 1)]
         for t in range(3):
             rb, qb = "RB%d%s" % (t, k), "QB%d%s" % (t, k)
             scan(T.RB[:, t, a:b], T.RST[:, a:b], pk[:, a:b], 0.0, A.add, A.min, ["RST", "kq" + k, "key" + h], [rb], [bk])
             tt(T.nq[:, a:b], T.RB[:, t, a:b], pk[:, a:b], A.not_equal, [rb, "kq" + k, "key" + h], ["nq" + k], [bk])
-            scan(T.QB[:, t, a:b], T.dn[:, a:b], T.nq[:, a:b], 0.0, A.add, A.mult, ["dn" + h, "nq" + k], [qb])
+            scan(T.QB[:, j, t, 0:n], T.dn[:, a:b], T.nq[:, a:b], 0.0, A.add, A.mult, ["dn" + h, "nq" + k], [qb])
             if t < 2:
-                tt(T.kp[:, a:b], ind(T.QB[:, t, a:b + 8 * (j == 2)], T.BL[:, 0:n // 16]), T.n7[:, 1 + a:1 + b], A.not_equal,
-                   [qb, "n7" + h, "BL"], ["pen" + k])
-                tt(pk[:, a:b], pk[:, a:b], T.kp[:, a:b], A.mult, ["kq" + k, "key" + h, "pen" + k], ["kq" + k], [bk])
+                tt(T.kp[:, j, 0:16 * m], ind(T.QB[:, j, t, 0:16 * m + 8], T.BL[:, 0:m]), T.n7[:, min(j, 1), 1 + a:1 + a + 16 * m],
+                   A.not_equal, [qb, "n7" + h, "BL"], ["pen" + k])
+                tt(pk[:, a:b], pk[:, a:b], T.kp[:, j, 0:n], A.mult, ["kq" + k, "key" + h, "pen" + k], ["kq" + k], [bk])
         rb, qb = ["RB%d%s" % (t, k) for t in range(3)], ["QB%d%s" % (t, k) for t in range(3)]
         if j or r + 1 < RO:
-            tt(T.RF[:, :, c0:c1], T.QB[:, :, a + 6:7 * c1:7], T.ON[:, :, c0:c1], A.add, qb + ["ON" + h], ["RF" + k])
+            tt(T.RF[:, :, c0:c1], T.QB[:, j, :, 6:n:7], T.ON[:, :, c0:c1], A.add, qb + ["ON" + h], ["RF" + k])
         if j:
             tt(T.NF[:, :, c0:c1], T.RF[:, :, c0:c1], T.SF[:, :, c0:c1], A.add, ["RF" + k] + SF, ["NF" + k])
         else:
-            tt(T.NF[:, :, c0:c1], T.QB[:, :, a + 6:7 * c1:7], T.OS[:, :, c0:c1], A.add, qb + ["OS" + h], ["NF" + k])
+            tt(T.NF[:, :, c0:c1], T.QB[:, j, :, 6:n:7], T.OS[:, :, c0:c1], A.add, qb + ["OS" + h], ["NF" + k])
         tt(T.Ki[:, :, c0:c1], T.NH[:, :, c0:c1], T.RB[:, :, a + 6:7 * c1:7], A.subtract, rb + ["NH" + h], ["Ki" + k])
         ts(T.xi[:, :, c0:c1], T.Ki[:, :, c0:c1], 2047, None, A.bitwise_and, None, ["Ki" + k], ["xi" + k])
         ts(T.EU[:, :, c0:c1], T.xi[:, :, c0:c1], 16.0, pm, A.mult, A.add, ["xi" + k, "PF"], ["EU" + k])
@@ -622,7 +646,7 @@ def rank_program(g, core, T, topo):
             ts(T.NU[:, :, c0:c1], T.NF[:, :, c0:c1], 1 / SC, None, A.mult, None, ["NF" + k], ["NU" + k])
             ts(T.EM[:, :, c0:c1], T.RF[:, :, c0:c1], 0.0, 16.0, A.is_equal, A.mult, ["RF" + k], ["EM" + k])
 
-    def new_weights(r, c0, c1, eng):
+    def new_weights(r, c0, c1, eng="sss", early=0.0):
         R = ["z", "zc0", "zc1", "zc2"] + ["cw%d%d" % (l, h) for l in range(3) for h in range(2)] + [t for q in range(r + 1) for t in wall(q)]
         for t in range(3):
             if r + 1 == RO:
@@ -633,9 +657,9 @@ def rank_program(g, core, T, topo):
                 o, w = wblk(r + 1, t, 16 * c0, 16 * c1), "w%d_%d%d" % (r + 1, c0 // 32, t)
             gather(eng[t], o, BG[:, 0:unit(r, 0) * U + V], T.EU[:, t, c0:c1], R + tok("EU", c0, c1), [w])
             if r + 1 == RO:
-                dma("y", "dout", [(T.yw[:, t * V + 16 * c0:t * V + 16 * c1], o)], [w], [])
+                dma("y", "dout", [(T.yw[:, t * V + 16 * c0:t * V + 16 * c1], o)], [w], [], early)
             elif c0 == 0:
-                ac(wblk(r + 1, t, 0, B), o, Cp, [w], ["w%d_2%d" % (r + 1, t)])
+                copy(wblk(r + 1, t, 0, B), o, B, [w], ["w%d_2%d" % (r + 1, t)])
 
     for r in range(RO):
         if r == 0:
@@ -657,12 +681,12 @@ def rank_program(g, core, T, topo):
         for j in range(3):
             choose(r, j)
         if r + 1 < RO:
-            new_weights(r, 0, 10, "sss")
+            new_weights(r, *CH[0])
             hand_over(r + 1)
-            new_weights(r, 10, 32, "sss")
-            new_weights(r, 32, 56, "sss")
-    for (c0, c1, _), eng in zip(EX, LE):
-        new_weights(RO - 1, c0, c1, eng)
+            new_weights(r, *CH[1])
+            new_weights(r, *CH[2])
+    for (c0, c1), (eng, early) in zip(EX, LE):
+        new_weights(RO - 1, c0, c1, eng, early)
     ts(T.q128[:], T.NF[:], 1 / (SC * B), 192.0 - (UB + 79.5) / B, A.mult, A.add, tok("NF"), ["q128"])
     ts(T.fb[:], T.NF[:], UB * SC, None, A.is_ge, None, tok("NF"), ["fb"])
     ts(T.NB[:], T.NF[:], 1 / SC, 1024.0 * rk, A.mult, A.add, tok("NF"), ["NB"])

from concourse.bass import DstId, RemoteDMATransfer
from concourse.mybir import AluOpType as A, ActivationFunctionType as F

V, B, CAP, NR, RO = 896, 160, 48, 6, 3
UB = V
X = UB + NR * B
U = X // 2
U16 = U // 16
W0 = 4 * U - 16
FL = 32768.0
GF = 8192.0
SC = 2.0 ** -13
BIG = 2.0 ** 23
CH = [(0, 10), (10, 32), (32, 56)]
EX = [(0, 16), (16, 32), (32, 56)]
PS = [(0, 256), (256, V)]
HS = [(0, 512), (512, V)]
GE = [[(0, 0, 16, "s"), (1, 0, 16, "v"), (2, 0, 16, "v")],
      [(0, 16, 56, "v"), (1, 16, 56, "s"), (2, 16, 36, "s"), (2, 36, 56, "v")]]
LE = (("sss", 3.0), ("sss", 2.0), ("svs", 0.0))
CY, WAKE, FLIGHT = 0.83e-3, 0.2, 5.0
PLAN = []

bf, f2, f4, i4, u2 = "bfloat16", "float16", "float32", "int32", "uint16"


def _s(n, d):
    return ("sbuf", [128] + list(n), d)


SCRATCH = {
    "BG": _s([(4 + 6 * RO) * U], bf),
    "nbi": _s([168], i4), "ia": _s([168], i4), "ib": _s([168], i4), "fa": _s([168], f4), "fb": _s([168], f4),
    "NU": _s([3, 56], u2), "RF": _s([3, 56], f2), "NF": _s([3, 56], f2), "ON": _s([3, 56], f2), "OS": _s([3, 56], f2),
    "EM": _s([3, 56], bf), "PN": _s([3, 56], f4), "VA": _s([56], f4), "PA": _s([3, 56], f4), "AB": _s([2, 3, 56], f4),
    "m1": _s([2, 56], f4), "m": _s([2, 56], i4), "oi": _s([56], i4), "OU": _s([56], u2), "WU": _s([56], u2),
    "nh": _s([3, 56], bf), "NH": _s([3, 56], f4), "gm": _s([3, 56], bf), "DA": _s([56], bf), "cmp": _s([2688], bf),
    "gI": _s([1152], bf), "ok": _s([176], bf), "d01": _s([56], bf), "die": _s([56], bf), "dieB": _s([16], bf),
    "cs": _s([16], bf), "G": _s([2688], bf), "TB": _s([512], bf), "H8": _s([3, 56], bf), "mk": _s([B], bf),
    "LS": _s([RO, B], bf), "ws": _s([V], bf), "tt": _s([V], bf), "wd2": _s([V], bf), "wr2": _s([V], bf),
    "Fg": _s([V], bf), "hr": _s([V], bf), "hy": _s([V], bf), "hyb": _s([B], bf), "P1": _s([400], bf), "P2": _s([400], bf),
    "n7": _s([2, 408], f4), "dn": _s([400], f4), "RB": _s([3, 400], f4), "QB": _s([4, 3, 184], f4), "nq": _s([400], bf),
    "kp": _s([4, 176], bf), "Ki": _s([3, 56], i4), "xi": _s([3, 56], i4), "EU": _s([3, 56], u2), "KS": _s([3, 56], f4),
    "KP": _s([3, 56], f4), "E": _s([128, 16], bf), "E2": _s([384], f4), "E3": _s([384], f2), "P0": _s([400], bf), "WF": _s([2688], bf), "HO": _s([V], bf),
    "NB": _s([168], f4), "YN": _s([168], f4), "q128": _s([168], bf),
    "PI": _s([2], i4), "PF": _s([16], f4), "J": _s([144], f4), "JG": _s([128], f4), "QS": _s([144], bf),
    "QK": _s([144], bf), "QH": _s([144], bf), "FM": _s([144], bf), "QF": _s([24], bf), "PT": _s([16, 144], bf),
    "OH": _s([16], f4), "O3": _s([6], f4), "ID": _s([128], bf), "NI": _s([128], bf), "HI": _s([128], bf),
    "IB": _s([128], bf), "N4": _s([128], f4), "I4": _s([48], f4), "S6": _s([128], bf), "I8": _s([128], bf),
    "N8": _s([128], bf), "ONE": _s([128], bf), "TRI": _s([128], bf), "tri0": _s([128], bf), "tri1": _s([128], bf),
    "c16": _s([56], f4), "VW": _s([56], f4), "SF": _s([3, 56], f2), "T7": _s([406], bf), "S7": _s([400], f2),
    "RST": _s([400], f4), "BL": _s([14], u2), "bli": _s([14], i4), "o16": _s([16], bf), "m56": _s([56], bf),
    "pA": ("psum", [128, 512], f4), "pV": ("psum", [128, 512], f4), "pN": ("psum", [128, 512], f4),
    "pK": ("psum", [128, 512], f4), "pT0": ("psum", [128, 512], f4), "pT1": ("psum", [128, 512], f4),
    "pH0": ("psum", [128, 512], f4), "pH1": ("psum", [128, 512], f4),
}
for _r in range(RO):
    SCRATCH["HW%d" % _r] = _s([X], bf)
    SCRATCH["DW%d" % _r] = _s([X], bf)
    SCRATCH["TT%d" % _r] = _s([X], bf)
    SCRATCH["SB%d" % _r] = _s([B], bf)

SEMAPHORES = ["cv", "cs", "ct", "cg", "snt", "dnb", "dhb", "dh", "dw", "dsb", "dout"] + \
    ["%s%d" % (k, r) for k in ("mh", "md", "mb", "mw", "ho") for r in range(RO)]


def unit(r, l):
    return 8 + 6 * r - 2 * l


def peers_of(core, T, turn=0):
    k = T.rank_of(core)
    p = list(T.cores[k + 1:]) + list(T.cores[:k])
    return p[turn:] + p[:turn]


def carriers(core, peers, topo):
    ok = [c for c in topo.cores_of(core) if c != core and all(topo.may_write(c, p) for p in peers)]
    return sorted(ok, key=lambda c: topo.die(c) == topo.die(core))[:3]


def common_mask(core, dsts, topo):
    mask = -1
    for c in dsts:
        mask &= topo.mask(core, c)
    return mask, len([e for e in topo.engines(core, dsts[0]) if mask >> e & 1])


def ids_of(core, dsts, topo):
    return [DstId(rid=topo.addr(c, core)[0], pnc=topo.addr(c, core)[1]) for c in dsts]


def spare(core, near, peers, topo):
    return [e for e in topo.engines(core, near) if not common_mask(core, peers, topo)[0] >> e & 1]


def carrier_program(g, core, owner, k, T, topo):
    peers = peers_of(owner, T, 2 * k)
    mask, ne = common_mask(core, peers, topo)
    ub = UB + B * T.rank_of(owner)
    for r in range(RO):
        g.wait_ge(T.sem["ho%d" % r], len(spare(owner, core, peers, topo)) // 2 if k < 2 else ne)
        o = unit(r, k) * U + ub
        g.remote_dma_fused([RemoteDMATransfer(dst_ids=ids_of(core, peers, topo), dma_engine_mask=mask, remote_sem=T.sem["mw%d" % r],
                                              src=T["SB%d" % r][:], dsts=[T.BG[:, o:o + B]] * len(peers))],
                           local_sem=T.sem.snt)
    g.wait_ge(T.sem.snt, RO * ne)


def rank_program(g, core, T, topo):
    rk = T.rank_of(core)
    if rk is None:
        for owner in T.cores:
            cs = carriers(owner, peers_of(owner, T), topo)
            if core in cs:
                carrier_program(g, core, owner, cs.index(core), T, topo)
        return
    Q = {"v": g.vector, "s": g.scalar, "t": g.tensor, "g": g, "y": g.sync}
    calls, wr, rd, bank, gathers = [], {}, {}, {}, []

    seen = {}

    def kind(e, t):
        for p in ("dw", "hb", "wb", "ls", "tb", "hf", "tf", "wf", "dwf", "h", "w"):
            if t.startswith(p) and t[len(p):len(p) + 1].isdigit():
                t = p + t[len(p) + 1:]
        return seen.setdefault(e + t, len(seen))

    def call(e, fn, hold, R, W, Bk=(), late=WAKE, sem=None):
        k = len(calls)
        dep = {wr[t] for t in list(R) + list(W) if t in wr}
        for t in W:
            dep.update(rd.get(t, ()))
        for b in Bk:
            who, now, before = bank.get(b, (e, [], []))
            if who != e:
                now, before = [], now
            dep.update(before + (now[-1:] if e == "t" and W else []))
            bank[b] = (e, now + [k], before)
        for t in R:
            rd.setdefault(t, []).append(k)
        for t in W:
            wr[t], rd[t] = k, []
        calls.append({"e": e, "fn": fn, "hold": hold, "late": late, "dep": dep, "sem": sem, "kind": kind(e, (list(W) or list(R))[-1])})
        return k

    def issue():
        n = len(calls)
        before = [sorted(c["dep"]) for c in calls]
        after = [[] for _ in calls]
        for k in range(n):
            for d in before[k]:
                after[d].append(k)

        def gap(d, k):
            return 0.0 if calls[d]["e"] == calls[k]["e"] == "t" else calls[d]["late"]

        def place(order):
            end, busy = [0.0] * n, {e: [] for e in "vstgyx"}
            for k in order:
                t = max([0.0] + [end[d] + gap(d, k) for d in before[k]])
                h, line = calls[k]["hold"], busy[calls[k]["e"]]
                i = len(line)
                while i and line[i - 1][1] > t:
                    i -= 1
                while i < len(line) and line[i][0] < t + h:
                    t = max(t, line[i][1])
                    i += 1
                line.insert(i, (t, t + h))
                end[k] = t + h
            return end
        if not PLAN:
            best, seed, bias = None, 1, [0.0] * len(seen)
            way = [0.0] * n
            for k in range(n - 1, -1, -1):
                way[k] = calls[k]["hold"] + max([calls[k]["late"]] + [way[j] + gap(k, j) for j in after[k]])
            for turn in range(1500):
                trial = list(bias)
                for _ in range(2 if turn else 0):
                    seed = (seed * 1103515245 + 12345) % 2 ** 31
                    j = (seed >> 8) % len(seen)
                    seed = (seed * 1103515245 + 12345) % 2 ** 31
                    trial[j] += 1.0 * (2 * seed / 2 ** 31 - 1)
                pr = [0.0] * n
                for k in range(n - 1, -1, -1):
                    pr[k] = max([way[k] + trial[calls[k]["kind"]]] + [pr[j] + 1e-3 for j in after[k]])
                end = place(sorted(range(n), key=lambda k: (-pr[k], k)))
                span = max(end[k] + calls[k]["late"] for k in range(n))
                if best is None or span <= best[0]:
                    best, bias = (span, end), trial
            PLAN.extend(sorted(range(n), key=lambda k: (best[1][k] - calls[k]["hold"], k)))
        cnt, waited = {}, {e: {} for e in Q}
        for k in PLAN:
            c = calls[k]
            e = c["e"]
            if e == "x":
                c["done"] = c["sem"]
                cnt[c["sem"][0]] = c["sem"][1]
                continue
            need = {}
            for d in before[k]:
                s, m = calls[d]["done"]
                if not (e == "t" and s == "ct"):
                    need[s] = max(need.get(s, 0), m)
            for s, m in need.items():
                if waited[e].get(s, 0) < m:
                    Q[e].wait_ge(T.sem[s], m)
                    waited[e][s] = m
            s, m = c["sem"] or ("c" + e, 1)
            c["fn"](s)
            cnt[s] = cnt.get(s, 0) + m
            c["done"] = (s, cnt[s])
        for s, m in cnt.items():
            g.wait_ge(T.sem[s], m)

    def size(o):
        n = 1
        for d in o.shape[1:]:
            n *= d
        return n

    def ind(win, off):
        gathers.append(win.indirect(off))
        return gathers[-1]

    def op(e, fn, o, i, per, R, W, Bk=()):
        if any(i is x for x in gathers):
            hold = 70 + 1.56 * size(o)
        else:
            if per == 1 and e == "v" and "16" in str(o.dtype) and "16" in str(i.dtype):
                per = 0.5
            hold = max(64, per * size(o))
        call(e, lambda s: fn().then_inc(T.sem[s], 1), CY * hold, R, W, Bk)

    def mms(lst, R, W, Bk):
        def fn(s):
            for a in lst[:-1]:
                g.tensor.matmul(*a)
            g.tensor.matmul(*lst[-1]).then_inc(T.sem[s], 1)
        call("t", fn, sum(CY / 1.8 * max(64, size(a[0])) * (4 if "32" in str(a[1].dtype) else 1) for a in lst), R, W, Bk)

    def dma(e, sem, pairs, R, W, early=0.0):
        def fn(s):
            for o, i in pairs:
                Q[e].dma_start(o, i).then_inc(T.sem[s], 16)
        if W:
            call(e, fn, 0.05 * len(pairs), R, W, late=2.0 + len(pairs), sem=(sem, 16 * len(pairs)))
        else:
            call(e, fn, 0.35, R, W, late=2.0 + early, sem=(sem, 16))

    peers = peers_of(core, T)
    mask, ne = common_mask(core, peers, topo)
    ids = ids_of(core, peers, topo)
    cars = carriers(core, peers, topo)
    on = spare(core, cars[0], peers, topo)

    def remote(trs, n, R, sem, m, tok, flight):
        k = call("g", lambda s: g.remote_dma_fused(trs, local_sem=T.sem[s]), 0.3, R, [], late=0.01, sem=("snt", n))
        calls[call("x", None, 0.0, [], [tok], late=flight, sem=(sem, m))]["dep"].add(k)

    def send(ap, sem, R, tok, src=None):
        remote([RemoteDMATransfer(dst_ids=ids, dma_engine_mask=mask, remote_sem=T.sem[sem], src=ap if src is None else src,
                                  dsts=[ap] * len(ids))], ne, R, sem, ne * len(ids), tok, FLIGHT)

    def hand_over(r):
        o = [unit(r, l) * U + UB + B * rk for l in range(3)]
        remote([RemoteDMATransfer(dst_ids=ids_of(core, [c], topo), dma_engine_mask=sum(1 << e for e in on[k::2]) if k < 2 else mask,
                                  remote_sem=T.sem["ho%d" % r], src=T.BG[:, o[k]:o[k] + B], dsts=[T["SB%d" % r][:]])
                for k, c in enumerate(cars)], len(on) + ne, ["wb%d%d" % (r, l) for l in range(3)],
               "mw%d" % r, 3 * ne * len(ids), "wf%d" % r, 2.2 * FLIGHT)

    v, s = g.vector, g.scalar

    def ts(o, i, a, b, o0, o1, R, W, Bk=()):
        op("v", (lambda: v.tensor_scalar(o, i, a, b, o0, o1)) if o1 is not None else
           (lambda: v.tensor_scalar(o, i, a, None, o0)), o, i, 1, R, W, Bk)

    def tt(o, i, j, o0, R, W, Bk=()):
        op("v", lambda: v.tensor_tensor(o, i, j, o0), o, i, 1.0001 if Bk else 2, R, W, Bk)

    def cp(o, i, R, W, Bk=()):
        op("v", lambda: v.tensor_copy(o, i), o, i, 1, R, W, Bk)

    def ms(o, c, W, Bk=()):
        op("v", lambda: v.memset(o, c), o, o, 1, [], W, Bk)

    def scan(o, a, b, c, o0, o1, R, W, Bk=()):
        op("v", lambda: v.tensor_tensor_scan(o, a, b, c, o0, o1), o, a, 1, R, W, Bk)

    def ac(o, i, f, R, W, Bk=(), bias=0.0, scale=1.0):
        op("s", lambda: s.activation(o, i, f, bias=bias, scale=scale), o, i, 1, R, W, Bk)

    def io(o, pat, base, cm, W, fl=True):
        op("g", (lambda: g.iota(o, pat, base, cm, allow_small_or_imprecise_dtypes=True)) if fl else
           (lambda: g.iota(o, pat, base, cm)), o, o, 3, [], W)

    def copy(o, i, n, R, W):
        call("g", lambda s: g.affine_select(o, i, [[0, n]], A.is_equal, 0.0, 0, 0).then_inc(T.sem[s], 1), 0.17 + 2 * CY * n, R, W)

    BG = T.BG
    HW = [T["HW%d" % r] for r in range(RO)]
    DW = [T["DW%d" % r] for r in range(RO)]
    TT = [T["TT%d" % r] for r in range(RO)]
    ub = UB + B * rk
    pT, pH = [T.pT0, T.pT1], [T.pH0, T.pH1]
    VAL, KEY, NAME = [(T.pV, "pV"), (T.pN, "pN")], [(T.pV, "pV"), (T.pK, "pK")], [(T.pA, "pA"), (T.pN, "pN")]
    I, Re, Cp = F.Identity, F.Relu, F.Copy

    def gather(e, o, win, off, R, W):
        if e == "s":
            ac(o, ind(win, off), Cp, R, W)
        else:
            cp(o, ind(win, off), R, W)

    def wblk(r, l, a=0, b=V):
        return BG[:, unit(r, l) * U + a:unit(r, l) * U + b]

    def cw(l, a=0, b=V):
        return BG[:, (3 - l) * U + a:(3 - l) * U + b]

    def hown(r, a=0, b=V):
        return HW[r][:, a:b] if r < RO else T.hr[:, a:b]

    def sel(tab, i):
        return tab[:, 15 - i:143 - i]

    PT = ["PT%d" % i for i in range(16)]
    T7 = ["T7%d" % c for c in range(3)]
    ET = ["E%d" % l for l in range(6)]
    GT = [["G%d%d" % (h, j) for j in range(len(GE[h]))] for h in range(2)]
    SF = ["SFa", "SFb"]

    def tok(name, c0=0, c1=56):
        return [name + k for k, (a, b) in zip("abc", EX) if a < c1 and c0 < b]

    def wown(r):
        return ["w%d_%d%d" % (r, h, c) for h in range(3) for c in range(3)]

    def wall(r):
        return wown(r) + ["wb%d%d" % (r, l) for l in range(3)] + ["wf%d" % r]

    def hall(r):
        return ["h%d0" % r, "h%d1" % r, "hb%d" % r, "hf%d" % r]

    def name_table():
        ts(T.H8[:], T.NF[:], 256.0, 127.516, A.mult, A.add, tok("NF"), ["H8"])
        mms([(T.pK[0:56, 128 * l:128 * (l + 1)], T.H8[:, l], T.I8[:], True, True) for l in range(3)], ["H8", "I8"], ["key1"], ["pK"])
        mms([(pT[0][0:56, 128 * l:128 * (l + 1)], a[:, l], b[:], k == 0, k == 1) for l in range(3)
             for k, (a, b) in enumerate(((T.NF, T.ID), (T.H8, T.N8)))], ["H8", "ID", "N8"] + tok("NF"), ["pT0"], ["pT0"])
        for l in range(6):
            src, t, b = (T.pK, "key1", "pK") if l < 3 else (pT[0], "pT0", "pT0")
            ac(T.E[0:56, l:128:16, :], src[0:56, 128 * (l % 3):128 * (l % 3 + 1)], I, [t, "Ez"], [ET[l]], [b], bias=-0.5 if l < 3 else 0.5)
        for h, (a, b) in enumerate(HS):
            lst = [(pT[h][:, 0:b - a], T.ID[:], BG[:, 0:b - a], True, False)] if h else []
            lst += [(pT[h][:, i:b - a:16], T.E[0:56, :, i], T.ID[0:56, a // 16:b // 16], h == 0, h == 0) for i in range(16)]
            mms(lst, ["ID", "z"] + ET, ["pT%d" % h], ["pT%d" % h])
        ac(T.TB[:], pT[0][:], Cp, ["pT0"], ["TB"], ["pT0"])
        ts(T.mk[:], T.TB[:, 0:B], T.O3[:, 3:4], 0.5, A.is_lt, A.mult, ["TB", "O33"], ["mk"])

    dma("y", "dhb", [(HW[0][:, ub:ub + B], T.h0[:, 0:B])], [], ["hb0"])
    dma("s", "dnb", [(T.nbi[:], T.nb[:])], [], ["nbi"])
    dma("y", "dsb", [(wblk(0, l, ub, ub + B), T.w0[:, l * V:l * V + B]) for l in range(3)], [], ["wb00", "wb01", "wb02"])
    dma("s", "dh", [(hown(0), T.h0[:]), (T.HO[:], T.h0[:])], [], ["h00", "h01", "hc0", "hc2"])
    dma("y", "dw", [(wblk(0, l), T.w0[:, l * V:(l + 1) * V]) for l in range(3)], [], wown(0))
    io(T.PI[:, 0:1], [[0, 1]], 0, 1, ["PI0"], False)
    io(T.J[:], [[1, 144]], 0, 0, ["J"])
    io(T.c16[:], [[16, 56]], 0, 0, ["c16"])
    io(T.JG[:], [[16, 8], [0, 16]], 0, 0, ["JG"])
    send(HW[0][:, ub:ub + B], "mh0", ["hb0"], "hf0")
    hand_over(0)
    io(T.T7[:], [[1, 58], [0, 7]], 0, 0, ["T7"])

    p, pm, pg = T.PF[:, 0:1], T.PF[:, 1:2], T.PF[:, 2:3]
    ms(BG[:, 0:U], 0.0, ["z"])
    ts(T.PI[:, 1:2], T.PI[:, 0:1], 15, None, A.bitwise_and, None, ["PI0"], ["PI1"])
    ms(T.DA[:], 0.0, ["DA0", "DA1", "DA2"])
    cp(T.PF[:, 0:2], T.PI[:, 0:2], ["PI0", "PI1"], ["PF"])
    ms(T.o16[:], 1.0, ["o16"])
    tt(pg, p, pm, A.subtract, ["PF"], ["pg"])
    ts(T.OH[:], T.J[:, 0:16], pm, None, A.is_equal, None, ["J", "PF"], ["OH"])
    ts(T.QS[:], T.J[:], pg, 15.0, A.subtract, A.is_equal, ["J", "pg"], ["QS"])
    ts(T.VW[:], T.c16[:], pm, None, A.add, None, ["PF", "c16"], ["VW"])
    ts(T.ID[:], T.J[:, 0:128], p, None, A.is_equal, None, ["J", "PF"], ["ID"])
    ms(T.E[:], 0.0, ["Ez"])
    for l in range(3):
        ts(T.SF[:, l, 0:10], T.VW[:, 0:10], float(ub), SC, A.add, A.mult, ["VW"], ["SFa"])
        ts(T.SF[:, l, 10:56], T.VW[:, 10:56], SC, None, A.mult, None, ["VW"], ["SFb"])
    for t, k in (("NI", -1.0), ("I8", 1 / 256.0), ("N8", -1 / 256.0), ("IB", BIG), ("N4", -1.0), ("HI", 0.5)):
        ac(T[t][:], T.ID[:], I, ["ID"], [t], scale=k)
    ac(T.I4[:], T.ID[:, 0:48], Cp, ["ID"], ["I4"])
    ac(T.QH[:], T.QS[:], I, ["QS"], ["QH"], scale=0.5)
    ac(T.QK[:], T.QS[:], I, ["QS"], ["QK"], scale=-2048.0)
    for i in range(16):
        ac(T.PT[:, i, :], T.QS[:], I, ["QS", "OH"], [PT[i]], scale=T.OH[:, i:i + 1])
    ts(T.ia[:], T.nbi[:], 10, None, A.arith_shift_right, None, ["nbi"], ["ia"])
    ts(T.ib[:], T.nbi[:], 1023, None, A.bitwise_and, None, ["nbi"], ["ib"])
    ts(T.fa[:], T.ia[:], float(B), float(UB), A.mult, A.add, ["ia"], ["fa"])
    ts(T.fb[:], T.ib[:], float(B), None, A.is_lt, None, ["ib"], ["fb"])
    tt(T.fa[:], T.fa[:], T.fb[:], A.mult, ["fa", "fb"], ["fa"])
    tt(T.fa[:], T.fa[:], T.ib[:], A.add, ["fa", "ib"], ["fa"])
    ts(T.NF[:], T.fa[:], SC, None, A.mult, None, ["fa"], tok("NF"))
    cp(T.NU[:], T.fa[:], ["fa"], tok("NU"))
    tt(T.RF[:], T.NF[:], T.SF[:], A.subtract, tok("NF") + SF, tok("RF"))
    ts(T.EM[:], T.RF[:], 0.0, 16.0, A.is_equal, A.mult, tok("RF"), tok("EM"))
    ts(T.O3[:, 0:1], pm, 3.0, None, A.is_lt, None, ["PF"], ["O30"])
    ts(T.O3[:, 3:4], T.O3[:, 0:1], 1.0 + (UB - 16) * SC, -1.0, A.mult, A.add, ["O30"], ["O33"])
    ts(T.ONE[:], T.JG[:], pg, 1.0 / FL, A.is_equal, A.mult, ["JG", "pg"], ["ONE"])
    ts(T.tri0[:], T.J[:, 0:128], p, -1.0, A.is_lt, A.mult, ["J", "PF"], ["tri0"])
    ac(T.tri1[:], T.ID[:], I, ["ID"], ["tri1"], scale=-64.0)
    tt(T.tri0[:], T.tri0[:], T.tri1[:], A.add, ["tri0", "tri1"], ["tri0"])
    tt(T.TRI[:], T.tri0[:], T.ONE[:], A.mult, ["tri0", "ONE"], ["TRI"])
    ts(T.S6[:], T.J[:, 0:128], p, 6.0, A.subtract, A.is_equal, ["J", "PF"], ["S6"])
    ts(T.S6[:], T.S6[:], T.O3[:, 0:1], None, A.mult, None, ["S6", "O30"], ["S6"])
    ms(T.S7[:], 0.0, ["S7"])
    for l in range(3):
        ts(T.T7[:, 3 + l:392:7], T.T7[:, 3 + l:392:7], float((3 - l) * U16), None, A.add, None, ["T7"], [T7[l]])
        cp(T.S7[:, 3 + l:392:7], T.SF[:, 0], SF + ["S7"], ["S7%d" % l])
        ms(cw(l, V, U), 0.0, ["zc%d" % l])
    for r in range(RO):
        ms(DW[r][:, 0:B], 0.0, ["dwz%d" % r])
        ms(TT[r][:, 0:B], 0.0, ["ttz%d" % r])
    ts(T.bli[:], T.VW[:, 0:14], -3.0, 1 / 7.0, A.add, A.mult, ["VW"], ["bli"])
    ts(T.BL[:], T.bli[:], 7.0, 6.0, A.mult, A.add, ["bli"], ["BL"])
    ms(T.RST[:], 0.0, ["RST"])
    ms(T.RST[:, 0:400:7], 4 * BIG, ["RST"])
    ms(T.n7[:, 0, 0:8], 4.0, ["n70"])
    ms(T.n7[:, 1, 112:120], 4.0, ["n71"])
    ms(T.n7[:, 1, 392:408], 4.0, ["n71"])
    ms(T.m56[:], -1.0, ["m56"])
    for j, u in enumerate("abcd"):
        ms(T.QB[:, j, 0:2, 64:184], 0.0, ["QB0" + u, "QB1" + u])
    for l in range(3):
        tt(T.O3[:, 1:2], T.OH[:, l:l + 1], T.OH[:, l + 3:l + 4], A.add, ["OH"], ["O31"])
        tt(T.O3[:, 2:3], T.O3[:, 1:2], T.OH[:, l + 6:l + 7], A.add, ["OH", "O31"], ["O32"])
        ts(T.QF[:, 8 * l:8 * (l + 1)], T.JG[:, 0:128:16], pg, T.O3[:, 2:3], A.is_equal, A.mult, ["JG", "pg", "O32"], ["QF%d" % l])
    ts(T.FM[:], T.QS[:], T.OH[:, 0:1], 0.5 / GF, A.mult, A.mult, ["QS", "OH"], ["FM"])
    mms([(T.pN[:, 56 * c:56 * (c + 1)], sel(T.QK, i), BG[:, unit(0, c) * U + i:unit(0, c) * U + V:16], i == 0, i == 15)
         for c in range(3) for i in range(16)], ["QK"] + wown(0), ["pN"], ["pN"])
    ac(T.KS[:], T.pN[:, 0:168], I, ["pN"], ["KS"], ["pN"], scale=-1.0)

    def votes(r, k):
        c0, c1 = CH[k]
        n, o = 16 * (c1 - c0), 3 * c0
        for l in range(3):
            out, w, t = T.cmp[:, 48 * c0 + n * l:48 * c0 + n * (l + 1)], ind(HW[r][:], T.NU[:, l, c0:c1]), hall(r) + tok("NU", c0, c1)
            if k != 1:
                tt(out, w, T.HO[:, 16 * c0:16 * c1], A.is_lt, t + ["hc%d" % k], ["cmp%d%d" % (k, l)])
                continue
            b, ps = "pH%d" % (l % 2), pH[l % 2][:, 0:n]
            ac(T.gI[:, l * n:(l + 1) * n], w, Cp, t, ["gI%d" % l])
            mms([(ps, T.ID[:], hown(r, 16 * c0, 16 * c1), True, False), (ps, T.NI[:], T.gI[:, l * n:(l + 1) * n], False, True)],
                ["ID", "NI", "gI%d" % l] + hall(r)[:2], [b], [b])
            ac(out, ps, F.Sign, [b], ["cmp1%d" % l], [b], bias=-0.5)
        lst = [(T.pA[:, o:3 * c1], T.ID[:], T.EM[:, :, c0:c1], True, False)]
        if k == 0:
            lst.append((T.pA[:, c0:c1], T.NI[:], T.DA[:, c0:c1], False, False))
        mms(lst, ["ID", "NI", "DA%d" % k] + tok("EM", c0, c1), ["vt%d" % k], ["pA"])
        mms([(T.pA[:, o:3 * c1], sel(T.QH if k == 1 else T.QS, i), T.cmp[:, 48 * c0 + i:48 * c1:16], False, i == 15) for i in range(16)],
            ["QS", "QH"] + ["cmp%d%d" % (k, l) for l in range(3)], ["vt%d" % k], ["pA"])

    def deaths(r, k):
        c0, c1 = CH[k]
        n, o = c1 - c0, 3 * c0
        ts(T.ok[:, o:o + 3 * n], T.pA[:, o:o + 3 * n], 1.0 if k == 1 else 9.0, 32.0, A.is_ge, A.mult, ["vt%d" % k], ["ok%d" % k], ["pA"])
        tt(T.d01[:, c0:c1], T.ok[:, o:o + n], T.ok[:, o + n:o + 2 * n], A.mult, ["ok%d" % k], ["d01%d" % k])
        tt(T.die[:, c0:c1], T.d01[:, c0:c1], T.ok[:, o + 2 * n:o + 3 * n], A.mult, ["ok%d" % k, "d01%d" % k], ["die%d" % k])
        die, ps, pn, at = T.die[:, c0:c1], (T.pV, T.pN, pH[1])[k][:, 0:16 * n], ("pV", "pN", "pH1")[k], 16 * c0
        if k == 0:
            cn, die, at = T.pA[:, 200:210], T.dieB[:, 0:10], ub
            scan(T.cs[:, 0:10], T.o16[:, 0:10], T.die[:, 0:10], 0.0, A.mult, A.add, ["o16", "die0"], ["cs"])
            mms([(cn, T.TRI[:], T.die[:, 0:10], True, False), (cn, T.ONE[:], T.cs[:, 0:10], False, True)],
                ["TRI", "ONE", "die0", "cs"], ["cn"], ["pA"])
            ts(die, cn, CAP - 64.0, FL, A.is_le, A.mult, ["cn"], ["dieB"], ["pA"])
        t = "dieB" if k == 0 else "die%d" % k
        mms([(ps[:, i:16 * n:16], sel(T.PT[:, i, :], 0), die, True, True) for i in range(16)], [t] + PT, [pn], [pn])
        ac(DW[r][:, at:at + 16 * n], ps, I, [pn], ["dw%d%d" % (r, k)], [pn], scale=GF / FL)
        if k == 0:
            send(DW[r][:, ub:ub + B], "md%d" % r, ["dw%d0" % r], "dwf%d" % r)
        tt(T.DA[:, c0:c1], T.DA[:, c0:c1], die, A.max, ["DA%d" % k, t], ["DA%d" % k])

    def before_gone(r):
        for l in range(3):
            ts(T.PN[:, l], T.NF[:, l], 0.25 * (2 - l), None, A.add, None, tok("NF"), ["PN%d" % l])
        tt(T.VA[:], T.VW[:], T.DA[:], A.subtract, ["VW", "DA0", "DA1", "DA2"], ["VA"])
        if r:
            tt(T.KS[:], T.Ki[:], T.xi[:], A.subtract, tok("Ki") + tok("xi"), ["KS"])
        for l in range(3):
            ac(T.PA[:, l], T.VA[:], I, ["VA"], ["PA%d" % l], bias=(unit(r, l) * U - W0) / GF, scale=1 / GF)
            ac(T.KP[:, l], T.KS[:, l], I, ["KS"], ["KP%d" % l], bias=float(unit(r, l) * U16))

    def gs(l, a, b):
        e, f = PS[int(a >= PS[1][0])]
        o = 2 * e + (f - e) * l
        return T.G[:, o + a:o + b]

    def gone(r, h):
        a, b = PS[h]
        c0, c1, k = a // 16, b // 16, str(h)
        dwt = ["dw%d%d" % (r, j) for j in range(3)] + ["dwf%d" % r, "dwz%d" % r] + tok("NU", c0, c1)
        gt = GT[h]
        for (l, e, f, eng), t in zip(GE[h], gt):
            gather(eng, gs(l, 16 * e, 16 * f), DW[r][:], T.NU[:, l, e:f], dwt, [t])
        if h == 0:
            pc = T.pV[:, 176:176 + B]
            mms([(pc, T.ID[:], T.TB[:, 0:B], True, False), (pc, T.S6[:], T.mk[:], False, False)], ["ID", "S6", "TB", "mk"], ["pV"], ["pV"])
            mms([(pc, sel(T.FM, 6 + l), gs(l, 0, B), False, l == 2) for l in range(3)], ["FM"] + gt, ["pV"], ["pV"])
            ac(T.LS[:, r], pc, Cp, ["pV"], ["ls%d" % r], ["pV"])
            send(TT[r][:, ub:ub + B], "mb%d" % r, ["ls%d" % r], "tf%d" % r, T.LS[:, r])
        o, bk = VAL[h][0][:, 0:3 * (c1 - c0)], VAL[h][1]
        mms([(o, sel(T.QS, i), T.G[:, 3 * a + i:3 * b:16], i == 0, i == 15) for i in range(16)], ["QS"] + gt, [bk], [bk])
        tt(T.AB[:, 1, :, c0:c1], o, T.PA[:, :, c0:c1], A.mult, [bk, "PA0", "PA1", "PA2"], ["AB1" + k], [bk])
        tt(T.AB[:, 0, :, c0:c1], o, T.PN[:, :, c0:c1], A.mult, [bk, "PN0", "PN1", "PN2"], ["AB0" + k], [bk])
        ac(T.gm[:, :, c0:c1], o, Cp, [bk], ["gm" + k], [bk])
        tt(T.m1[:, :, c0:c1], T.AB[:, :, 0, c0:c1], T.AB[:, :, 2, c0:c1], A.max, ["AB0" + k, "AB1" + k], ["m1" + k])
        tt(T.m[:, :, c0:c1], T.m1[:, :, c0:c1], T.AB[:, :, 1, c0:c1], A.max, ["m1" + k, "AB0" + k, "AB1" + k], ["m" + k])
        cp(T.WU[:, c0:c1], T.m[:, 1, c0:c1], ["m" + k], ["WU" + k])
        ts(T.oi[:, c0:c1], T.m[:, 0, c0:c1], 2047, None, A.bitwise_and, None, ["m" + k], ["oi" + k])
        cp(T.OU[:, c0:c1], T.oi[:, c0:c1], ["oi" + k], ["OU" + k])
        ts(T.nh[:, 0, c0:c1], T.m[:, 1, c0:c1], 0.0, None, A.is_le, None, ["m" + k], ["nh" + k])
        for t in (1, 2):
            ac(T.nh[:, t, c0:c1], T.nh[:, 0, c0:c1], Cp, ["nh" + k], ["nh%d%s" % (t, k)])
        gather("s", T.ws[:, a:b], BG[:, W0:unit(r, 0) * U + V], T.WU[:, c0:c1],
               ["zc0", "WU" + k] + [t for q in range(r + 1) for t in wall(q)], ["ws" + k])

    def marks(r):
        mms([(pT[0][:], T.ID[:], T.TB[:], True, False)] +
            [(pT[0][:, a:b], sel(T.FM, 6 + l), gs(l, a, b), False, a > 0 and l == 2) for a, b in ((0, 256), (256, 512)) for l in range(3)],
            ["FM", "ID", "TB"] + GT[0] + GT[1], ["pT0"], ["pT0"])
        mms([(pT[1][:, 0:384], sel(T.FM, 6 + l), gs(l, 512, V), False, l == 2) for l in range(3)], ["FM"] + GT[1], ["pT1"], ["pT1"])
        ac(TT[r][:, ub:ub + B], pT[0][:, 0:B], Cp, ["pT0"], ["tb%d" % r], ["pT0"])
        ac(TT[r][:, B:512], pT[0][:, B:512], Cp, ["pT0"], ["TT0"], ["pT0"])
        ac(TT[r][:, 512:V], pT[1][:, 0:384], Cp, ["pT1"], ["TT1"], ["pT1"])

    def border_heights(r):
        pb = T.pA[:, 352:512]
        mms([(pb, T.ID[:], T.ws[:, 0:B], True, False), (pb, T.NI[:], hown(r, 0, B), False, True)], ["ID", "NI", "ws0", "h%d0" % r], ["pb"], ["pA"])
        ac(T.hyb[:], pb, Re, ["pb"], ["hyb"], ["pA"])
        ac(T.hyb[:], T.hyb[:], I, ["hyb"], ["hyb"], bias=255.6)
        mms([(pb, T.ID[:], hown(r, 0, B), True, False), (pb, T.HI[:], T.hyb[:], False, True)], ["ID", "HI", "hyb", "h%d0" % r], ["pb"], ["pA"])
        ac(HW[r + 1][:, ub:ub + B], pb, I, ["pb"], ["hb%d" % (r + 1)], ["pA"], bias=-128.0)
        send(HW[r + 1][:, ub:ub + B], "mh%d" % (r + 1), ["hb%d" % (r + 1)], "hf%d" % (r + 1))
        copy(T.HO[:, 0:B], HW[r + 1][:, ub:ub + B], B, ["hb%d" % (r + 1)], ["hc0"])

    def splice(r, h):
        a, b = PS[h]
        c0, c1, k = a // 16, b // 16, str(h)
        n, x, y = c1 - c0, 7 * c0, 7 * c1
        od, ou = T.OU[:, c0:c1], ["OU" + k]
        (pk, bk), (pn, bn) = KEY[h], NAME[h]
        nh = ["nh" + k, "nh1" + k, "nh2" + k]

        def col(p, c):
            return p[:, x + c:7 * c1:7]
        mms([(pk[:, x:y], T.NI[:], T.T7[:, x:y], True, False), (col(pk, 6), T.IB[:], T.m56[:, 0:n], False, False)] +
            [(col(pk, c), T.N4[:], T.KP[:, c, c0:c1], False, False) for c in range(3)],
            ["NI", "N4", "IB", "m56", "KP0", "KP1", "KP2"] + T7, ["key" + k], [bk])
        mms([(col(pk, c), T.IB[:], T.gm[:, c, c0:c1], False, False) for c in range(3)] +
            [(col(pk, c), T.IB[:], T.nh[:, 0, c0:c1], False, False) for c in range(6)], ["IB", "nh" + k, "gm" + k, "key" + k], [], [bk])
        tt(T.ON[:, :, c0:c1], T.RF[:, :, c0:c1], T.nh[:, :, c0:c1], A.mult, tok("RF", c0, c1) + nh, ["ON" + k])
        tt(T.NH[:, :, c0:c1], T.KP[:, :, c0:c1], T.nh[:, :, c0:c1], A.mult, ["KP0", "KP1", "KP2"] + nh, ["NH" + k])
        if h == 0:
            tt(T.OS[:, :, c0:c1], T.ON[:, :, c0:c1], T.SF[:, :, c0:c1], A.add, ["ON" + k] + SF, ["OS" + k])
        tt(T.tt[:, a:b], ind(HW[r][:], od), T.ws[:, a:b], A.subtract, hall(r) + ou + ["ws" + k], ["tt" + k])
        cut = [(256, 512), (512, V)] if h else []
        if h:
            ac(T.wd2[:, a:b], ind(wblk(r, 2, 0, X), od), Cp, wall(r) + ou, ["wd2" + k])
        for e, f in cut:
            j = e // 512
            ps = pH[j][:, e - 512 * j:f - 512 * j]
            mms([(ps, T.ID[:], T.wd2[:, e:f], True, False), (ps, T.NI[:], T.tt[:, e:f], False, True)],
                ["ID", "NI", "wd2" + k, "tt" + k], ["pH%d" % j], ["pH%d" % j])
            ac(T.wr2[:, e:f], ps, Re, ["pH%d" % j], ["wr%d" % e], ["pH%d" % j])
        for l in range(3):
            t = "cw%d%s" % (l, k)
            if l < 2 or not h:
                tt(cw(l, a, b), ind(wblk(r, l, 0, X), od), T.tt[:, a:b], A.subtract, wall(r) + ou + ["tt" + k], [t])
                ts(cw(l, a, b), cw(l, a, b), 0.0, 255.0, A.max, A.min, [t], [t])
            else:
                ts(cw(l, a, b), T.wr2[:, a:b], 255.0, None, A.min, None, ["wr%d" % e for e, f in cut], [t])
            mms([(col(pk, 3 + l), sel(T.QK, i), BG[:, (3 - l) * U + a + i:(3 - l) * U + b:16], False, False) for i in range(16)],
                ["QK", t, "key" + k], [], [bk])
        ac(T.Fg[:, a:b], ind(TT[r][:], od), Cp, ["TT0", "TT1", "tb%d" % r, "tf%d" % r, "ttz%d" % r] + ou, ["Fg" + k])
        mms([(pT[h][0:n, i:384:16], T.Fg[:, a + i:b:16], T.QF[:], True, True) for i in range(16)], ["QF0", "QF1", "QF2", "Fg" + k],
            ["pT" + k], ["pT" + k])
        e2, i2 = (T.E2[0:n, :], T.I4) if h else (T.E3[0:n, :], T.ID)
        if h:
            ac(e2, pT[1][0:n, 0:384], Cp, ["pT1"], ["E2" + k], ["pT1"])
        else:
            cp(e2, pT[0][0:n, 0:384], ["pT0"], ["E2" + k], ["pT0"])
        mms([(pn[:, x:y], T.NI[:], T.S7[:, x:y], True, False)] + [(col(pn, c), T.ID[:], T.RF[:, c, c0:c1], False, False) for c in range(3)],
            ["ID", "NI", "S70", "S71", "S72"] + tok("RF", c0, c1), ["nam" + k], [bn])
        mms([(col(pn, 3 + l), e2[:, 128 * l:128 * (l + 1)], i2[0:n, 0:n], False, l == 2) for l in range(3)],
            ["I4", "E2" + k], ["nam" + k], [bn])
        if h:
            ac(T.P2[:, x:y], pn[:, x:y], Re, ["nam" + k], ["P2" + k], [bn], bias=-64.0, scale=256.0)
            ac(T.P0[:, x:y], pn[:, x:y], F.Abs, ["nam" + k], ["P0"], [bn])
            ac(T.P1[:, x:y], T.P0[:, x:y], Re, ["P0"], ["P1" + k], bias=1.0, scale=-2 / SC)
        else:
            ts(T.P1[:, x:y], pn[:, x:y], 0.0, None, A.is_equal, None, ["nam" + k], ["P1" + k], [bn])
            ts(T.P2[:, x:y], pn[:, x:y], 0.25, None, A.is_gt, None, ["nam" + k], ["P2" + k], [bn])
        ac(T.n7[:, h, 1 + x:1 + y], pn[:, x:y], Cp, ["nam" + k], ["n7" + k], [bn])
        mms([(pk[:, x:y], T.IB[:], q[:, x:y], False, j == 1) for j, q in enumerate((T.P2, T.P1))], ["IB", "P1" + k, "P2" + k], ["key" + k], [bk])
        tt(T.dn[:, x:y], T.n7[:, h, x:y], pn[:, x:y], A.subtract, ["n7" + k, "nam" + k], ["dn" + k], [bn])
        ac(T.n7[:, h, x + 7:y + 1:7], T.RST[:, x + 1:y:7], I, ["RST"], ["n7" + k], bias=4.0)

    def heights(r):
        for h, (a, b) in enumerate(HS):
            ps, bk, k = pH[h][:, 0:b - a], "pH%d" % h, str(h)
            mms([(ps, T.ID[:], T.ws[:, a:b], True, False), (ps, T.NI[:], hown(r, a, b), False, True)],
                ["ID", "NI", "ws0", "ws1", "h%d%d" % (r, h)], [bk], [bk])
            ac(T.hr[:, a:b], ps, Re, [bk], ["hr" + k], [bk])
            ac(T.hy[:, a:b], T.hr[:, a:b], I, ["hr" + k], ["hy" + k], bias=255.6)
            mms([(ps, T.ID[:], hown(r, a, b), True, False), (ps, T.HI[:], T.hy[:, a:b], False, True)],
                ["ID", "HI", "hy" + k, "h%d%d" % (r, h)], [bk], [bk])
            ac(hown(r + 1, a, b), ps, I, [bk], ["h%d%d" % (r + 1, h), "hr" + k], [bk], bias=-128.0)
        if r + 1 < RO:
            copy(T.HO[:, 16 * CH[2][0]:V], hown(r + 1, 16 * CH[2][0], V), V - 16 * CH[2][0], ["h%d1" % (r + 1)], ["hc2"])
        else:
            dma("y", "dout", [(T.yh[:], hown(RO))], ["h%d0" % RO, "h%d1" % RO], [])

    def choose(r, j):
        c0, c1 = EX[j]
        a, b, k, h = 7 * c0, 7 * c1, "abc"[j], str(min(j, 1))
        n, m = b - a, -(-(b - a) // 16)
        pk, bk = KEY[min(j, 1)]
        for t in range(3):
            rb, qb = "RB%d%s" % (t, k), "QB%d%s" % (t, k)
            scan(T.RB[:, t, a:b], T.RST[:, a:b], pk[:, a:b], 0.0, A.add, A.min, ["RST", "kq" + k, "key" + h], [rb], [bk])
            tt(T.nq[:, a:b], T.RB[:, t, a:b], pk[:, a:b], A.not_equal, [rb, "kq" + k, "key" + h], ["nq" + k], [bk])
            scan(T.QB[:, j, t, 0:n], T.dn[:, a:b], T.nq[:, a:b], 0.0, A.add, A.mult, ["dn" + h, "nq" + k], [qb])
            if t < 2:
                tt(T.kp[:, j, 0:16 * m], ind(T.QB[:, j, t, 0:16 * m + 8], T.BL[:, 0:m]), T.n7[:, min(j, 1), 1 + a:1 + a + 16 * m],
                   A.not_equal, [qb, "n7" + h, "BL"], ["pen" + k])
                tt(pk[:, a:b], pk[:, a:b], T.kp[:, j, 0:n], A.mult, ["kq" + k, "key" + h, "pen" + k], ["kq" + k], [bk])
        rb, qb = ["RB%d%s" % (t, k) for t in range(3)], ["QB%d%s" % (t, k) for t in range(3)]
        if j or r + 1 < RO:
            tt(T.RF[:, :, c0:c1], T.QB[:, j, :, 6:n:7], T.ON[:, :, c0:c1], A.add, qb + ["ON" + h], ["RF" + k])
        if j:
            tt(T.NF[:, :, c0:c1], T.RF[:, :, c0:c1], T.SF[:, :, c0:c1], A.add, ["RF" + k] + SF, ["NF" + k])
        else:
            tt(T.NF[:, :, c0:c1], T.QB[:, j, :, 6:n:7], T.OS[:, :, c0:c1], A.add, qb + ["OS" + h], ["NF" + k])
        tt(T.Ki[:, :, c0:c1], T.NH[:, :, c0:c1], T.RB[:, :, a + 6:7 * c1:7], A.subtract, rb + ["NH" + h], ["Ki" + k])
        ts(T.xi[:, :, c0:c1], T.Ki[:, :, c0:c1], 2047, None, A.bitwise_and, None, ["Ki" + k], ["xi" + k])
        ts(T.EU[:, :, c0:c1], T.xi[:, :, c0:c1], 16.0, pm, A.mult, A.add, ["xi" + k, "PF"], ["EU" + k])
        if r + 1 < RO:
            ts(T.NU[:, :, c0:c1], T.NF[:, :, c0:c1], 1 / SC, None, A.mult, None, ["NF" + k], ["NU" + k])
            ts(T.EM[:, :, c0:c1], T.RF[:, :, c0:c1], 0.0, 16.0, A.is_equal, A.mult, ["RF" + k], ["EM" + k])

    def new_weights(r, c0, c1, eng="sss", early=0.0):
        R = ["z", "zc0", "zc1", "zc2"] + ["cw%d%d" % (l, h) for l in range(3) for h in range(2)] + [t for q in range(r + 1) for t in wall(q)]
        for t in range(3):
            if r + 1 == RO:
                o, w = T.WF[:, t * V + 16 * c0:t * V + 16 * c1], "yw%d%d" % (t, c0)
            elif c0 == 0:
                o, w = wblk(r + 1, t, ub, ub + B), "wb%d%d" % (r + 1, t)
            else:
                o, w = wblk(r + 1, t, 16 * c0, 16 * c1), "w%d_%d%d" % (r + 1, c0 // 32, t)
            gather(eng[t], o, BG[:, 0:unit(r, 0) * U + V], T.EU[:, t, c0:c1], R + tok("EU", c0, c1), [w])
            if r + 1 == RO:
                dma("y", "dout", [(T.yw[:, t * V + 16 * c0:t * V + 16 * c1], o)], [w], [], early)
            elif c0 == 0:
                copy(wblk(r + 1, t, 0, B), o, B, [w], ["w%d_2%d" % (r + 1, t)])

    for r in range(RO):
        if r == 0:
            name_table()
        for k in range(3):
            votes(r, k)
            deaths(r, k)
        if r:
            name_table()
        before_gone(r)
        gone(r, 0)
        gone(r, 1)
        marks(r)
        if r + 1 < RO:
            border_heights(r)
        splice(r, 0)
        splice(r, 1)
        heights(r)
        for j in range(3):
            choose(r, j)
        if r + 1 < RO:
            new_weights(r, *CH[0])
            hand_over(r + 1)
            new_weights(r, *CH[1])
            new_weights(r, *CH[2])
    for (c0, c1), (eng, early) in zip(EX, LE):
        new_weights(RO - 1, c0, c1, eng, early)
    ts(T.q128[:], T.NF[:], 1 / (SC * B), 192.0 - (UB + 79.5) / B, A.mult, A.add, tok("NF"), ["q128"])
    ts(T.fb[:], T.NF[:], UB * SC, None, A.is_ge, None, tok("NF"), ["fb"])
    ts(T.NB[:], T.NF[:], 1 / SC, 1024.0 * rk, A.mult, A.add, tok("NF"), ["NB"])
    ts(T.fa[:], T.q128[:], 864.0, -192.0 * 864 - UB - 1024.0 * rk, A.mult, A.add, ["q128"], ["fa"])
    tt(T.fa[:], T.fa[:], T.fb[:], A.mult, ["fa", "fb"], ["fa"])
    tt(T.YN[:], T.fa[:], T.NB[:], A.add, ["fa", "NB"], ["YN"])
    dma("y", "dout", [(T.yn[:], T.YN[:])], ["YN"], [])
    issue()
